import numpy as np
import ml_dtypes


def mxq(x, axis, fmt="e4m3"):
    dtype, down = {"e4m3": (ml_dtypes.float8_e4m3fn, 7), "e5m2": (ml_dtypes.float8_e5m2, 14)}[fmt]
    v = np.moveaxis(np.asarray(x, np.float32).astype(ml_dtypes.bfloat16).astype(np.float64), axis, -1)
    blocks = v.reshape(v.shape[:-1] + (-1, 32))
    amax = np.abs(blocks).max(-1, keepdims=True)
    byte = np.maximum(np.where(amax > 0, np.frexp(amax)[1] - 1 + 127, 0) - down, 1)
    scale = np.exp2(byte - 127.0)
    codes = (blocks / scale).astype(np.float32).astype(dtype).astype(np.float64)
    return np.moveaxis((codes * scale).reshape(v.shape), -1, axis)


WIDE = False


def mx_kscale(k):
    if not WIDE:
        return np.ones(k)
    levels = np.array([10, -10, 5, -5, 0])
    if k % 512:
        return np.exp2(np.random.permutation(np.resize(levels, k // 32))).repeat(32)
    a = np.empty((k // 512, 16))
    for p in range(k // 512):
        a[p, :8] = np.random.permutation(np.resize(levels, 8))
        for g in range(8):
            far = levels[np.abs(levels - a[p, g]) >= 10]
            a[p, g + 8] = far[np.random.randint(len(far))]
    return np.exp2(a.ravel()).repeat(32)


def f64(x):
    return np.asarray(x).astype(np.float64)


def striped(idx):
    return np.tile(idx.reshape(-1, 16).T, (8, 1)).astype(np.uint16)


def unstriped(offs):
    return offs[:16].T.reshape(-1).astype(np.int64)


def striped8(idx):
    return np.concatenate([x.reshape(-1, 16).T for x in idx]).astype(np.uint16)


def runs(offs, k):
    lists = np.stack([offs[16 * r : 16 * r + 16].T.reshape(-1) for r in range(8)]).astype(np.int64)
    return lists[np.arange(k) % 512 // 64]


def pack_weight(w):
    k, n = w.shape
    w = f64(np.asarray(w, np.float32).astype(ml_dtypes.bfloat16)).reshape(k // 32, 32, n)
    amax = np.abs(w).max(1)
    byte = np.clip(np.where(amax > 0, np.frexp(amax)[1] - 1 + 127 - 7, 1), 1, 254)
    scaled = (w * np.exp2(127.0 - byte)[:, None, :]).reshape(k, n).astype(np.float32)
    words = np.ascontiguousarray(scaled.reshape(k // 512, 128, 4, n).transpose(0, 1, 3, 2)).astype(ml_dtypes.float8_e4m3fn).view(np.uint8)
    return words, np.ascontiguousarray(byte.astype(np.uint8).reshape(k // 512, 16, n))


def unpack_weight(words, scales):
    g, p, n, _ = words.shape
    vals = np.ascontiguousarray(words).view(ml_dtypes.float8_e4m3fn).astype(np.float64) * np.repeat(np.exp2(scales.astype(np.float64) - 127.0), 8, axis=1)[..., None]
    return vals.transpose(0, 1, 3, 2).reshape(g * 512, n)


def sigmoid(v):
    return 1.0 / (1.0 + np.exp(-np.maximum(v, -700.0)))


K, T, S, N, H = 512, 2048, 512, 512, 512


def setup_inputs():
    n = np.random.standard_normal
    s = mx_kscale(K)[:, None]
    u = mx_kscale(H)
    packed_xT = pack_weight(n((K, T)) * s)
    return {
        "x_words": packed_xT[0],
        "x_scales": packed_xT[1],
        "w1": (n((K, H)) / np.sqrt(K) / s).astype(np.float32),
        "w2": (n((K, H)) / np.sqrt(K) / s * u).astype(np.float32),
        "w3": (n((H, N)) / np.sqrt(H) / u[:, None]).astype(np.float32),
        "offs": striped(np.random.permutation(T)[:S]),
        "tap": striped8(np.stack([np.random.permutation(S) for _ in range(8)])),
    }


def reference(x_words, x_scales, w1, w2, w3, offs, tap):
    xq = unpack_weight(x_words, x_scales)[:, unstriped(offs)]
    e = mxq(f64(w2), 0, "e4m3").T @ xq
    y = mxq(f64(w1), 0, "e4m3").T @ xq
    z = (e + e[np.arange(H)[:, None], runs(tap, H)]) * (sigmoid(y + y[np.arange(H)[:, None], runs(tap, H)]))
    return mxq(f64(w3), 0, "e4m3").T @ mxq(z, 0, "e4m3")

@@ -1,0 +1,133 @@
+from contextlib import ExitStack
+
+import concourse.mybir as mybir
+
+K, T, S, N, H = 512, 2048, 512, 512, 512
+FLOPS = 2 * K * H * S * 2 + 2 * H * N * S
+
+F32 = mybir.dt.float32
+BF16 = mybir.dt.bfloat16
+I32 = mybir.dt.int32
+U32 = mybir.dt.uint32
+U16 = mybir.dt.uint16
+U8 = mybir.dt.uint8
+FP8X4 = mybir.dt.float8_e4m3fn_x4
+ADD = mybir.AluOpType.add
+MULT = mybir.AluOpType.mult
+SIGMOID = mybir.ActivationFunctionType.Sigmoid
+
+P = 128
+PACK = 4
+CHUNKS = (256, 128, 128)
+Y_CHUNK = 256
+
+
+def tile_picked_glutap_none_p_kernel(tc, x_words, x_scales, w1, w2, w3, offs, tap, out):
+    nc = tc.nc
+    with ExitStack() as ctx:
+        keep = ctx.enter_context(tc.tile_pool(name="keep", bufs=1))
+        psum = ctx.enter_context(tc.psum_pool(name="psum", bufs=1))
+
+        offs_t = keep.tile([P, S // 16], U16, name="offs_t")
+        tap_t = keep.tile([P, S // 16], U16, name="tap_t")
+        xw = keep.tile([P, T], I32, name="xw", align_bytes=64)
+        xs = keep.tile([P, T], U8, name="xs", align_bytes=64)
+        raw1 = keep.tile([P, PACK, H], F32, name="raw1", align_bytes=64)
+
+        nc.vector.memset(xs[:].bitcast(I32), 0)
+        nc.sync.dma_start(offs_t[:], offs)
+        nc.sync.dma_start(xw[:], x_words[0].rearrange("p n t -> p (n t)").bitcast(I32))
+        for q in range(4):
+            nc.scalar.dma_start(xs[32 * q : 32 * q + 4, :].bitcast(I32), x_scales[0, 4 * q : 4 * q + 4, :].bitcast(I32))
+        nc.sync.dma_start(raw1[:], w1.rearrange("(p j) c -> p j c", j=PACK))
+        nc.sync.dma_start(tap_t[:], tap)
+
+        xg_s = keep.tile([P, S], U8, name="xg_s", align_bytes=64)
+        xg_w = keep.tile([P, S], U32, name="xg_w", align_bytes=64)
+        nc.vector.tensor_copy(xg_s[:], xs[:].indirect(offs_t[:]))
+        nc.vector.tensor_copy(xg_w[:], xw[:].bitcast(U32).indirect(offs_t[:]))
+
+        raw2 = keep.tile([P, PACK, H], F32, name="xs", align_bytes=64)
+        nc.sync.dma_start(raw2[:], w2.rearrange("(p j) c -> p j c", j=PACK))
+        raw3 = keep.tile([P, PACK, N], F32, name="xw", align_bytes=64)
+        w3v = w3.rearrange("(b t q) n -> t b q n", t=PACK, q=8)
+        for t in range(PACK):
+            nc.sync.dma_start(raw3[:, t, :], w3v[t])
+
+        def cast_first(raw, t, name, eng):
+            g = keep.tile([P, P * PACK], BF16, name=name, align_bytes=64)
+            dst = g[:].rearrange("p (b h i j) -> p b h j i", h=2, i=4, j=PACK)
+            src = raw[:].rearrange("p j (b t h i) -> p t b h j i", t=PACK, h=2, i=4)[:, t]
+            if eng == "v":
+                nc.vector.tensor_copy(dst, src)
+            else:
+                nc.scalar.copy(dst, src)
+            return g
+
+        def quant(g, width, name):
+            codes = keep.tile([P, width], U32, name=name + "_c", align_bytes=64)
+            scales = keep.tile([P, width], U8, name=name + "_s", align_bytes=64)
+            nc.vector.quantize_mx(out=codes[:].bitcast(FP8X4), scales=scales[:], in_=g[:])
+            return codes, scales
+
+        def project(codes, scales, bank):
+            acc = psum.tile([P, S], F32, name="bank%d" % bank)
+            nc.tensor.matmul_mx(out=acc[:], lhsT=codes[:].bitcast(FP8X4), lhsT_scale=scales[:],
+                                rhs=xg_w[:].bitcast(FP8X4), rhs_scale=xg_s[:], start=True, stop=True)
+            return acc
+
+        def spill(acc, name):
+            win = keep.tile([P, S], F32, name=name + "_win", align_bytes=64)
+            own = keep.tile([P, S], F32, name=name + "_own", align_bytes=64)
+            nc.scalar.copy(win[:], acc[:])
+            nc.scalar.copy(own[:], acc[:])
+            return win, own
+
+        g1 = [cast_first(raw1, t, "g1_%d" % t, "v" if t < 2 else "s") for t in range(PACK)]
+        q1 = [quant(g1[t], P, "q1_%d" % t) for t in range(PACK)]
+        ys = [spill(project(q1[t][0], q1[t][1], t), "y%d" % t) for t in range(PACK)]
+
+        g2 = [cast_first(raw2, t, "g2_%d" % t, "v") for t in range(PACK)]
+        q2 = [quant(g2[t], P, "q2_%d" % t) for t in range(PACK)]
+
+        ysum = keep.tile([P, PACK, S], F32, name="ysum", align_bytes=64)
+        gate = keep.tile([P, PACK, S], F32, name="gate", align_bytes=64)
+        es = []
+        for t in range(PACK):
+            win, own = ys[t]
+            for c0 in range(0, S, Y_CHUNK):
+                nc.vector.tensor_tensor(ysum[:, t, c0 : c0 + Y_CHUNK], win[:].indirect(tap_t[:, c0 // 16 : (c0 + Y_CHUNK) // 16]),
+                                        own[:, c0 : c0 + Y_CHUNK], ADD)
+            es.append(spill(project(q2[t][0], q2[t][1], 4 + t), "e%d" % t))
+            nc.scalar.activation(gate[:, t, :], ysum[:, t, :], SIGMOID)
+
+        g3 = keep.tile([P, N * PACK], BF16, name="g3", align_bytes=64)
+        nc.scalar.copy(g3[:].rearrange("p (c i j) -> p c j i", i=4, j=PACK), raw3[:].rearrange("p j (c i) -> p c j i", i=4))
+        c3, s3 = quant(g3, N, "q3")
+
+        c0 = 0
+        for n, width in enumerate(CHUNKS):
+            esum = keep.tile([P, PACK, width], F32, name="esum%d" % n, align_bytes=64)
+            for t in range(PACK):
+                win, own = es[t]
+                nc.vector.tensor_tensor(esum[:, t, :], win[:].indirect(tap_t[:, c0 // 16 : (c0 + width) // 16]),
+                                        own[:, c0 : c0 + width], ADD)
+            z = keep.tile([P, width * PACK], BF16, name="z%d" % n, align_bytes=64)
+            nc.vector.tensor_tensor(z[:].rearrange("p (c i j) -> p c j i", i=4, j=PACK),
+                                    esum[:].rearrange("p j (c i) -> p c j i", i=4),
+                                    gate[:, :, c0 : c0 + width].rearrange("p j (c i) -> p c j i", i=4), MULT)
+            zc, zs = quant(z, width, "z%d" % n)
+            res = keep.tile([P, N // P, width], F32, name="res%d" % n, align_bytes=64)
+            for half in range(2):
+                acc = psum.tile([P, 2, width], F32, name="bank%d" % ((2 * n + half) % 4))
+                for u in range(2):
+                    m = 2 * half + u
+                    nc.tensor.matmul_mx(out=acc[:, u, :], lhsT=c3[:, m * P : (m + 1) * P].bitcast(FP8X4), lhsT_scale=s3[:, m * P : (m + 1) * P],
+                                        rhs=zc[:].bitcast(FP8X4), rhs_scale=zs[:], start=True, stop=True)
+                if n == len(CHUNKS) - 1 and half == 1:
+                    nc.vector.tensor_copy(res[:, 2 * half : 2 * half + 2, :], acc[:])
+                else:
+                    nc.scalar.copy(res[:, 2 * half : 2 * half + 2, :], acc[:])
+                nc.sync.dma_start(out[2 * half * P : (2 * half + 2) * P, c0 : c0 + width].rearrange("(u p) c -> p u c", p=P),
+                                  res[:, 2 * half : 2 * half + 2, :])
+            c0 = c0 + width

@@ -18,8 +18,8 @@ SIGMOID = mybir.ActivationFunctionType.Sigmoid
 
 P = 128
 PACK = 4
-CHUNKS = (256, 128, 128)
-Y_CHUNK = 256
+HALF = S // 2
+CHUNKS = ((0, 256), (256, 128), (384, 128))
 
 
 def tile_picked_glutap_none_p_kernel(tc, x_words, x_scales, w1, w2, w3, offs, tap, out):
@@ -28,11 +28,18 @@ def tile_picked_glutap_none_p_kernel(tc, x_words, x_scales, w1, w2, w3, offs, ta
         keep = ctx.enter_context(tc.tile_pool(name="keep", bufs=1))
         psum = ctx.enter_context(tc.psum_pool(name="psum", bufs=1))
 
+        def sb(shape, dtype, name):
+            return keep.tile(shape, dtype, name=name, align_bytes=64)
+
+        def bank(shape, b):
+            return psum.tile(shape, F32, name="bank%d" % b)
+
         offs_t = keep.tile([P, S // 16], U16, name="offs_t")
         tap_t = keep.tile([P, S // 16], U16, name="tap_t")
-        xw = keep.tile([P, T], I32, name="xw", align_bytes=64)
-        xs = keep.tile([P, T], U8, name="xs", align_bytes=64)
-        raw1 = keep.tile([P, PACK, H], F32, name="raw1", align_bytes=64)
+        xw = sb([P, T], I32, "xw")
+        xs = sb([P, T], U8, "xs")
+        raw1 = sb([P, PACK, H], F32, "raw1")
+        warm = sb([P, 16], F32, "raw2")
 
         nc.vector.memset(xs[:].bitcast(I32), 0)
         nc.sync.dma_start(offs_t[:], offs)
@@ -41,93 +48,105 @@ def tile_picked_glutap_none_p_kernel(tc, x_words, x_scales, w1, w2, w3, offs, ta
             nc.scalar.dma_start(xs[32 * q : 32 * q + 4, :].bitcast(I32), x_scales[0, 4 * q : 4 * q + 4, :].bitcast(I32))
         nc.sync.dma_start(raw1[:], w1.rearrange("(p j) c -> p j c", j=PACK))
         nc.sync.dma_start(tap_t[:], tap)
+        nc.vector.memset(warm[:, 0:8], 0.0)
+        nc.scalar.activation(warm[:, 8:16], warm[:, 0:8], SIGMOID)
+        raw2 = sb([P, PACK, H], F32, "raw2")
+        nc.sync.dma_start(raw2[:], w2.rearrange("(p j) c -> p j c", j=PACK))
 
-        xg_s = keep.tile([P, S], U8, name="xg_s", align_bytes=64)
-        xg_w = keep.tile([P, S], U32, name="xg_w", align_bytes=64)
+        xg_s = sb([P, S], U8, "xg_s")
+        xg_w = sb([P, S], U32, "xg_w")
         nc.vector.tensor_copy(xg_s[:], xs[:].indirect(offs_t[:]))
         nc.vector.tensor_copy(xg_w[:], xw[:].bitcast(U32).indirect(offs_t[:]))
 
-        raw2 = keep.tile([P, PACK, H], F32, name="xs", align_bytes=64)
-        nc.sync.dma_start(raw2[:], w2.rearrange("(p j) c -> p j c", j=PACK))
-        raw3 = keep.tile([P, PACK, N], F32, name="xw", align_bytes=64)
+        raw3 = sb([P, PACK, N], F32, "xs")
         w3v = w3.rearrange("(b t q) n -> t b q n", t=PACK, q=8)
         for t in range(PACK):
             nc.sync.dma_start(raw3[:, t, :], w3v[t])
 
-        def cast_first(raw, t, name, eng):
-            g = keep.tile([P, P * PACK], BF16, name=name, align_bytes=64)
+        def cast_first(raw, t, name, copy):
+            g = sb([P, P * PACK], BF16, name)
             dst = g[:].rearrange("p (b h i j) -> p b h j i", h=2, i=4, j=PACK)
             src = raw[:].rearrange("p j (b t h i) -> p t b h j i", t=PACK, h=2, i=4)[:, t]
-            if eng == "v":
-                nc.vector.tensor_copy(dst, src)
-            else:
-                nc.scalar.copy(dst, src)
+            copy(dst, src)
             return g
 
         def quant(g, width, name):
-            codes = keep.tile([P, width], U32, name=name + "_c", align_bytes=64)
-            scales = keep.tile([P, width], U8, name=name + "_s", align_bytes=64)
+            codes = sb([P, width], U32, name + "_c")
+            scales = sb([P, width], U8, name + "_s")
             nc.vector.quantize_mx(out=codes[:].bitcast(FP8X4), scales=scales[:], in_=g[:])
             return codes, scales
 
-        def project(codes, scales, bank):
-            acc = psum.tile([P, S], F32, name="bank%d" % bank)
-            nc.tensor.matmul_mx(out=acc[:], lhsT=codes[:].bitcast(FP8X4), lhsT_scale=scales[:],
-                                rhs=xg_w[:].bitcast(FP8X4), rhs_scale=xg_s[:], start=True, stop=True)
+        def project(q, c0, width, b):
+            acc = bank([P, width], b)
+            nc.tensor.matmul_mx(out=acc[:], lhsT=q[0][:].bitcast(FP8X4), lhsT_scale=q[1][:],
+                                rhs=xg_w[:, c0 : c0 + width].bitcast(FP8X4), rhs_scale=xg_s[:, c0 : c0 + width], start=True, stop=True)
             return acc
 
-        def spill(acc, name):
-            win = keep.tile([P, S], F32, name=name + "_win", align_bytes=64)
-            own = keep.tile([P, S], F32, name=name + "_own", align_bytes=64)
-            nc.scalar.copy(win[:], acc[:])
-            nc.scalar.copy(own[:], acc[:])
-            return win, own
+        def tap_add(dst, window, own, c0, width):
+            nc.vector.tensor_tensor(dst, window[:].indirect(tap_t[:, c0 // 16 : (c0 + width) // 16]), own, ADD)
 
-        g1 = [cast_first(raw1, t, "g1_%d" % t, "v" if t < 2 else "s") for t in range(PACK)]
+        copies1 = (nc.vector.tensor_copy, nc.vector.tensor_copy, nc.scalar.copy, nc.scalar.copy)
+        g1 = [cast_first(raw1, t, "g1_%d" % t, copies1[t]) for t in range(PACK)]
         q1 = [quant(g1[t], P, "q1_%d" % t) for t in range(PACK)]
-        ys = [spill(project(q1[t][0], q1[t][1], t), "y%d" % t) for t in range(PACK)]
 
-        g2 = [cast_first(raw2, t, "g2_%d" % t, "v") for t in range(PACK)]
+        ywin = [sb([P, S if t == 0 else 2 * S], F32, "ywin%d" % t) for t in range(PACK)]
+        ylast = sb([P, S], F32, "ylast")
+        yown = [ywin[t + 1][:, S : 2 * S] if t + 1 < PACK else ylast[:] for t in range(PACK)]
+        ysum0 = sb([P, S], F32, "ysum0")
+
+        ya = project(q1[0], 0, HALF, 0)
+        yb = project(q1[0], HALF, HALF, 1)
+        nc.scalar.copy(ywin[0][:, 0:HALF], ya[:])
+        nc.vector.tensor_copy(yown[0][:, 0:HALF], ya[:])
+        nc.scalar.copy(ywin[0][:, HALF:S], yb[:])
+        nc.scalar.copy(yown[0][:, HALF:S], yb[:])
+        tap_add(ysum0[:, 0:HALF], ywin[0], yown[0][:, 0:HALF], 0, HALF)
+        tap_add(ysum0[:, HALF:S], ywin[0], yown[0][:, HALF:S], HALF, HALF)
+        for t in range(1, PACK):
+            acc = project(q1[t], 0, S, 1 + t)
+            nc.scalar.copy(ywin[t][:, 0:S], acc[:])
+            nc.scalar.copy(yown[t], acc[:])
+
+        ewin = [sb([P, S], F32, "ewin%d" % t) for t in range(PACK)]
+        eown = [sb([P, S], F32, "eown%d" % t) for t in range(PACK)]
+        g2 = [cast_first(raw2, t, "g2_%d" % t, nc.vector.tensor_copy) for t in range(PACK)]
         q2 = [quant(g2[t], P, "q2_%d" % t) for t in range(PACK)]
-
-        ysum = keep.tile([P, PACK, S], F32, name="ysum", align_bytes=64)
-        gate = keep.tile([P, PACK, S], F32, name="gate", align_bytes=64)
-        es = []
         for t in range(PACK):
-            win, own = ys[t]
-            for c0 in range(0, S, Y_CHUNK):
-                nc.vector.tensor_tensor(ysum[:, t, c0 : c0 + Y_CHUNK], win[:].indirect(tap_t[:, c0 // 16 : (c0 + Y_CHUNK) // 16]),
-                                        own[:, c0 : c0 + Y_CHUNK], ADD)
-            es.append(spill(project(q2[t][0], q2[t][1], 4 + t), "e%d" % t))
-            nc.scalar.activation(gate[:, t, :], ysum[:, t, :], SIGMOID)
+            acc = project(q2[t], 0, S, (5 + t) % 8)
+            nc.scalar.copy(ewin[t][:], acc[:])
+            nc.sync.dma_start(eown[t][:], ewin[t][:])
+        ysum = sb([P, PACK - 1, S], F32, "g2_2")
+        for t in range(1, PACK):
+            tap_add(ysum[:, t - 1, :], ywin[t], yown[t], 0, S)
+        gate = sb([P, PACK, S], F32, "q2_3_s")
 
-        g3 = keep.tile([P, N * PACK], BF16, name="g3", align_bytes=64)
+        g3 = sb([P, N * PACK], BF16, "q2_3_c")
         nc.scalar.copy(g3[:].rearrange("p (c i j) -> p c j i", i=4, j=PACK), raw3[:].rearrange("p j (c i) -> p c j i", i=4))
         c3, s3 = quant(g3, N, "q3")
+        nc.scalar.activation(gate[:, 0, :], ysum0[:], SIGMOID)
 
-        c0 = 0
-        for n, width in enumerate(CHUNKS):
-            esum = keep.tile([P, PACK, width], F32, name="esum%d" % n, align_bytes=64)
-            for t in range(PACK):
-                win, own = es[t]
-                nc.vector.tensor_tensor(esum[:, t, :], win[:].indirect(tap_t[:, c0 // 16 : (c0 + width) // 16]),
-                                        own[:, c0 : c0 + width], ADD)
-            z = keep.tile([P, width * PACK], BF16, name="z%d" % n, align_bytes=64)
+        esum = None
+        for n, (c0, width) in enumerate(CHUNKS):
+            if c0 % HALF == 0:
+                esum = sb([P, PACK, HALF], F32, "esum")
+                nc.scalar.activation(gate[:, 1:PACK, c0 : c0 + HALF], ysum[:, :, c0 : c0 + HALF], SIGMOID)
+                for t in range(PACK):
+                    tap_add(esum[:, t, :], ewin[t], eown[t][:, c0 : c0 + HALF], c0, HALF)
+            e0 = c0 % HALF
+            z = sb([P, width * PACK], BF16, "z%d" % n)
             nc.vector.tensor_tensor(z[:].rearrange("p (c i j) -> p c j i", i=4, j=PACK),
-                                    esum[:].rearrange("p j (c i) -> p c j i", i=4),
+                                    esum[:, :, e0 : e0 + width].rearrange("p j (c i) -> p c j i", i=4),
                                     gate[:, :, c0 : c0 + width].rearrange("p j (c i) -> p c j i", i=4), MULT)
             zc, zs = quant(z, width, "z%d" % n)
-            res = keep.tile([P, N // P, width], F32, name="res%d" % n, align_bytes=64)
             for half in range(2):
-                acc = psum.tile([P, 2, width], F32, name="bank%d" % ((2 * n + half) % 4))
+                acc = bank([P, 2, width], 1 + 2 * n + half)
                 for u in range(2):
                     m = 2 * half + u
                     nc.tensor.matmul_mx(out=acc[:, u, :], lhsT=c3[:, m * P : (m + 1) * P].bitcast(FP8X4), lhsT_scale=s3[:, m * P : (m + 1) * P],
                                         rhs=zc[:].bitcast(FP8X4), rhs_scale=zs[:], start=True, stop=True)
+                res = sb([P, 2, width], F32, "res%d_%d" % (n, half))
                 if n == len(CHUNKS) - 1 and half == 1:
-                    nc.vector.tensor_copy(res[:, 2 * half : 2 * half + 2, :], acc[:])
+                    nc.vector.tensor_copy(res[:], acc[:])
                 else:
-                    nc.scalar.copy(res[:, 2 * half : 2 * half + 2, :], acc[:])
-                nc.sync.dma_start(out[2 * half * P : (2 * half + 2) * P, c0 : c0 + width].rearrange("(u p) c -> p u c", p=P),
-                                  res[:, 2 * half : 2 * half + 2, :])
-            c0 = c0 + width
+                    nc.scalar.copy(res[:], acc[:])
+                nc.sync.dma_start(out[2 * half * P : (2 * half + 2) * P, c0 : c0 + width].rearrange("(u p) c -> p u c", p=P), res[:])

@@ -41,13 +41,13 @@ def tile_picked_glutap_none_p_kernel(tc, x_words, x_scales, w1, w2, w3, offs, ta
         raw1 = sb([P, PACK, H], F32, "raw1")
         warm = sb([P, 16], F32, "raw2")
 
-        nc.vector.memset(xs[:].bitcast(I32), 0)
-        nc.sync.dma_start(offs_t[:], offs)
+        nc.gpsimd.memset(xs[:].bitcast(I32), 0)
         nc.sync.dma_start(xw[:], x_words[0].rearrange("p n t -> p (n t)").bitcast(I32))
+        nc.sync.dma_start(offs_t[:], offs)
         for q in range(4):
-            nc.scalar.dma_start(xs[32 * q : 32 * q + 4, :].bitcast(I32), x_scales[0, 4 * q : 4 * q + 4, :].bitcast(I32))
-        nc.sync.dma_start(raw1[:], w1.rearrange("(p j) c -> p j c", j=PACK))
+            nc.sync.dma_start(xs[32 * q : 32 * q + 4, :].bitcast(I32), x_scales[0, 4 * q : 4 * q + 4, :].bitcast(I32))
         nc.sync.dma_start(tap_t[:], tap)
+        nc.sync.dma_start(raw1[:], w1.rearrange("(p j) c -> p j c", j=PACK))
         nc.vector.memset(warm[:, 0:8], 0.0)
         nc.scalar.activation(warm[:, 8:16], warm[:, 0:8], SIGMOID)
         raw2 = sb([P, PACK, H], F32, "raw2")
@@ -55,13 +55,8 @@ def tile_picked_glutap_none_p_kernel(tc, x_words, x_scales, w1, w2, w3, offs, ta
 
         xg_s = sb([P, S], U8, "xg_s")
         xg_w = sb([P, S], U32, "xg_w")
-        nc.vector.tensor_copy(xg_s[:], xs[:].indirect(offs_t[:]))
         nc.vector.tensor_copy(xg_w[:], xw[:].bitcast(U32).indirect(offs_t[:]))
-
-        raw3 = sb([P, PACK, N], F32, "xs")
-        w3v = w3.rearrange("(b t q) n -> t b q n", t=PACK, q=8)
-        for t in range(PACK):
-            nc.sync.dma_start(raw3[:, t, :], w3v[t])
+        nc.vector.tensor_copy(xg_s[:], xs[:].indirect(offs_t[:]))
 
         def cast_first(raw, t, name, copy):
             g = sb([P, P * PACK], BF16, name)
@@ -88,6 +83,11 @@ def tile_picked_glutap_none_p_kernel(tc, x_words, x_scales, w1, w2, w3, offs, ta
         copies1 = (nc.vector.tensor_copy, nc.vector.tensor_copy, nc.scalar.copy, nc.scalar.copy)
         g1 = [cast_first(raw1, t, "g1_%d" % t, copies1[t]) for t in range(PACK)]
         q1 = [quant(g1[t], P, "q1_%d" % t) for t in range(PACK)]
+
+        raw3 = sb([P, PACK, N], F32, "raw1")
+        w3v = w3.rearrange("(b t q) n -> t b q n", t=PACK, q=8)
+        for t in range(PACK):
+            nc.sync.dma_start(raw3[:, t, :], w3v[t])
 
         ywin = [sb([P, S if t == 0 else 2 * S], F32, "ywin%d" % t) for t in range(PACK)]
         ylast = sb([P, S], F32, "ylast")
@@ -134,9 +134,9 @@ def tile_picked_glutap_none_p_kernel(tc, x_words, x_scales, w1, w2, w3, offs, ta
                     tap_add(esum[:, t, :], ewin[t], eown[t][:, c0 : c0 + HALF], c0, HALF)
             e0 = c0 % HALF
             z = sb([P, width * PACK], BF16, "z%d" % n)
-            nc.vector.tensor_tensor(z[:].rearrange("p (c i j) -> p c j i", i=4, j=PACK),
-                                    esum[:, :, e0 : e0 + width].rearrange("p j (c i) -> p c j i", i=4),
-                                    gate[:, :, c0 : c0 + width].rearrange("p j (c i) -> p c j i", i=4), MULT)
+            nc.vector.tensor_tensor(z[:].rearrange("p (c i j) -> p c j i", i=2, j=PACK),
+                                    esum[:, :, e0 : e0 + width].rearrange("p j (c i) -> p c j i", i=2),
+                                    gate[:, :, c0 : c0 + width].rearrange("p j (c i) -> p c j i", i=2), MULT)
             zc, zs = quant(z, width, "z%d" % n)
             for half in range(2):
                 acc = bank([P, 2, width], 1 + 2 * n + half)
@@ -149,4 +149,5 @@ def tile_picked_glutap_none_p_kernel(tc, x_words, x_scales, w1, w2, w3, offs, ta
                     nc.vector.tensor_copy(res[:], acc[:])
                 else:
                     nc.scalar.copy(res[:], acc[:])
-                nc.sync.dma_start(out[2 * half * P : (2 * half + 2) * P, c0 : c0 + width].rearrange("(u p) c -> p u c", p=P), res[:])
+                queue = nc.scalar if n == len(CHUNKS) - 1 and half == 0 else nc.sync
+                queue.dma_start(out[2 * half * P : (2 * half + 2) * P, c0 : c0 + width].rearrange("(u p) c -> p u c", p=P), res[:])

@@ -19,7 +19,7 @@ SIGMOID = mybir.ActivationFunctionType.Sigmoid
 P = 128
 PACK = 4
 HALF = S // 2
-CHUNKS = ((0, 256), (256, 128), (384, 128))
+CHUNK = 128
 
 
 def tile_picked_glutap_none_p_kernel(tc, x_words, x_scales, w1, w2, w3, offs, tap, out):
@@ -58,9 +58,8 @@ def tile_picked_glutap_none_p_kernel(tc, x_words, x_scales, w1, w2, w3, offs, ta
         nc.vector.tensor_copy(xg_w[:], xw[:].bitcast(U32).indirect(offs_t[:]))
         nc.vector.tensor_copy(xg_s[:], xs[:].indirect(offs_t[:]))
 
-        def cast_first(raw, t, name, copy):
-            g = sb([P, P * PACK], BF16, name)
-            dst = g[:].rearrange("p (b h i j) -> p b h j i", h=2, i=4, j=PACK)
+        def cast_first(raw, t, g, copy):
+            dst = g.rearrange("p (b h i j) -> p b h j i", h=2, i=4, j=PACK)
             src = raw[:].rearrange("p j (b t h i) -> p t b h j i", t=PACK, h=2, i=4)[:, t]
             copy(dst, src)
             return g
@@ -68,7 +67,7 @@ def tile_picked_glutap_none_p_kernel(tc, x_words, x_scales, w1, w2, w3, offs, ta
         def quant(g, width, name):
             codes = sb([P, width], U32, name + "_c")
             scales = sb([P, width], U8, name + "_s")
-            nc.vector.quantize_mx(out=codes[:].bitcast(FP8X4), scales=scales[:], in_=g[:])
+            nc.vector.quantize_mx(out=codes[:].bitcast(FP8X4), scales=scales[:], in_=g)
             return codes, scales
 
         def project(q, c0, width, b):
@@ -81,7 +80,7 @@ def tile_picked_glutap_none_p_kernel(tc, x_words, x_scales, w1, w2, w3, offs, ta
             nc.vector.tensor_tensor(dst, window[:].indirect(tap_t[:, c0 // 16 : (c0 + width) // 16]), own, ADD)
 
         copies1 = (nc.vector.tensor_copy, nc.vector.tensor_copy, nc.scalar.copy, nc.scalar.copy)
-        g1 = [cast_first(raw1, t, "g1_%d" % t, copies1[t]) for t in range(PACK)]
+        g1 = [cast_first(raw1, t, sb([P, P * PACK], BF16, "g1_%d" % t)[:], copies1[t]) for t in range(PACK)]
         q1 = [quant(g1[t], P, "q1_%d" % t) for t in range(PACK)]
 
         raw3 = sb([P, PACK, N], F32, "raw1")
@@ -89,65 +88,101 @@ def tile_picked_glutap_none_p_kernel(tc, x_words, x_scales, w1, w2, w3, offs, ta
         for t in range(PACK):
             nc.sync.dma_start(raw3[:, t, :], w3v[t])
 
-        ywin = [sb([P, S if t == 0 else 2 * S], F32, "ywin%d" % t) for t in range(PACK)]
-        ylast = sb([P, S], F32, "ylast")
-        yown = [ywin[t + 1][:, S : 2 * S] if t + 1 < PACK else ylast[:] for t in range(PACK)]
-        ysum0 = sb([P, S], F32, "ysum0")
+        win = [sb([P, S if u == 0 else 2 * S], F32, "win%d" % u) for u in range(2 * PACK)]
+        last = sb([P, S], F32, "last")
+        host = (1, 3, 4, 2, 5, 6, 7)
+        own = [win[host[u]][:, S : 2 * S] if u + 1 < 2 * PACK else last[:] for u in range(2 * PACK)]
 
+        def leave_bank(q, u, b):
+            acc = project(q, 0, S, b)
+            nc.scalar.copy(win[u][:, 0:S], acc[:])
+
+        def plain_by_dma(u):
+            nc.sync.dma_start(own[u], win[u][:, 0:S])
+
+        def plain_by_vector(u):
+            nc.vector.tensor_copy(own[u], win[u][:, 0:S])
+
+        def whole_tap(u, name):
+            total = sb([P, S], F32, name)
+            tap_add(total[:], win[u], own[u], 0, S)
+            return total
+
+        g2 = [sb([P, P * PACK], BF16, "g2_%d" % t)[:] for t in range(PACK)]
+        q2 = []
+
+        def round_w2(t, copy):
+            cast_first(raw2, t, g2[t], copy)
+
+        def quant_w2(t):
+            q2.append(quant(g2[t], P, "q2_%d" % t))
+
+        ysum = [sb([P, S], F32, "ysum0")]
         ya = project(q1[0], 0, HALF, 0)
         yb = project(q1[0], HALF, HALF, 1)
-        nc.scalar.copy(ywin[0][:, 0:HALF], ya[:])
-        nc.vector.tensor_copy(yown[0][:, 0:HALF], ya[:])
-        nc.scalar.copy(ywin[0][:, HALF:S], yb[:])
-        nc.scalar.copy(yown[0][:, HALF:S], yb[:])
-        tap_add(ysum0[:, 0:HALF], ywin[0], yown[0][:, 0:HALF], 0, HALF)
-        tap_add(ysum0[:, HALF:S], ywin[0], yown[0][:, HALF:S], HALF, HALF)
+        nc.scalar.copy(win[0][:, 0:HALF], ya[:])
+        nc.vector.tensor_copy(win[0][:, HALF:S], yb[:])
+        nc.scalar.copy(own[0][:, 0:HALF], ya[:])
+        round_w2(0, nc.vector.tensor_copy)
+        tap_add(ysum[0][:, 0:HALF], win[0], own[0][:, 0:HALF], 0, HALF)
+        quant_w2(0)
+        leave_bank(q1[1], 1, 2)
+        nc.scalar.copy(own[0][:, HALF:S], yb[:])
+        plain_by_vector(1)
+        tap_add(ysum[0][:, HALF:S], win[0], own[0][:, HALF:S], HALF, HALF)
+        ysum.append(whole_tap(1, "ysum1"))
+        leave_bank(q1[3], 3, 4)
+        plain_by_dma(3)
+        leave_bank(q1[2], 2, 3)
+        plain_by_vector(2)
+        round_w2(1, nc.scalar.copy)
+        quant_w2(1)
+        round_w2(2, nc.scalar.copy)
+        quant_w2(2)
+        ysum.append(whole_tap(2, "ysum2"))
+        leave_bank(q2[0], 4, 5)
+        plain_by_dma(4)
+        round_w2(3, nc.scalar.copy)
+        quant_w2(3)
+        ysum.append(whole_tap(3, "raw2"))
         for t in range(1, PACK):
-            acc = project(q1[t], 0, S, 1 + t)
-            nc.scalar.copy(ywin[t][:, 0:S], acc[:])
-            nc.scalar.copy(yown[t], acc[:])
-
-        ewin = [sb([P, S], F32, "ewin%d" % t) for t in range(PACK)]
-        eown = [sb([P, S], F32, "eown%d" % t) for t in range(PACK)]
-        g2 = [cast_first(raw2, t, "g2_%d" % t, nc.vector.tensor_copy) for t in range(PACK)]
-        q2 = [quant(g2[t], P, "q2_%d" % t) for t in range(PACK)]
+            leave_bank(q2[t], PACK + t, (5 + t) % 8)
+            plain_by_dma(PACK + t)
+        gate = sb([P, PACK, S], F32, "gate")
         for t in range(PACK):
-            acc = project(q2[t], 0, S, (5 + t) % 8)
-            nc.scalar.copy(ewin[t][:], acc[:])
-            nc.sync.dma_start(eown[t][:], ewin[t][:])
-        ysum = sb([P, PACK - 1, S], F32, "g2_2")
-        for t in range(1, PACK):
-            tap_add(ysum[:, t - 1, :], ywin[t], yown[t], 0, S)
-        gate = sb([P, PACK, S], F32, "q2_3_s")
+            nc.scalar.activation(gate[:, t, :], ysum[t][:], SIGMOID)
+        esum = sb([P, PACK, S], F32, "esum")
+        for t in range(PACK):
+            tap_add(esum[:, t, :], win[PACK + t], own[PACK + t], 0, S)
 
         g3 = sb([P, N * PACK], BF16, "q2_3_c")
         nc.scalar.copy(g3[:].rearrange("p (c i j) -> p c j i", i=4, j=PACK), raw3[:].rearrange("p j (c i) -> p c j i", i=4))
-        c3, s3 = quant(g3, N, "q3")
-        nc.scalar.activation(gate[:, 0, :], ysum0[:], SIGMOID)
 
-        esum = None
-        for n, (c0, width) in enumerate(CHUNKS):
-            if c0 % HALF == 0:
-                esum = sb([P, PACK, HALF], F32, "esum")
-                nc.scalar.activation(gate[:, 1:PACK, c0 : c0 + HALF], ysum[:, :, c0 : c0 + HALF], SIGMOID)
-                for t in range(PACK):
-                    tap_add(esum[:, t, :], ewin[t], eown[t][:, c0 : c0 + HALF], c0, HALF)
-            e0 = c0 % HALF
-            z = sb([P, width * PACK], BF16, "z%d" % n)
+        def product(n):
+            cols = slice(n * CHUNK, (n + 1) * CHUNK)
+            z = sb([P, CHUNK * PACK], BF16, "z%d" % n)
             nc.vector.tensor_tensor(z[:].rearrange("p (c i j) -> p c j i", i=2, j=PACK),
-                                    esum[:, :, e0 : e0 + width].rearrange("p j (c i) -> p c j i", i=2),
-                                    gate[:, :, c0 : c0 + width].rearrange("p j (c i) -> p c j i", i=2), MULT)
-            zc, zs = quant(z, width, "z%d" % n)
+                                    esum[:, :, cols].rearrange("p j (c i) -> p c j i", i=2),
+                                    gate[:, :, cols].rearrange("p j (c i) -> p c j i", i=2), MULT)
+            return z
+
+        chunks = S // CHUNK
+        zs = [product(0)]
+        c3, s3 = quant(g3[:], N, "q3")
+        for n in range(chunks):
+            if n + 1 < chunks:
+                zs.append(product(n + 1))
+            zc, zp = quant(zs[n][:], CHUNK, "z%d" % n)
             for half in range(2):
-                acc = bank([P, 2, width], 1 + 2 * n + half)
+                acc = bank([P, 2, CHUNK], (1 + 2 * n + half) % 8)
                 for u in range(2):
                     m = 2 * half + u
                     nc.tensor.matmul_mx(out=acc[:, u, :], lhsT=c3[:, m * P : (m + 1) * P].bitcast(FP8X4), lhsT_scale=s3[:, m * P : (m + 1) * P],
-                                        rhs=zc[:].bitcast(FP8X4), rhs_scale=zs[:], start=True, stop=True)
-                res = sb([P, 2, width], F32, "res%d_%d" % (n, half))
-                if n == len(CHUNKS) - 1 and half == 1:
+                                        rhs=zc[:].bitcast(FP8X4), rhs_scale=zp[:], start=True, stop=True)
+                res = sb([P, 2, CHUNK], F32, "res%d_%d" % (n, half))
+                if n == chunks - 1 and half == 1:
                     nc.vector.tensor_copy(res[:], acc[:])
                 else:
                     nc.scalar.copy(res[:], acc[:])
-                queue = nc.scalar if n == len(CHUNKS) - 1 and half == 0 else nc.sync
-                queue.dma_start(out[2 * half * P : (2 * half + 2) * P, c0 : c0 + width].rearrange("(u p) c -> p u c", p=P), res[:])
+                queue = nc.scalar if n == chunks - 1 and half == 0 else nc.sync
+                queue.dma_start(out[2 * half * P : (2 * half + 2) * P, n * CHUNK : (n + 1) * CHUNK].rearrange("(u p) c -> p u c", p=P), res[:])

@@ -83,15 +83,14 @@ def tile_picked_glutap_none_p_kernel(tc, x_words, x_scales, w1, w2, w3, offs, ta
         g1 = [cast_first(raw1, t, sb([P, P * PACK], BF16, "g1_%d" % t)[:], copies1[t]) for t in range(PACK)]
         q1 = [quant(g1[t], P, "q1_%d" % t) for t in range(PACK)]
 
-        raw3 = sb([P, PACK, N], F32, "raw1")
+        raw3 = sb([P, PACK, N], F32, "xw")
         w3v = w3.rearrange("(b t q) n -> t b q n", t=PACK, q=8)
         for t in range(PACK):
             nc.sync.dma_start(raw3[:, t, :], w3v[t])
 
         win = [sb([P, S if u == 0 else 2 * S], F32, "win%d" % u) for u in range(2 * PACK)]
         last = sb([P, S], F32, "last")
-        host = (1, 3, 4, 2, 5, 6, 7)
-        own = [win[host[u]][:, S : 2 * S] if u + 1 < 2 * PACK else last[:] for u in range(2 * PACK)]
+        own = [win[u + 1][:, S : 2 * S] if u + 1 < 2 * PACK else last[:] for u in range(2 * PACK)]
 
         def leave_bank(q, u, b):
             acc = project(q, 0, S, b)
@@ -131,14 +130,14 @@ def tile_picked_glutap_none_p_kernel(tc, x_words, x_scales, w1, w2, w3, offs, ta
         plain_by_vector(1)
         tap_add(ysum[0][:, HALF:S], win[0], own[0][:, HALF:S], HALF, HALF)
         ysum.append(whole_tap(1, "ysum1"))
-        leave_bank(q1[3], 3, 4)
-        plain_by_dma(3)
-        leave_bank(q1[2], 2, 3)
-        plain_by_vector(2)
         round_w2(1, nc.scalar.copy)
         quant_w2(1)
+        leave_bank(q1[3], 3, 4)
+        plain_by_dma(3)
         round_w2(2, nc.scalar.copy)
         quant_w2(2)
+        leave_bank(q1[2], 2, 3)
+        plain_by_vector(2)
         ysum.append(whole_tap(2, "ysum2"))
         leave_bank(q2[0], 4, 5)
         plain_by_dma(4)
@@ -149,18 +148,20 @@ def tile_picked_glutap_none_p_kernel(tc, x_words, x_scales, w1, w2, w3, offs, ta
             leave_bank(q2[t], PACK + t, (5 + t) % 8)
             plain_by_dma(PACK + t)
         gate = sb([P, PACK, S], F32, "gate")
-        for t in range(PACK):
+        for t in range(2):
+            nc.scalar.activation(gate[:, t, :], ysum[t][:], SIGMOID)
+        g3 = sb([P, N * PACK], BF16, "q2_3_c")
+        nc.scalar.copy(g3[:].rearrange("p (c i j) -> p c j i", i=4, j=PACK), raw3[:].rearrange("p j (c i) -> p c j i", i=4))
+        c3, s3 = quant(g3[:], N, "q3")
+        for t in range(2, PACK):
             nc.scalar.activation(gate[:, t, :], ysum[t][:], SIGMOID)
         esum = sb([P, PACK, S], F32, "esum")
         for t in range(PACK):
             tap_add(esum[:, t, :], win[PACK + t], own[PACK + t], 0, S)
 
-        g3 = sb([P, N * PACK], BF16, "q2_3_c")
-        nc.scalar.copy(g3[:].rearrange("p (c i j) -> p c j i", i=4, j=PACK), raw3[:].rearrange("p j (c i) -> p c j i", i=4))
-
         def product(n):
             cols = slice(n * CHUNK, (n + 1) * CHUNK)
-            z = sb([P, CHUNK * PACK], BF16, "z%d" % n)
+            z = sb([P, CHUNK * PACK], BF16, "z%d" % (n if n < 3 else 1))
             nc.vector.tensor_tensor(z[:].rearrange("p (c i j) -> p c j i", i=2, j=PACK),
                                     esum[:, :, cols].rearrange("p j (c i) -> p c j i", i=2),
                                     gate[:, :, cols].rearrange("p j (c i) -> p c j i", i=2), MULT)
@@ -168,10 +169,11 @@ def tile_picked_glutap_none_p_kernel(tc, x_words, x_scales, w1, w2, w3, offs, ta
 
         chunks = S // CHUNK
         zs = [product(0)]
-        c3, s3 = quant(g3[:], N, "q3")
         for n in range(chunks):
-            if n + 1 < chunks:
+            if n + 2 < chunks:
                 zs.append(product(n + 1))
+            elif n + 1 == chunks:
+                zs.append(product(n))
             zc, zp = quant(zs[n][:], CHUNK, "z%d" % n)
             for half in range(2):
                 acc = bank([P, 2, CHUNK], (1 + 2 * n + half) % 8)

@@ -34,35 +34,38 @@ def tile_picked_glutap_none_p_kernel(tc, x_words, x_scales, w1, w2, w3, offs, ta
         def bank(shape, b):
             return psum.tile(shape, F32, name="bank%d" % b)
 
+        def load_half(w, half, name):
+            raw = sb([P, PACK, HALF], F32, name)
+            nc.sync.dma_start(raw[:], w.rearrange("(p j) c -> p j c", j=PACK)[:, :, half * HALF : (half + 1) * HALF])
+            return raw
+
         offs_t = keep.tile([P, S // 16], U16, name="offs_t")
         tap_t = keep.tile([P, S // 16], U16, name="tap_t")
         xw = sb([P, T], I32, "xw")
         xs = sb([P, T], U8, "xs")
-        raw1 = sb([P, PACK, H], F32, "raw1")
-        warm = sb([P, 16], F32, "raw2")
+        warm = sb([P, 16], F32, "raw2_0")
+        warm_out = sb([P, 16], F32, "raw2_1")
 
         nc.gpsimd.memset(xs[:].bitcast(I32), 0)
-        nc.sync.dma_start(xw[:], x_words[0].rearrange("p n t -> p (n t)").bitcast(I32))
         nc.sync.dma_start(offs_t[:], offs)
+        nc.sync.dma_start(xw[:], x_words[0].rearrange("p n t -> p (n t)").bitcast(I32))
+        nc.sync.dma_start(tap_t[:], tap)
         for q in range(4):
             nc.sync.dma_start(xs[32 * q : 32 * q + 4, :].bitcast(I32), x_scales[0, 4 * q : 4 * q + 4, :].bitcast(I32))
-        nc.sync.dma_start(tap_t[:], tap)
-        nc.sync.dma_start(raw1[:], w1.rearrange("(p j) c -> p j c", j=PACK))
+        raw1 = [load_half(w1, half, "raw1_%d" % half) for half in range(2)]
         nc.vector.memset(warm[:, 0:8], 0.0)
-        nc.scalar.activation(warm[:, 8:16], warm[:, 0:8], SIGMOID)
-        raw2 = sb([P, PACK, H], F32, "raw2")
-        nc.sync.dma_start(raw2[:], w2.rearrange("(p j) c -> p j c", j=PACK))
+        nc.scalar.activation(warm_out[:, 0:8], warm[:, 0:8], SIGMOID)
+        raw2 = [load_half(w2, half, "raw2_%d" % half) for half in range(2)]
 
         xg_s = sb([P, S], U8, "xg_s")
         xg_w = sb([P, S], U32, "xg_w")
         nc.vector.tensor_copy(xg_w[:], xw[:].bitcast(U32).indirect(offs_t[:]))
         nc.vector.tensor_copy(xg_s[:], xs[:].indirect(offs_t[:]))
 
-        def cast_first(raw, t, g, copy):
-            dst = g.rearrange("p (b h i j) -> p b h j i", h=2, i=4, j=PACK)
-            src = raw[:].rearrange("p j (b t h i) -> p t b h j i", t=PACK, h=2, i=4)[:, t]
+        def round_half(raw, half, g, t0, t1, copy):
+            dst = g[:, t0:t1, half * HALF : (half + 1) * HALF].rearrange("p t (u i j) -> p t u j i", i=4, j=PACK)
+            src = raw[half][:].rearrange("p j (u t i) -> p t u j i", t=PACK, i=4)[:, t0:t1]
             copy(dst, src)
-            return g
 
         def quant(g, width, name):
             codes = sb([P, width], U32, name + "_c")
@@ -72,89 +75,84 @@ def tile_picked_glutap_none_p_kernel(tc, x_words, x_scales, w1, w2, w3, offs, ta
 
         def project(q, c0, width, b):
             acc = bank([P, width], b)
-            nc.tensor.matmul_mx(out=acc[:], lhsT=q[0][:].bitcast(FP8X4), lhsT_scale=q[1][:],
+            nc.tensor.matmul_mx(out=acc[:], lhsT=q[0].bitcast(FP8X4), lhsT_scale=q[1],
                                 rhs=xg_w[:, c0 : c0 + width].bitcast(FP8X4), rhs_scale=xg_s[:, c0 : c0 + width], start=True, stop=True)
             return acc
 
         def tap_add(dst, window, own, c0, width):
             nc.vector.tensor_tensor(dst, window[:].indirect(tap_t[:, c0 // 16 : (c0 + width) // 16]), own, ADD)
 
-        copies1 = (nc.vector.tensor_copy, nc.vector.tensor_copy, nc.scalar.copy, nc.scalar.copy)
-        g1 = [cast_first(raw1, t, sb([P, P * PACK], BF16, "g1_%d" % t)[:], copies1[t]) for t in range(PACK)]
-        q1 = [quant(g1[t], P, "q1_%d" % t) for t in range(PACK)]
+        g1 = sb([P, PACK, P * PACK], BF16, "g1")
+        round_half(raw1, 0, g1, 0, PACK, nc.scalar.copy)
+        q1 = []
+        for t in range(PACK):
+            round_half(raw1, 1, g1, t, t + 1, nc.scalar.copy if t else nc.vector.tensor_copy)
+            codes, scales = quant(g1[:, t, :], P, "q1_%d" % t)
+            q1.append((codes[:], scales[:]))
+        g2 = sb([P, PACK, P * PACK], BF16, "g2")
+        round_half(raw2, 0, g2, 0, PACK - 1, nc.vector.tensor_copy)
+        round_half(raw2, 0, g2, PACK - 1, PACK, nc.scalar.copy)
+
+        round_half(raw2, 1, g2, 0, 2, nc.vector.tensor_copy)
+        round_half(raw2, 1, g2, 2, PACK, nc.vector.tensor_copy)
 
         raw3 = sb([P, PACK, N], F32, "xw")
-        w3v = w3.rearrange("(b t q) n -> t b q n", t=PACK, q=8)
+        w3v = w3.rearrange("(u t i) n -> t u i n", t=PACK, i=4)
         for t in range(PACK):
             nc.sync.dma_start(raw3[:, t, :], w3v[t])
 
-        win = [sb([P, S if u == 0 else 2 * S], F32, "win%d" % u) for u in range(2 * PACK)]
+        widths = [S, 2 * S, 3 * S] + [2 * S] * (PACK + 1)
+        win = [sb([P, widths[u]], F32, "raw2_1" if u == 2 else "win%d" % u) for u in range(2 * PACK)]
         last = sb([P, S], F32, "last")
         own = [win[u + 1][:, S : 2 * S] if u + 1 < 2 * PACK else last[:] for u in range(2 * PACK)]
 
         def leave_bank(q, u, b):
             acc = project(q, 0, S, b)
             nc.scalar.copy(win[u][:, 0:S], acc[:])
+            return acc
 
         def plain_by_dma(u):
             nc.sync.dma_start(own[u], win[u][:, 0:S])
 
-        def plain_by_vector(u):
-            nc.vector.tensor_copy(own[u], win[u][:, 0:S])
-
         def whole_tap(u, name):
             total = sb([P, S], F32, name)
             tap_add(total[:], win[u], own[u], 0, S)
-            return total
+            return total[:]
 
-        g2 = [sb([P, P * PACK], BF16, "g2_%d" % t)[:] for t in range(PACK)]
-        q2 = []
+        def quant_pair(t):
+            codes, scales = quant(g2[:, t : t + 2, :].rearrange("p t c -> p (t c)"), 2 * P, "q2_%d" % t)
+            return [(codes[:, u * P : (u + 1) * P], scales[:, u * P : (u + 1) * P]) for u in range(2)]
 
-        def round_w2(t, copy):
-            cast_first(raw2, t, g2[t], copy)
-
-        def quant_w2(t):
-            q2.append(quant(g2[t], P, "q2_%d" % t))
-
-        ysum = [sb([P, S], F32, "ysum0")]
         ya = project(q1[0], 0, HALF, 0)
         yb = project(q1[0], HALF, HALF, 1)
         nc.scalar.copy(win[0][:, 0:HALF], ya[:])
         nc.vector.tensor_copy(win[0][:, HALF:S], yb[:])
         nc.scalar.copy(own[0][:, 0:HALF], ya[:])
-        round_w2(0, nc.vector.tensor_copy)
+        q2 = quant_pair(0)
+        ysum = [win[2][:, 2 * S :]]
         tap_add(ysum[0][:, 0:HALF], win[0], own[0][:, 0:HALF], 0, HALF)
-        quant_w2(0)
+        q2.extend(quant_pair(2))
         leave_bank(q1[1], 1, 2)
         nc.scalar.copy(own[0][:, HALF:S], yb[:])
-        plain_by_vector(1)
+        nc.vector.tensor_copy(own[1], win[1][:, 0:S])
         tap_add(ysum[0][:, HALF:S], win[0], own[0][:, HALF:S], HALF, HALF)
         ysum.append(whole_tap(1, "ysum1"))
-        round_w2(1, nc.scalar.copy)
-        quant_w2(1)
         leave_bank(q1[3], 3, 4)
         plain_by_dma(3)
-        round_w2(2, nc.scalar.copy)
-        quant_w2(2)
-        leave_bank(q1[2], 2, 3)
-        plain_by_vector(2)
-        ysum.append(whole_tap(2, "ysum2"))
-        leave_bank(q2[0], 4, 5)
-        plain_by_dma(4)
-        round_w2(3, nc.scalar.copy)
-        quant_w2(3)
-        ysum.append(whole_tap(3, "raw2"))
-        for t in range(1, PACK):
+        acc = leave_bank(q1[2], 2, 3)
+        nc.scalar.copy(own[2], acc[:])
+        for t in range(PACK):
             leave_bank(q2[t], PACK + t, (5 + t) % 8)
             plain_by_dma(PACK + t)
+        ysum.extend(whole_tap(t, "ysum%d" % t) for t in range(2, PACK))
         gate = sb([P, PACK, S], F32, "gate")
         for t in range(2):
-            nc.scalar.activation(gate[:, t, :], ysum[t][:], SIGMOID)
-        g3 = sb([P, N * PACK], BF16, "q2_3_c")
+            nc.scalar.activation(gate[:, t, :], ysum[t], SIGMOID)
+        g3 = sb([P, N * PACK], BF16, "q2_2_c")
         nc.scalar.copy(g3[:].rearrange("p (c i j) -> p c j i", i=4, j=PACK), raw3[:].rearrange("p j (c i) -> p c j i", i=4))
         c3, s3 = quant(g3[:], N, "q3")
         for t in range(2, PACK):
-            nc.scalar.activation(gate[:, t, :], ysum[t][:], SIGMOID)
+            nc.scalar.activation(gate[:, t, :], ysum[t], SIGMOID)
         esum = sb([P, PACK, S], F32, "esum")
         for t in range(PACK):
             tap_add(esum[:, t, :], win[PACK + t], own[PACK + t], 0, S)
@@ -175,16 +173,20 @@ def tile_picked_glutap_none_p_kernel(tc, x_words, x_scales, w1, w2, w3, offs, ta
             elif n + 1 == chunks:
                 zs.append(product(n))
             zc, zp = quant(zs[n][:], CHUNK, "z%d" % n)
+            def last_product(dst, m):
+                nc.tensor.matmul_mx(out=dst, lhsT=c3[:, m * P : (m + 1) * P].bitcast(FP8X4), lhsT_scale=s3[:, m * P : (m + 1) * P],
+                                    rhs=zc[:].bitcast(FP8X4), rhs_scale=zp[:], start=True, stop=True)
+
             for half in range(2):
-                acc = bank([P, 2, CHUNK], (1 + 2 * n + half) % 8)
-                for u in range(2):
-                    m = 2 * half + u
-                    nc.tensor.matmul_mx(out=acc[:, u, :], lhsT=c3[:, m * P : (m + 1) * P].bitcast(FP8X4), lhsT_scale=s3[:, m * P : (m + 1) * P],
-                                        rhs=zc[:].bitcast(FP8X4), rhs_scale=zp[:], start=True, stop=True)
                 res = sb([P, 2, CHUNK], F32, "res%d_%d" % (n, half))
-                if n == chunks - 1 and half == 1:
-                    nc.vector.tensor_copy(res[:], acc[:])
-                else:
+                if n + 1 < chunks:
+                    acc = bank([P, 2, CHUNK], 1 + 2 * n + half)
+                    for u in range(2):
+                        last_product(acc[:, u, :], 2 * half + u)
                     nc.scalar.copy(res[:], acc[:])
-                queue = nc.scalar if n == chunks - 1 and half == 0 else nc.sync
-                queue.dma_start(out[2 * half * P : (2 * half + 2) * P, n * CHUNK : (n + 1) * CHUNK].rearrange("(u p) c -> p u c", p=P), res[:])
+                else:
+                    for u in range(2):
+                        acc = bank([P, CHUNK], (7 + 2 * half + u) % 8)
+                        last_product(acc[:], 2 * half + u)
+                        (nc.vector.tensor_copy if u else nc.scalar.copy)(res[:, u, :], acc[:])
+                nc.sync.dma_start(out[2 * half * P : (2 * half + 2) * P, n * CHUNK : (n + 1) * CHUNK].rearrange("(u p) c -> p u c", p=P), res[:])

@@ -47,12 +47,13 @@ def tile_picked_glutap_none_p_kernel(tc, x_words, x_scales, w1, w2, w3, offs, ta
         warm_out = sb([P, 16], F32, "raw2_1")
 
         nc.gpsimd.memset(xs[:].bitcast(I32), 0)
-        nc.sync.dma_start(offs_t[:], offs)
         nc.sync.dma_start(xw[:], x_words[0].rearrange("p n t -> p (n t)").bitcast(I32))
-        nc.sync.dma_start(tap_t[:], tap)
+        nc.sync.dma_start(offs_t[:], offs)
         for q in range(4):
             nc.sync.dma_start(xs[32 * q : 32 * q + 4, :].bitcast(I32), x_scales[0, 4 * q : 4 * q + 4, :].bitcast(I32))
-        raw1 = [load_half(w1, half, "raw1_%d" % half) for half in range(2)]
+        nc.sync.dma_start(tap_t[:], tap)
+        raw1 = sb([P, PACK, H], F32, "raw1")
+        nc.sync.dma_start(raw1[:], w1.rearrange("(p j) c -> p j c", j=PACK))
         nc.vector.memset(warm[:, 0:8], 0.0)
         nc.scalar.activation(warm_out[:, 0:8], warm[:, 0:8], SIGMOID)
         raw2 = [load_half(w2, half, "raw2_%d" % half) for half in range(2)]
@@ -82,16 +83,15 @@ def tile_picked_glutap_none_p_kernel(tc, x_words, x_scales, w1, w2, w3, offs, ta
         def tap_add(dst, window, own, c0, width):
             nc.vector.tensor_tensor(dst, window[:].indirect(tap_t[:, c0 // 16 : (c0 + width) // 16]), own, ADD)
 
-        g1 = sb([P, PACK, P * PACK], BF16, "g1")
-        round_half(raw1, 0, g1, 0, PACK, nc.scalar.copy)
         q1 = []
         for t in range(PACK):
-            round_half(raw1, 1, g1, t, t + 1, nc.scalar.copy if t else nc.vector.tensor_copy)
-            codes, scales = quant(g1[:, t, :], P, "q1_%d" % t)
+            g1 = sb([P, P * PACK], BF16, "g1_%d" % t)
+            copy = nc.scalar.copy if t else nc.vector.tensor_copy
+            copy(g1[:].rearrange("p (u i j) -> p u j i", i=4, j=PACK), raw1[:].rearrange("p j (u t i) -> p t u j i", t=PACK, i=4)[:, t])
+            codes, scales = quant(g1[:], P, "q1_%d" % t)
             q1.append((codes[:], scales[:]))
         g2 = sb([P, PACK, P * PACK], BF16, "g2")
-        round_half(raw2, 0, g2, 0, PACK - 1, nc.vector.tensor_copy)
-        round_half(raw2, 0, g2, PACK - 1, PACK, nc.scalar.copy)
+        round_half(raw2, 0, g2, 0, PACK, nc.vector.tensor_copy)
 
         round_half(raw2, 1, g2, 0, 2, nc.vector.tensor_copy)
         round_half(raw2, 1, g2, 2, PACK, nc.vector.tensor_copy)
@@ -101,10 +101,13 @@ def tile_picked_glutap_none_p_kernel(tc, x_words, x_scales, w1, w2, w3, offs, ta
         for t in range(PACK):
             nc.sync.dma_start(raw3[:, t, :], w3v[t])
 
-        widths = [S, 2 * S, 3 * S] + [2 * S] * (PACK + 1)
+        widths = [S, 2 * S, 2 * S + HALF] + [2 * S] * PACK + [S]
         win = [sb([P, widths[u]], F32, "raw2_1" if u == 2 else "win%d" % u) for u in range(2 * PACK)]
-        last = sb([P, S], F32, "last")
-        own = [win[u + 1][:, S : 2 * S] if u + 1 < 2 * PACK else last[:] for u in range(2 * PACK)]
+        sums = sb([P, PACK * S + CHUNK], F32, "sums")
+        esum = sums[:, 0 : PACK * S].rearrange("p (t c) -> p t c", t=PACK)
+        own = [win[u + 1][:, S : 2 * S] for u in range(PACK + 2)]
+        own.append(sb([P, S], F32, "own6")[:])
+        own7 = (esum[:, PACK - 1, HALF:S], sb([P, HALF], F32, "own7")[:])
 
         def leave_bank(q, u, b):
             acc = project(q, 0, S, b)
@@ -128,51 +131,59 @@ def tile_picked_glutap_none_p_kernel(tc, x_words, x_scales, w1, w2, w3, offs, ta
         nc.scalar.copy(win[0][:, 0:HALF], ya[:])
         nc.vector.tensor_copy(win[0][:, HALF:S], yb[:])
         nc.scalar.copy(own[0][:, 0:HALF], ya[:])
+        ysum0 = (sb([P, HALF], F32, "ysum0")[:], win[2][:, 2 * S :])
+        tap_add(ysum0[0], win[0], own[0][:, 0:HALF], 0, HALF)
         q2 = quant_pair(0)
-        ysum = [win[2][:, 2 * S :]]
-        tap_add(ysum[0][:, 0:HALF], win[0], own[0][:, 0:HALF], 0, HALF)
         q2.extend(quant_pair(2))
         leave_bank(q1[1], 1, 2)
         nc.scalar.copy(own[0][:, HALF:S], yb[:])
         nc.vector.tensor_copy(own[1], win[1][:, 0:S])
-        tap_add(ysum[0][:, HALF:S], win[0], own[0][:, HALF:S], HALF, HALF)
-        ysum.append(whole_tap(1, "ysum1"))
+        tap_add(ysum0[1], win[0], own[0][:, HALF:S], HALF, HALF)
+        ysum = [None, whole_tap(1, "ysum1")]
         leave_bank(q1[3], 3, 4)
         plain_by_dma(3)
         acc = leave_bank(q1[2], 2, 3)
         nc.scalar.copy(own[2], acc[:])
-        for t in range(PACK):
-            leave_bank(q2[t], PACK + t, (5 + t) % 8)
+        for t in range(PACK - 1):
+            leave_bank(q2[t], PACK + t, 5 + t)
             plain_by_dma(PACK + t)
         ysum.extend(whole_tap(t, "ysum%d" % t) for t in range(2, PACK))
         gate = sb([P, PACK, S], F32, "gate")
-        for t in range(2):
+        for half in range(2):
+            nc.scalar.activation(gate[:, 0, half * HALF : (half + 1) * HALF], ysum0[half], SIGMOID)
+        nc.scalar.activation(gate[:, 1, :], ysum[1], SIGMOID)
+        leave_bank(q2[3], 7, 0)
+        for half in range(2):
+            nc.sync.dma_start(own7[half], win[7][:, half * HALF : (half + 1) * HALF])
+        for t in range(2, PACK):
             nc.scalar.activation(gate[:, t, :], ysum[t], SIGMOID)
         g3 = sb([P, N * PACK], BF16, "q2_2_c")
         nc.scalar.copy(g3[:].rearrange("p (c i j) -> p c j i", i=4, j=PACK), raw3[:].rearrange("p j (c i) -> p c j i", i=4))
-        c3, s3 = quant(g3[:], N, "q3")
-        for t in range(2, PACK):
-            nc.scalar.activation(gate[:, t, :], ysum[t], SIGMOID)
-        esum = sb([P, PACK, S], F32, "esum")
-        for t in range(PACK):
+        for t in range(PACK - 1):
             tap_add(esum[:, t, :], win[PACK + t], own[PACK + t], 0, S)
+        tap_add(esum[:, PACK - 1, 0:HALF], win[7], own7[0], 0, HALF)
+        c3, s3 = quant(g3[:], N, "q3")
+
+        def last_tap(n):
+            tap_add(esum[:, PACK - 1, n * CHUNK : (n + 1) * CHUNK], win[7], own7[1][:, n * CHUNK - HALF : (n + 1) * CHUNK - HALF], n * CHUNK, CHUNK)
 
         def product(n):
             cols = slice(n * CHUNK, (n + 1) * CHUNK)
-            z = sb([P, CHUNK * PACK], BF16, "z%d" % (n if n < 3 else 1))
-            nc.vector.tensor_tensor(z[:].rearrange("p (c i j) -> p c j i", i=2, j=PACK),
+            z = sums[:, PACK * S - CHUNK :].bitcast(BF16) if n == 1 else sb([P, CHUNK * PACK], BF16, "z%d" % n)[:]
+            nc.vector.tensor_tensor(z.rearrange("p (c i j) -> p c j i", i=2, j=PACK),
                                     esum[:, :, cols].rearrange("p j (c i) -> p c j i", i=2),
                                     gate[:, :, cols].rearrange("p j (c i) -> p c j i", i=2), MULT)
             return z
 
         chunks = S // CHUNK
-        zs = [product(0)]
+        zs = [product(0), product(1)]
         for n in range(chunks):
-            if n + 2 < chunks:
-                zs.append(product(n + 1))
-            elif n + 1 == chunks:
+            if n >= 2:
                 zs.append(product(n))
-            zc, zp = quant(zs[n][:], CHUNK, "z%d" % n)
+            if n in (1, 2):
+                last_tap(n + 1)
+            zc, zp = quant(zs[n], CHUNK, "z%d" % n)
+
             def last_product(dst, m):
                 nc.tensor.matmul_mx(out=dst, lhsT=c3[:, m * P : (m + 1) * P].bitcast(FP8X4), lhsT_scale=s3[:, m * P : (m + 1) * P],
                                     rhs=zc[:].bitcast(FP8X4), rhs_scale=zp[:], start=True, stop=True)

@@ -49,11 +49,11 @@ def tile_picked_glutap_none_p_kernel(tc, x_words, x_scales, w1, w2, w3, offs, ta
         nc.gpsimd.memset(xs[:].bitcast(I32), 0)
         nc.sync.dma_start(xw[:], x_words[0].rearrange("p n t -> p (n t)").bitcast(I32))
         nc.sync.dma_start(offs_t[:], offs)
-        for q in range(4):
-            nc.sync.dma_start(xs[32 * q : 32 * q + 4, :].bitcast(I32), x_scales[0, 4 * q : 4 * q + 4, :].bitcast(I32))
-        nc.sync.dma_start(tap_t[:], tap)
+        for r in range(4):
+            nc.sync.dma_start(xs[r:P:32, :].bitcast(I32), x_scales[0, r:16:4, :].bitcast(I32))
         raw1 = sb([P, PACK, H], F32, "raw1")
         nc.sync.dma_start(raw1[:], w1.rearrange("(p j) c -> p j c", j=PACK))
+        nc.sync.dma_start(tap_t[:], tap)
         nc.vector.memset(warm[:, 0:8], 0.0)
         nc.scalar.activation(warm_out[:, 0:8], warm[:, 0:8], SIGMOID)
         raw2 = [load_half(w2, half, "raw2_%d" % half) for half in range(2)]
@@ -83,26 +83,39 @@ def tile_picked_glutap_none_p_kernel(tc, x_words, x_scales, w1, w2, w3, offs, ta
         def tap_add(dst, window, own, c0, width):
             nc.vector.tensor_tensor(dst, window[:].indirect(tap_t[:, c0 // 16 : (c0 + width) // 16]), own, ADD)
 
-        q1 = []
+        def quant_tiles(g, t0, t1, name):
+            codes, scales = quant(g[:, t0:t1, :].rearrange("p t c -> p (t c)"), (t1 - t0) * P, "%s_%d" % (name, t0))
+            return [(codes[:, u * P : (u + 1) * P], scales[:, u * P : (u + 1) * P]) for u in range(t1 - t0)]
+
+        g1 = sb([P, PACK, P * PACK], BF16, "g1")
         for t in range(PACK):
-            g1 = sb([P, P * PACK], BF16, "g1_%d" % t)
             copy = nc.scalar.copy if t else nc.vector.tensor_copy
-            copy(g1[:].rearrange("p (u i j) -> p u j i", i=4, j=PACK), raw1[:].rearrange("p j (u t i) -> p t u j i", t=PACK, i=4)[:, t])
-            codes, scales = quant(g1[:], P, "q1_%d" % t)
-            q1.append((codes[:], scales[:]))
+            copy(g1[:, t, :].rearrange("p (u i j) -> p u j i", i=4, j=PACK), raw1[:].rearrange("p j (u t i) -> p t u j i", t=PACK, i=4)[:, t])
+        q1 = quant_tiles(g1, 0, 1, "q1") + quant_tiles(g1, 1, 2, "q1")
         g2 = sb([P, PACK, P * PACK], BF16, "g2")
         round_half(raw2, 0, g2, 0, PACK, nc.vector.tensor_copy)
-
-        round_half(raw2, 1, g2, 0, 2, nc.vector.tensor_copy)
-        round_half(raw2, 1, g2, 2, PACK, nc.vector.tensor_copy)
 
         raw3 = sb([P, PACK, N], F32, "xw")
         w3v = w3.rearrange("(u t i) n -> t u i n", t=PACK, i=4)
         for t in range(PACK):
             nc.sync.dma_start(raw3[:, t, :], w3v[t])
 
-        widths = [S, 2 * S, 2 * S + HALF] + [2 * S] * PACK + [S]
-        win = [sb([P, widths[u]], F32, "raw2_1" if u == 2 else "win%d" % u) for u in range(2 * PACK)]
+        win = [sb([P, S], F32, "win0"), sb([P, 2 * S], F32, "win1")]
+        ya = project(q1[0], 0, HALF, 0)
+        yb = project(q1[0], HALF, HALF, 1)
+        nc.scalar.copy(win[0][:, 0:HALF], ya[:])
+        nc.vector.tensor_copy(win[0][:, HALF:S], yb[:])
+        nc.scalar.copy(win[1][:, S : S + HALF], ya[:])
+        q1.extend(quant_tiles(g1, 2, PACK, "q1"))
+        first = sb([P, HALF], F32, "ysum0")
+        tap_add(first[:], win[0], win[1][:, S : S + HALF], 0, HALF)
+        round_half(raw2, 1, g2, 0, 2, nc.vector.tensor_copy)
+        round_half(raw2, 1, g2, 2, PACK, nc.vector.tensor_copy)
+
+        win.append(sb([P, 2 * S + HALF], F32, "raw2_1"))
+        win.extend(sb([P, 2 * S], F32, "win%d" % u) for u in range(3, 2 * PACK - 1))
+        win.append(sb([P, S], F32, "win7"))
+        ysum0 = (first[:], win[2][:, 2 * S :])
         sums = sb([P, PACK * S + CHUNK], F32, "sums")
         esum = sums[:, 0 : PACK * S].rearrange("p (t c) -> p t c", t=PACK)
         own = [win[u + 1][:, S : 2 * S] for u in range(PACK + 2)]
@@ -122,19 +135,7 @@ def tile_picked_glutap_none_p_kernel(tc, x_words, x_scales, w1, w2, w3, offs, ta
             tap_add(total[:], win[u], own[u], 0, S)
             return total[:]
 
-        def quant_pair(t):
-            codes, scales = quant(g2[:, t : t + 2, :].rearrange("p t c -> p (t c)"), 2 * P, "q2_%d" % t)
-            return [(codes[:, u * P : (u + 1) * P], scales[:, u * P : (u + 1) * P]) for u in range(2)]
-
-        ya = project(q1[0], 0, HALF, 0)
-        yb = project(q1[0], HALF, HALF, 1)
-        nc.scalar.copy(win[0][:, 0:HALF], ya[:])
-        nc.vector.tensor_copy(win[0][:, HALF:S], yb[:])
-        nc.scalar.copy(own[0][:, 0:HALF], ya[:])
-        ysum0 = (sb([P, HALF], F32, "ysum0")[:], win[2][:, 2 * S :])
-        tap_add(ysum0[0], win[0], own[0][:, 0:HALF], 0, HALF)
-        q2 = quant_pair(0)
-        q2.extend(quant_pair(2))
+        q2 = quant_tiles(g2, 0, 2, "q2") + quant_tiles(g2, 2, PACK, "q2")
         leave_bank(q1[1], 1, 2)
         nc.scalar.copy(own[0][:, HALF:S], yb[:])
         nc.vector.tensor_copy(own[1], win[1][:, 0:S])
@@ -188,16 +189,19 @@ def tile_picked_glutap_none_p_kernel(tc, x_words, x_scales, w1, w2, w3, offs, ta
                 nc.tensor.matmul_mx(out=dst, lhsT=c3[:, m * P : (m + 1) * P].bitcast(FP8X4), lhsT_scale=s3[:, m * P : (m + 1) * P],
                                     rhs=zc[:].bitcast(FP8X4), rhs_scale=zp[:], start=True, stop=True)
 
-            for half in range(2):
-                res = sb([P, 2, CHUNK], F32, "res%d_%d" % (n, half))
-                if n + 1 < chunks:
+            cols = slice(n * CHUNK, (n + 1) * CHUNK)
+            if n + 1 < chunks:
+                for half in range(2):
                     acc = bank([P, 2, CHUNK], 1 + 2 * n + half)
                     for u in range(2):
                         last_product(acc[:, u, :], 2 * half + u)
+                    res = sb([P, 2, CHUNK], F32, "res%d_%d" % (n, half))
                     nc.scalar.copy(res[:], acc[:])
-                else:
-                    for u in range(2):
-                        acc = bank([P, CHUNK], (7 + 2 * half + u) % 8)
-                        last_product(acc[:], 2 * half + u)
-                        (nc.vector.tensor_copy if u else nc.scalar.copy)(res[:, u, :], acc[:])
-                nc.sync.dma_start(out[2 * half * P : (2 * half + 2) * P, n * CHUNK : (n + 1) * CHUNK].rearrange("(u p) c -> p u c", p=P), res[:])
+                    nc.sync.dma_start(out[2 * half * P : (2 * half + 2) * P, cols].rearrange("(u p) c -> p u c", p=P), res[:])
+            else:
+                for m in range(PACK):
+                    acc = bank([P, CHUNK], (7 + m) % 8)
+                    last_product(acc[:], m)
+                    res = sb([P, CHUNK], F32, "res%d_%d" % (n, m))
+                    (nc.vector.tensor_copy if m % 2 else nc.scalar.copy)(res[:], acc[:])
+                    nc.sync.dma_start(out[m * P : (m + 1) * P, cols], res[:])

@@ -34,44 +34,40 @@ def tile_picked_glutap_none_p_kernel(tc, x_words, x_scales, w1, w2, w3, offs, ta
         def bank(shape, b):
             return psum.tile(shape, F32, name="bank%d" % b)
 
-        def load_half(w, half, name):
-            raw = sb([P, PACK, HALF], F32, name)
-            nc.sync.dma_start(raw[:], w.rearrange("(p j) c -> p j c", j=PACK)[:, :, half * HALF : (half + 1) * HALF])
-            return raw
-
         offs_t = keep.tile([P, S // 16], U16, name="offs_t")
         tap_t = keep.tile([P, S // 16], U16, name="tap_t")
         xw = sb([P, T], I32, "xw")
         xs = sb([P, T], U8, "xs")
-        warm = sb([P, 16], F32, "raw2_0")
-        warm_out = sb([P, 16], F32, "raw2_1")
+        warm = sb([P, 16], F32, "warm")
+        warm_out = sb([P, 16], F32, "warm_out")
+        raw1 = sb([P, PACK, H], F32, "raw1")
+        raw2 = [sb([P, PACK, HALF], F32, "raw2_%d" % half) for half in range(2)]
 
         nc.gpsimd.memset(xs[:].bitcast(I32), 0)
-        nc.sync.dma_start(xw[:], x_words[0].rearrange("p n t -> p (n t)").bitcast(I32))
+        nc.sync.dma_start(raw1[:], w1.rearrange("(p j) c -> p j c", j=PACK))
         nc.sync.dma_start(offs_t[:], offs)
         for r in range(4):
             nc.sync.dma_start(xs[r:P:32, :].bitcast(I32), x_scales[0, r:16:4, :].bitcast(I32))
-        raw1 = sb([P, PACK, H], F32, "raw1")
-        nc.sync.dma_start(raw1[:], w1.rearrange("(p j) c -> p j c", j=PACK))
+        nc.sync.dma_start(xw[:], x_words[0].rearrange("p n t -> p (n t)").bitcast(I32))
         nc.sync.dma_start(tap_t[:], tap)
         nc.vector.memset(warm[:, 0:8], 0.0)
         nc.scalar.activation(warm_out[:, 0:8], warm[:, 0:8], SIGMOID)
-        raw2 = [load_half(w2, half, "raw2_%d" % half) for half in range(2)]
+        for half in range(2):
+            nc.sync.dma_start(raw2[half][:], w2.rearrange("(p j) c -> p j c", j=PACK)[:, :, half * HALF : (half + 1) * HALF])
 
         xg_s = sb([P, S], U8, "xg_s")
         xg_w = sb([P, S], U32, "xg_w")
-        nc.vector.tensor_copy(xg_w[:], xw[:].bitcast(U32).indirect(offs_t[:]))
-        nc.vector.tensor_copy(xg_s[:], xs[:].indirect(offs_t[:]))
 
-        def round_half(raw, half, g, t0, t1, copy):
-            dst = g[:, t0:t1, half * HALF : (half + 1) * HALF].rearrange("p t (u i j) -> p t u j i", i=4, j=PACK)
-            src = raw[half][:].rearrange("p j (u t i) -> p t u j i", t=PACK, i=4)[:, t0:t1]
+        def round_half(half, pair, copy):
+            dst = g2[pair][:, :, half * HALF : (half + 1) * HALF].rearrange("p t (u i j) -> p t u j i", i=4, j=PACK)
+            src = raw2[half][:].rearrange("p j (u t i) -> p t u j i", t=PACK, i=4)[:, 2 * pair : 2 * pair + 2]
             copy(dst, src)
 
-        def quant(g, width, name):
-            codes = sb([P, width], U32, name + "_c")
+        def quant(g, width, name, codes=None):
+            if codes is None:
+                codes = sb([P, width], U32, name + "_c")[:]
             scales = sb([P, width], U8, name + "_s")
-            nc.vector.quantize_mx(out=codes[:].bitcast(FP8X4), scales=scales[:], in_=g)
+            nc.vector.quantize_mx(out=codes.bitcast(FP8X4), scales=scales[:], in_=g)
             return codes, scales
 
         def project(q, c0, width, b):
@@ -83,39 +79,28 @@ def tile_picked_glutap_none_p_kernel(tc, x_words, x_scales, w1, w2, w3, offs, ta
         def tap_add(dst, window, own, c0, width):
             nc.vector.tensor_tensor(dst, window[:].indirect(tap_t[:, c0 // 16 : (c0 + width) // 16]), own, ADD)
 
-        def quant_tiles(g, t0, t1, name):
-            codes, scales = quant(g[:, t0:t1, :].rearrange("p t c -> p (t c)"), (t1 - t0) * P, "%s_%d" % (name, t0))
+        def quant_tiles(g, t0, t1, name, codes=None):
+            codes, scales = quant(g[:, t0:t1, :].rearrange("p t c -> p (t c)"), (t1 - t0) * P, "%s_%d" % (name, t0), codes)
             return [(codes[:, u * P : (u + 1) * P], scales[:, u * P : (u + 1) * P]) for u in range(t1 - t0)]
 
         g1 = sb([P, PACK, P * PACK], BF16, "g1")
         for t in range(PACK):
             copy = nc.scalar.copy if t else nc.vector.tensor_copy
             copy(g1[:, t, :].rearrange("p (u i j) -> p u j i", i=4, j=PACK), raw1[:].rearrange("p j (u t i) -> p t u j i", t=PACK, i=4)[:, t])
-        q1 = quant_tiles(g1, 0, 1, "q1") + quant_tiles(g1, 1, 2, "q1")
-        g2 = sb([P, PACK, P * PACK], BF16, "g2")
-        round_half(raw2, 0, g2, 0, PACK, nc.vector.tensor_copy)
-
+        nc.vector.tensor_copy(xg_s[:], xs[:].indirect(offs_t[:]))
+        c1 = sb([P, PACK * P], U32, "xs")
+        q1 = quant_tiles(g1, 0, 2, "q1", c1[:, 0 : 2 * P]) + quant_tiles(g1, 2, PACK, "q1", c1[:, 2 * P :])
+        for half in range(2):
+            nc.vector.tensor_copy(xg_w[:, half * HALF : (half + 1) * HALF], xw[:].bitcast(U32).indirect(offs_t[:, half * HALF // 16 : (half + 1) * HALF // 16]))
+        g2 = [sb([P, 2, P * PACK], BF16, "g2_%d" % pair) for pair in range(2)]
+        for pair in range(2):
+            round_half(0, pair, nc.vector.tensor_copy)
         raw3 = sb([P, PACK, N], F32, "xw")
         w3v = w3.rearrange("(u t i) n -> t u i n", t=PACK, i=4)
         for t in range(PACK):
             nc.sync.dma_start(raw3[:, t, :], w3v[t])
 
-        win = [sb([P, S], F32, "win0"), sb([P, 2 * S], F32, "win1")]
-        ya = project(q1[0], 0, HALF, 0)
-        yb = project(q1[0], HALF, HALF, 1)
-        nc.scalar.copy(win[0][:, 0:HALF], ya[:])
-        nc.vector.tensor_copy(win[0][:, HALF:S], yb[:])
-        nc.scalar.copy(win[1][:, S : S + HALF], ya[:])
-        q1.extend(quant_tiles(g1, 2, PACK, "q1"))
-        first = sb([P, HALF], F32, "ysum0")
-        tap_add(first[:], win[0], win[1][:, S : S + HALF], 0, HALF)
-        round_half(raw2, 1, g2, 0, 2, nc.vector.tensor_copy)
-        round_half(raw2, 1, g2, 2, PACK, nc.vector.tensor_copy)
-
-        win.append(sb([P, 2 * S + HALF], F32, "raw2_1"))
-        win.extend(sb([P, 2 * S], F32, "win%d" % u) for u in range(3, 2 * PACK - 1))
-        win.append(sb([P, S], F32, "win7"))
-        ysum0 = (first[:], win[2][:, 2 * S :])
+        win = [sb([P, S], F32, "win0")] + [sb([P, 2 * S], F32, "win%d" % u) for u in range(1, 2 * PACK - 1)] + [sb([P, S], F32, "win7")]
         sums = sb([P, PACK * S + CHUNK], F32, "sums")
         esum = sums[:, 0 : PACK * S].rearrange("p (t c) -> p t c", t=PACK)
         own = [win[u + 1][:, S : 2 * S] for u in range(PACK + 2)]
@@ -130,36 +115,43 @@ def tile_picked_glutap_none_p_kernel(tc, x_words, x_scales, w1, w2, w3, offs, ta
         def plain_by_dma(u):
             nc.sync.dma_start(own[u], win[u][:, 0:S])
 
-        def whole_tap(u, name):
-            total = sb([P, S], F32, name)
-            tap_add(total[:], win[u], own[u], 0, S)
-            return total[:]
-
-        q2 = quant_tiles(g2, 0, 2, "q2") + quant_tiles(g2, 2, PACK, "q2")
-        leave_bank(q1[1], 1, 2)
+        ya = project(q1[0], 0, HALF, 0)
+        yb = project(q1[0], HALF, HALF, 1)
+        nc.scalar.copy(win[0][:, 0:HALF], ya[:])
+        nc.scalar.copy(own[0][:, 0:HALF], ya[:])
+        nc.scalar.copy(win[0][:, HALF:S], yb[:])
+        ysum0a = sb([P, HALF], F32, "raw2_0")
+        tap_add(ysum0a[:], win[0], own[0][:, 0:HALF], 0, HALF)
+        for u in (2, 3):
+            leave_bank(q1[u], u, u)
+            plain_by_dma(u)
         nc.scalar.copy(own[0][:, HALF:S], yb[:])
-        nc.vector.tensor_copy(own[1], win[1][:, 0:S])
-        tap_add(ysum0[1], win[0], own[0][:, HALF:S], HALF, HALF)
-        ysum = [None, whole_tap(1, "ysum1")]
-        leave_bank(q1[3], 3, 4)
-        plain_by_dma(3)
-        acc = leave_bank(q1[2], 2, 3)
-        nc.scalar.copy(own[2], acc[:])
-        for t in range(PACK - 1):
-            leave_bank(q2[t], PACK + t, 5 + t)
-            plain_by_dma(PACK + t)
-        ysum.extend(whole_tap(t, "ysum%d" % t) for t in range(2, PACK))
-        gate = sb([P, PACK, S], F32, "gate")
-        for half in range(2):
-            nc.scalar.activation(gate[:, 0, half * HALF : (half + 1) * HALF], ysum0[half], SIGMOID)
-        nc.scalar.activation(gate[:, 1, :], ysum[1], SIGMOID)
-        leave_bank(q2[3], 7, 0)
+        acc = leave_bank(q1[1], 1, 4)
+        nc.scalar.copy(own[1], acc[:])
+        for pair in range(2):
+            round_half(1, pair, nc.vector.tensor_copy)
+        q2 = quant_tiles(g2[0], 0, 2, "q2a") + quant_tiles(g2[1], 0, 2, "q2b")
+        for t in range(PACK):
+            leave_bank(q2[t], PACK + t, (5 + t) % 8)
+            if t + 1 < PACK:
+                plain_by_dma(PACK + t)
         for half in range(2):
             nc.sync.dma_start(own7[half], win[7][:, half * HALF : (half + 1) * HALF])
+        ysum0b = sb([P, HALF], F32, "g2_0")
+        tap_add(ysum0b[:], win[0], own[0][:, HALF:S], HALF, HALF)
+        ysum1 = sb([P, S], F32, "g2_1")
+        ysum23 = sb([P, 2, S], F32, "raw2_1")
+        ysum = [None, ysum1[:], ysum23[:, 0, :], ysum23[:, 1, :]]
+        for t in range(1, PACK):
+            tap_add(ysum[t], win[t], own[t], 0, S)
+        gate = sb([P, PACK, S], F32, "q2b_0_s")
+        nc.scalar.activation(gate[:, 0, 0:HALF], ysum0a[:], SIGMOID)
+        nc.scalar.activation(gate[:, 0, HALF:S], ysum0b[:], SIGMOID)
+        nc.scalar.activation(gate[:, 1, :], ysum[1], SIGMOID)
+        g3 = sb([P, N * PACK], BF16, "q2b_0_c")
+        nc.scalar.copy(g3[:].rearrange("p (c i j) -> p c j i", i=4, j=PACK), raw3[:].rearrange("p j (c i) -> p c j i", i=4))
         for t in range(2, PACK):
             nc.scalar.activation(gate[:, t, :], ysum[t], SIGMOID)
-        g3 = sb([P, N * PACK], BF16, "q2_2_c")
-        nc.scalar.copy(g3[:].rearrange("p (c i j) -> p c j i", i=4, j=PACK), raw3[:].rearrange("p j (c i) -> p c j i", i=4))
         for t in range(PACK - 1):
             tap_add(esum[:, t, :], win[PACK + t], own[PACK + t], 0, S)
         tap_add(esum[:, PACK - 1, 0:HALF], win[7], own7[0], 0, HALF)
@@ -187,7 +179,7 @@ def tile_picked_glutap_none_p_kernel(tc, x_words, x_scales, w1, w2, w3, offs, ta
 
             def last_product(dst, m):
                 nc.tensor.matmul_mx(out=dst, lhsT=c3[:, m * P : (m + 1) * P].bitcast(FP8X4), lhsT_scale=s3[:, m * P : (m + 1) * P],
-                                    rhs=zc[:].bitcast(FP8X4), rhs_scale=zp[:], start=True, stop=True)
+                                    rhs=zc.bitcast(FP8X4), rhs_scale=zp[:], start=True, stop=True)
 
             cols = slice(n * CHUNK, (n + 1) * CHUNK)
             if n + 1 < chunks:

@@ -41,21 +41,21 @@ def tile_picked_glutap_none_p_kernel(tc, x_words, x_scales, w1, w2, w3, offs, ta
         warm = sb([P, 16], F32, "warm")
         warm_out = sb([P, 16], F32, "warm_out")
         raw1 = sb([P, PACK, H], F32, "raw1")
-        raw2 = [sb([P, PACK, HALF], F32, "raw2_%d" % half) for half in range(2)]
+        xg_s = sb([P, S], U8, "xg_s")
 
         nc.gpsimd.memset(xs[:].bitcast(I32), 0)
-        nc.sync.dma_start(raw1[:], w1.rearrange("(p j) c -> p j c", j=PACK))
+        nc.gpsimd.memset(xg_s[:].bitcast(I32), 0)
+        w1v = w1.rearrange("(p j) c -> p j c", j=PACK)
+        nc.sync.dma_start(raw1[:, 0:2, :], w1v[:, 0:2, :])
         nc.sync.dma_start(offs_t[:], offs)
-        for r in range(4):
-            nc.sync.dma_start(xs[r:P:32, :].bitcast(I32), x_scales[0, r:16:4, :].bitcast(I32))
+        nc.sync.dma_start(xs[0:P:8, :].bitcast(I32), x_scales[0].bitcast(I32))
+        nc.sync.dma_start(raw1[:, 2:PACK, :], w1v[:, 2:PACK, :])
         nc.sync.dma_start(xw[:], x_words[0].rearrange("p n t -> p (n t)").bitcast(I32))
         nc.sync.dma_start(tap_t[:], tap)
         nc.vector.memset(warm[:, 0:8], 0.0)
         nc.scalar.activation(warm_out[:, 0:8], warm[:, 0:8], SIGMOID)
-        for half in range(2):
-            nc.sync.dma_start(raw2[half][:], w2.rearrange("(p j) c -> p j c", j=PACK)[:, :, half * HALF : (half + 1) * HALF])
 
-        xg_s = sb([P, S], U8, "xg_s")
+        picked = sb([P, S], U8, "picked")
         xg_w = sb([P, S], U32, "xg_w")
 
         def round_half(half, pair, copy):
@@ -84,12 +84,18 @@ def tile_picked_glutap_none_p_kernel(tc, x_words, x_scales, w1, w2, w3, offs, ta
             return [(codes[:, u * P : (u + 1) * P], scales[:, u * P : (u + 1) * P]) for u in range(t1 - t0)]
 
         g1 = sb([P, PACK, P * PACK], BF16, "g1")
-        for t in range(PACK):
-            copy = nc.scalar.copy if t else nc.vector.tensor_copy
-            copy(g1[:, t, :].rearrange("p (u i j) -> p u j i", i=4, j=PACK), raw1[:].rearrange("p j (u t i) -> p t u j i", t=PACK, i=4)[:, t])
-        nc.vector.tensor_copy(xg_s[:], xs[:].indirect(offs_t[:]))
-        c1 = sb([P, PACK * P], U32, "xs")
-        q1 = quant_tiles(g1, 0, 2, "q1", c1[:, 0 : 2 * P]) + quant_tiles(g1, 2, PACK, "q1", c1[:, 2 * P :])
+        nc.vector.tensor_copy(picked[:], xs[:].indirect(offs_t[:]))
+        for r in range(4):
+            nc.sync.dma_start(xg_s[r:P:32, :].bitcast(I32), picked[8 * r : P : 32, :].bitcast(I32))
+        dst1 = g1[:].rearrange("p t (u i j) -> p t u j i", i=4, j=PACK)
+        src1 = raw1[:].rearrange("p j (u t i) -> p t u j i", t=PACK, i=4)
+        nc.vector.tensor_copy(dst1[:, 0:2], src1[:, 0:2])
+        for t in range(2, PACK):
+            nc.scalar.copy(dst1[:, t], src1[:, t])
+        raw2 = [sb([P, PACK, HALF], F32, name) for name in ("xs", "raw1")]
+        for half in range(2):
+            nc.sync.dma_start(raw2[half][:], w2.rearrange("(p j) c -> p j c", j=PACK)[:, :, half * HALF : (half + 1) * HALF])
+        q1 = quant_tiles(g1, 0, 2, "q1") + quant_tiles(g1, 2, PACK, "q1")
         for half in range(2):
             nc.vector.tensor_copy(xg_w[:, half * HALF : (half + 1) * HALF], xw[:].bitcast(U32).indirect(offs_t[:, half * HALF // 16 : (half + 1) * HALF // 16]))
         g2 = [sb([P, 2, P * PACK], BF16, "g2_%d" % pair) for pair in range(2)]
@@ -120,7 +126,7 @@ def tile_picked_glutap_none_p_kernel(tc, x_words, x_scales, w1, w2, w3, offs, ta
         nc.scalar.copy(win[0][:, 0:HALF], ya[:])
         nc.scalar.copy(own[0][:, 0:HALF], ya[:])
         nc.scalar.copy(win[0][:, HALF:S], yb[:])
-        ysum0a = sb([P, HALF], F32, "raw2_0")
+        ysum0a = sb([P, HALF], F32, "xs")
         tap_add(ysum0a[:], win[0], own[0][:, 0:HALF], 0, HALF)
         for u in (2, 3):
             leave_bank(q1[u], u, u)
@@ -140,7 +146,7 @@ def tile_picked_glutap_none_p_kernel(tc, x_words, x_scales, w1, w2, w3, offs, ta
         ysum0b = sb([P, HALF], F32, "g2_0")
         tap_add(ysum0b[:], win[0], own[0][:, HALF:S], HALF, HALF)
         ysum1 = sb([P, S], F32, "g2_1")
-        ysum23 = sb([P, 2, S], F32, "raw2_1")
+        ysum23 = sb([P, 2, S], F32, "raw1")
         ysum = [None, ysum1[:], ysum23[:, 0, :], ysum23[:, 1, :]]
         for t in range(1, PACK):
             tap_add(ysum[t], win[t], own[t], 0, S)

@@ -1,6 +1,7 @@
 from contextlib import ExitStack
 
 import concourse.mybir as mybir
+from concourse.masks import make_identity
 
 K, T, S, N, H = 512, 2048, 512, 512, 512
 FLOPS = 2 * K * H * S * 2 + 2 * H * N * S
@@ -45,6 +46,8 @@ def tile_picked_glutap_none_p_kernel(tc, x_words, x_scales, w1, w2, w3, offs, ta
 
         nc.gpsimd.memset(xs[:].bitcast(I32), 0)
         nc.gpsimd.memset(xg_s[:].bitcast(I32), 0)
+        ident = sb([P, P], F32, "ident")
+        make_identity(nc, ident[:])
         w1v = w1.rearrange("(p j) c -> p j c", j=PACK)
         nc.sync.dma_start(raw1[:, 0:2, :], w1v[:, 0:2, :])
         nc.sync.dma_start(offs_t[:], offs)
@@ -60,7 +63,7 @@ def tile_picked_glutap_none_p_kernel(tc, x_words, x_scales, w1, w2, w3, offs, ta
 
         def round_half(half, pair, copy):
             dst = g2[pair][:, :, half * HALF : (half + 1) * HALF].rearrange("p t (u i j) -> p t u j i", i=4, j=PACK)
-            src = raw2[half][:].rearrange("p j (u t i) -> p t u j i", t=PACK, i=4)[:, 2 * pair : 2 * pair + 2]
+            src = raw2[half].rearrange("p j (u t i) -> p t u j i", t=PACK, i=4)[:, 2 * pair : 2 * pair + 2]
             copy(dst, src)
 
         def quant(g, width, name, codes=None):
@@ -92,9 +95,14 @@ def tile_picked_glutap_none_p_kernel(tc, x_words, x_scales, w1, w2, w3, offs, ta
         nc.vector.tensor_copy(dst1[:, 0:2], src1[:, 0:2])
         for t in range(2, PACK):
             nc.scalar.copy(dst1[:, t], src1[:, t])
-        raw2 = [sb([P, PACK, HALF], F32, name) for name in ("xs", "raw1")]
+        win = [sb([P, 3 * S], F32, "xs"), sb([P, 2 * S], F32, "win1"), sb([P, 2 * S], F32, "win2"), sb([P, 2 * S], F32, "raw1")]
+        win.extend(sb([P, 2 * S], F32, "win%d" % u) for u in range(PACK, 2 * PACK - 1))
+        win.append(sb([P, S], F32, "win7"))
+        for u in (2, 4):
+            nc.gpsimd.memset(win[u][:, S:], 0.0)
+        raw2 = [raw.rearrange("p (j c) -> p j c", j=PACK) for raw in (win[0][:, S:], win[3][:])]
         for half in range(2):
-            nc.sync.dma_start(raw2[half][:], w2.rearrange("(p j) c -> p j c", j=PACK)[:, :, half * HALF : (half + 1) * HALF])
+            nc.sync.dma_start(raw2[half], w2.rearrange("(p j) c -> p j c", j=PACK)[:, :, half * HALF : (half + 1) * HALF])
         q1 = quant_tiles(g1, 0, 2, "q1") + quant_tiles(g1, 2, PACK, "q1")
         for half in range(2):
             nc.vector.tensor_copy(xg_w[:, half * HALF : (half + 1) * HALF], xw[:].bitcast(U32).indirect(offs_t[:, half * HALF // 16 : (half + 1) * HALF // 16]))
@@ -106,80 +114,85 @@ def tile_picked_glutap_none_p_kernel(tc, x_words, x_scales, w1, w2, w3, offs, ta
         for t in range(PACK):
             nc.sync.dma_start(raw3[:, t, :], w3v[t])
 
-        win = [sb([P, S], F32, "win0")] + [sb([P, 2 * S], F32, "win%d" % u) for u in range(1, 2 * PACK - 1)] + [sb([P, S], F32, "win7")]
         sums = sb([P, PACK * S + CHUNK], F32, "sums")
         esum = sums[:, 0 : PACK * S].rearrange("p (t c) -> p t c", t=PACK)
-        own = [win[u + 1][:, S : 2 * S] for u in range(PACK + 2)]
-        own.append(sb([P, S], F32, "own6")[:])
-        own7 = (esum[:, PACK - 1, HALF:S], sb([P, HALF], F32, "own7")[:])
 
         def leave_bank(q, u, b):
             acc = project(q, 0, S, b)
             nc.scalar.copy(win[u][:, 0:S], acc[:])
             return acc
 
-        def plain_by_dma(u):
-            nc.sync.dma_start(own[u], win[u][:, 0:S])
+        def turn(dst, src, start, stop):
+            nc.tensor.matmul(dst, lhsT=src, rhs=ident[:], start=start, stop=stop, is_transpose=True)
 
+        def fetch(dst, u):
+            nc.vector.tensor_copy(dst, win[u][:].indirect(tap_t[:]))
+
+        def turned_gate(t, fetched, b):
+            acc = bank([P, chunks, P], b)
+            for n in range(chunks):
+                turn(acc[:, n, :], win[t][:, n * CHUNK : (n + 1) * CHUNK], n == 0, False)
+            for n in range(chunks):
+                turn(acc[:, n, :], fetched[:, n * CHUNK : (n + 1) * CHUNK], False, n + 1 == chunks)
+            turned = sb([P, chunks, P], F32, ("q2a_0_s", "q2b_0_s", "turned2", "turned3")[t])
+            nc.scalar.activation(turned[:], acc[:], SIGMOID)
+            return turned
+
+        chunks = S // CHUNK
         ya = project(q1[0], 0, HALF, 0)
         yb = project(q1[0], HALF, HALF, 1)
         nc.scalar.copy(win[0][:, 0:HALF], ya[:])
-        nc.scalar.copy(own[0][:, 0:HALF], ya[:])
         nc.scalar.copy(win[0][:, HALF:S], yb[:])
-        ysum0a = sb([P, HALF], F32, "xs")
-        tap_add(ysum0a[:], win[0], own[0][:, 0:HALF], 0, HALF)
-        for u in (2, 3):
-            leave_bank(q1[u], u, u)
-            plain_by_dma(u)
-        nc.scalar.copy(own[0][:, HALF:S], yb[:])
-        acc = leave_bank(q1[1], 1, 4)
-        nc.scalar.copy(own[1], acc[:])
-        for pair in range(2):
-            round_half(1, pair, nc.vector.tensor_copy)
+        leave_bank(q1[1], 1, 2)
+        fetch(win[1][:, S:], 0)
+        round_half(1, 0, nc.vector.tensor_copy)
+        round_half(1, 1, nc.scalar.copy)
+        leave_bank(q1[2], 2, 3)
         q2 = quant_tiles(g2[0], 0, 2, "q2a") + quant_tiles(g2[1], 0, 2, "q2b")
+        leave_bank(q1[3], 3, 4)
+        own = {4: win[5][:, S:], 5: win[6][:, S:], 6: sb([P, S], F32, "own6")[:]}
+        own7 = sb([P, S], F32, "own7")
+        accs = []
         for t in range(PACK):
-            leave_bank(q2[t], PACK + t, (5 + t) % 8)
-            if t + 1 < PACK:
-                plain_by_dma(PACK + t)
-        for half in range(2):
-            nc.sync.dma_start(own7[half], win[7][:, half * HALF : (half + 1) * HALF])
-        ysum0b = sb([P, HALF], F32, "g2_0")
-        tap_add(ysum0b[:], win[0], own[0][:, HALF:S], HALF, HALF)
-        ysum1 = sb([P, S], F32, "g2_1")
-        ysum23 = sb([P, 2, S], F32, "raw1")
-        ysum = [None, ysum1[:], ysum23[:, 0, :], ysum23[:, 1, :]]
+            accs.append(leave_bank(q2[t], PACK + t, (5 + t) % 8))
+            if t in (1, 2):
+                nc.sync.dma_start(own[PACK + t], win[PACK + t][:, 0:S])
+            if t == 2:
+                nc.scalar.copy(own[PACK], accs[0][:])
+        nc.sync.dma_start(own7[:], win[7][:])
+        fetched23 = sb([P, 2 * S], F32, "g2_1")
+        fetched = [win[1][:, S:], win[3][:, S:], fetched23[:, 0:S], fetched23[:, S:]]
         for t in range(1, PACK):
-            tap_add(ysum[t], win[t], own[t], 0, S)
-        gate = sb([P, PACK, S], F32, "q2b_0_s")
-        nc.scalar.activation(gate[:, 0, 0:HALF], ysum0a[:], SIGMOID)
-        nc.scalar.activation(gate[:, 0, HALF:S], ysum0b[:], SIGMOID)
-        nc.scalar.activation(gate[:, 1, :], ysum[1], SIGMOID)
-        g3 = sb([P, N * PACK], BF16, "q2b_0_c")
+            fetch(fetched[t], t)
+        turned = [turned_gate(t, fetched[t], (6, 7, 0, 5)[t]) for t in range(PACK)]
+        gate = [bank([P, PACK, CHUNK], (1, 2, 3, 4)[n]) for n in range(chunks)]
+        for t in range(PACK):
+            for n in range(chunks):
+                nc.tensor.transpose(gate[n][:, t, :], turned[t][:, n, :], ident[:])
+        g3 = sb([P, N * PACK], BF16, "q2a_0_s")
         nc.scalar.copy(g3[:].rearrange("p (c i j) -> p c j i", i=4, j=PACK), raw3[:].rearrange("p j (c i) -> p c j i", i=4))
-        for t in range(2, PACK):
-            nc.scalar.activation(gate[:, t, :], ysum[t], SIGMOID)
         for t in range(PACK - 1):
             tap_add(esum[:, t, :], win[PACK + t], own[PACK + t], 0, S)
-        tap_add(esum[:, PACK - 1, 0:HALF], win[7], own7[0], 0, HALF)
-        c3, s3 = quant(g3[:], N, "q3")
+        tap_add(esum[:, PACK - 1, 0:HALF], win[7], own7[:, 0:HALF], 0, HALF)
 
         def last_tap(n):
-            tap_add(esum[:, PACK - 1, n * CHUNK : (n + 1) * CHUNK], win[7], own7[1][:, n * CHUNK - HALF : (n + 1) * CHUNK - HALF], n * CHUNK, CHUNK)
+            tap_add(esum[:, PACK - 1, n * CHUNK : (n + 1) * CHUNK], win[7], own7[:, n * CHUNK : (n + 1) * CHUNK], n * CHUNK, CHUNK)
 
         def product(n):
             cols = slice(n * CHUNK, (n + 1) * CHUNK)
             z = sums[:, PACK * S - CHUNK :].bitcast(BF16) if n == 1 else sb([P, CHUNK * PACK], BF16, "z%d" % n)[:]
             nc.vector.tensor_tensor(z.rearrange("p (c i j) -> p c j i", i=2, j=PACK),
                                     esum[:, :, cols].rearrange("p j (c i) -> p c j i", i=2),
-                                    gate[:, :, cols].rearrange("p j (c i) -> p c j i", i=2), MULT)
+                                    gate[n][:].rearrange("p j (c i) -> p c j i", i=2), MULT)
             return z
 
-        chunks = S // CHUNK
+        last_tap(2)
         zs = [product(0), product(1)]
+        c3, s3 = quant(g3[:], N, "q3")
         for n in range(chunks):
             if n >= 2:
                 zs.append(product(n))
-            if n in (1, 2):
+            if n == 2:
                 last_tap(n + 1)
             zc, zp = quant(zs[n], CHUNK, "z%d" % n)
 
@@ -190,7 +203,7 @@ def tile_picked_glutap_none_p_kernel(tc, x_words, x_scales, w1, w2, w3, offs, ta
             cols = slice(n * CHUNK, (n + 1) * CHUNK)
             if n + 1 < chunks:
                 for half in range(2):
-                    acc = bank([P, 2, CHUNK], 1 + 2 * n + half)
+                    acc = bank([P, 2, CHUNK], ((6, 7), (0, 5), (1, 2))[n][half])
                     for u in range(2):
                         last_product(acc[:, u, :], 2 * half + u)
                     res = sb([P, 2, CHUNK], F32, "res%d_%d" % (n, half))
@@ -198,7 +211,7 @@ def tile_picked_glutap_none_p_kernel(tc, x_words, x_scales, w1, w2, w3, offs, ta
                     nc.sync.dma_start(out[2 * half * P : (2 * half + 2) * P, cols].rearrange("(u p) c -> p u c", p=P), res[:])
             else:
                 for m in range(PACK):
-                    acc = bank([P, CHUNK], (7 + m) % 8)
+                    acc = bank([P, CHUNK], (3, 6, 7, 0)[m])
                     last_product(acc[:], m)
                     res = sb([P, CHUNK], F32, "res%d_%d" % (n, m))
                     (nc.vector.tensor_copy if m % 2 else nc.scalar.copy)(res[:], acc[:])

@@ -16,6 +16,7 @@ FP8X4 = mybir.dt.float8_e4m3fn_x4
 ADD = mybir.AluOpType.add
 MULT = mybir.AluOpType.mult
 SIGMOID = mybir.ActivationFunctionType.Sigmoid
+COPY = mybir.ActivationFunctionType.Copy
 
 P = 128
 PACK = 4
@@ -41,18 +42,18 @@ def tile_picked_glutap_none_p_kernel(tc, x_words, x_scales, w1, w2, w3, offs, ta
         xs = sb([P, T], U8, "xs")
         warm = sb([P, 16], F32, "warm")
         warm_out = sb([P, 16], F32, "warm_out")
-        raw1 = sb([P, PACK, H], F32, "raw1")
+        raw2 = sb([P, PACK, H], F32, "raw2")
         xg_s = sb([P, S], U8, "xg_s")
 
         nc.gpsimd.memset(xs[:].bitcast(I32), 0)
         nc.gpsimd.memset(xg_s[:].bitcast(I32), 0)
         ident = sb([P, P], F32, "ident")
         make_identity(nc, ident[:])
-        w1v = w1.rearrange("(p j) c -> p j c", j=PACK)
-        nc.sync.dma_start(raw1[:, 0:2, :], w1v[:, 0:2, :])
+        w2v = w2.rearrange("(p j) c -> p j c", j=PACK)
+        nc.sync.dma_start(raw2[:, 0:2, :], w2v[:, 0:2, :])
         nc.sync.dma_start(offs_t[:], offs)
         nc.sync.dma_start(xs[0:P:8, :].bitcast(I32), x_scales[0].bitcast(I32))
-        nc.sync.dma_start(raw1[:, 2:PACK, :], w1v[:, 2:PACK, :])
+        nc.sync.dma_start(raw2[:, 2:PACK, :], w2v[:, 2:PACK, :])
         nc.sync.dma_start(xw[:], x_words[0].rearrange("p n t -> p (n t)").bitcast(I32))
         nc.sync.dma_start(tap_t[:], tap)
         nc.vector.memset(warm[:, 0:8], 0.0)
@@ -61,17 +62,15 @@ def tile_picked_glutap_none_p_kernel(tc, x_words, x_scales, w1, w2, w3, offs, ta
         picked = sb([P, S], U8, "picked")
         xg_w = sb([P, S], U32, "xg_w")
 
-        def round_half(half, pair, copy):
-            dst = g2[pair][:, :, half * HALF : (half + 1) * HALF].rearrange("p t (u i j) -> p t u j i", i=4, j=PACK)
-            src = raw2[half].rearrange("p j (u t i) -> p t u j i", t=PACK, i=4)[:, 2 * pair : 2 * pair + 2]
-            copy(dst, src)
-
-        def quant(g, width, name, codes=None):
-            if codes is None:
-                codes = sb([P, width], U32, name + "_c")[:]
+        def quant(g, width, name, codes_name=None):
+            codes = sb([P, width], U32, codes_name or name + "_c")
             scales = sb([P, width], U8, name + "_s")
-            nc.vector.quantize_mx(out=codes.bitcast(FP8X4), scales=scales[:], in_=g)
+            nc.vector.quantize_mx(out=codes[:].bitcast(FP8X4), scales=scales[:], in_=g)
             return codes, scales
+
+        def quant_tiles(g, t0, t1, name):
+            codes, scales = quant(g[:, t0:t1, :].rearrange("p t c -> p (t c)"), (t1 - t0) * P, "%s_%d" % (name, t0))
+            return [(codes[:, u * P : (u + 1) * P], scales[:, u * P : (u + 1) * P]) for u in range(t1 - t0)]
 
         def project(q, c0, width, b):
             acc = bank([P, width], b)
@@ -79,140 +78,152 @@ def tile_picked_glutap_none_p_kernel(tc, x_words, x_scales, w1, w2, w3, offs, ta
                                 rhs=xg_w[:, c0 : c0 + width].bitcast(FP8X4), rhs_scale=xg_s[:, c0 : c0 + width], start=True, stop=True)
             return acc
 
-        def tap_add(dst, window, own, c0, width):
-            nc.vector.tensor_tensor(dst, window[:].indirect(tap_t[:, c0 // 16 : (c0 + width) // 16]), own, ADD)
+        def looked_up(window, c0, width):
+            return window[:].indirect(tap_t[:, c0 // 16 : (c0 + width) // 16])
 
-        def quant_tiles(g, t0, t1, name, codes=None):
-            codes, scales = quant(g[:, t0:t1, :].rearrange("p t c -> p (t c)"), (t1 - t0) * P, "%s_%d" % (name, t0), codes)
-            return [(codes[:, u * P : (u + 1) * P], scales[:, u * P : (u + 1) * P]) for u in range(t1 - t0)]
-
-        g1 = sb([P, PACK, P * PACK], BF16, "g1")
+        g2 = sb([P, PACK, P * PACK], BF16, "g2")
         nc.vector.tensor_copy(picked[:], xs[:].indirect(offs_t[:]))
         for r in range(4):
             nc.sync.dma_start(xg_s[r:P:32, :].bitcast(I32), picked[8 * r : P : 32, :].bitcast(I32))
-        dst1 = g1[:].rearrange("p t (u i j) -> p t u j i", i=4, j=PACK)
-        src1 = raw1[:].rearrange("p j (u t i) -> p t u j i", t=PACK, i=4)
-        nc.vector.tensor_copy(dst1[:, 0:2], src1[:, 0:2])
+        dst2 = g2[:].rearrange("p t (u i j) -> p t u j i", i=4, j=PACK)
+        src2 = raw2[:].rearrange("p j (u t i) -> p t u j i", t=PACK, i=4)
+        nc.vector.tensor_copy(dst2[:, 0:2], src2[:, 0:2])
         for t in range(2, PACK):
-            nc.scalar.copy(dst1[:, t], src1[:, t])
-        win = [sb([P, 3 * S], F32, "xs"), sb([P, 2 * S], F32, "win1"), sb([P, 2 * S], F32, "win2"), sb([P, 2 * S], F32, "raw1")]
-        win.extend(sb([P, 2 * S], F32, "win%d" % u) for u in range(PACK, 2 * PACK - 1))
-        win.append(sb([P, S], F32, "win7"))
-        for u in (2, 4):
-            nc.gpsimd.memset(win[u][:, S:], 0.0)
-        raw2 = [raw.rearrange("p (j c) -> p j c", j=PACK) for raw in (win[0][:, S:], win[3][:])]
+            nc.scalar.copy(dst2[:, t], src2[:, t])
+
+        ewin = [sb([P, S], F32, "e%d" % t) for t in range(PACK)]
+        early = sb([P, 3 * S - CHUNK], F32, "xs")
+        y1 = sb([P, 3 * S], F32, "raw2")
+        raw1 = [early[:, S - CHUNK :].rearrange("p (j c) -> p j c", j=PACK), y1[:, S:].rearrange("p (j c) -> p j c", j=PACK)]
         for half in range(2):
-            nc.sync.dma_start(raw2[half], w2.rearrange("(p j) c -> p j c", j=PACK)[:, :, half * HALF : (half + 1) * HALF])
-        q1 = quant_tiles(g1, 0, 2, "q1") + quant_tiles(g1, 2, PACK, "q1")
+            nc.sync.dma_start(raw1[half], w1.rearrange("(p j) c -> p j c", j=PACK)[:, :, half * HALF : (half + 1) * HALF])
+        q2 = quant_tiles(g2, 0, 2, "q2") + quant_tiles(g2, 2, PACK, "q2")
         for half in range(2):
             nc.vector.tensor_copy(xg_w[:, half * HALF : (half + 1) * HALF], xw[:].bitcast(U32).indirect(offs_t[:, half * HALF // 16 : (half + 1) * HALF // 16]))
-        g2 = [sb([P, 2, P * PACK], BF16, "g2_%d" % pair) for pair in range(2)]
-        for pair in range(2):
-            round_half(0, pair, nc.vector.tensor_copy)
         raw3 = sb([P, PACK, N], F32, "xw")
         w3v = w3.rearrange("(u t i) n -> t u i n", t=PACK, i=4)
         for t in range(PACK):
             nc.sync.dma_start(raw3[:, t, :], w3v[t])
+        later = sb([P, 2, 2 * S], F32, "later")
+        esum = [raw1[1], later[:, 0, :].rearrange("p (t c) -> p t c", t=PACK)]
+        g1 = sb([P, PACK, P * PACK], BF16, "g1")
 
-        sums = sb([P, PACK * S + CHUNK], F32, "sums")
-        esum = sums[:, 0 : PACK * S].rearrange("p (t c) -> p t c", t=PACK)
+        def round_w1(half, t0, t1, u0, u1):
+            dst = g1[:, t0:t1, half * HALF : (half + 1) * HALF].rearrange("p t (u i j) -> p t u j i", i=4, j=PACK)
+            src = raw1[half].rearrange("p j (u t i) -> p t u j i", t=PACK, i=4)[:, t0:t1]
+            nc.vector.tensor_copy(dst[:, :, u0:u1], src[:, :, u0:u1])
 
-        def leave_bank(q, u, b):
-            acc = project(q, 0, S, b)
-            nc.scalar.copy(win[u][:, 0:S], acc[:])
-            return acc
+        round_w1(0, 0, PACK, 0, 8)
+        round_w1(0, 0, PACK, 8, 16)
+
+        ywin = [y1 if t == 1 else sb([P, S], F32, "y%d" % t) for t in range(PACK)]
+        own = [ap.rearrange("p (h c) -> p h c", h=2) for ap in (sb([P, S], F32, "own0")[:], early[:, 0:S])]
+        own.extend(later[:, :, c0 : c0 + HALF] for c0 in (CHUNK, S + CHUNK))
+        halves = [project(q2[0], half * HALF, HALF, half) for half in range(2)]
+        for dst in (ewin[0][:].rearrange("p (h c) -> p h c", h=2), own[0]):
+            for half in range(2):
+                nc.scalar.copy(dst[:, half, :], halves[half][:])
+        e1 = project(q2[1], 0, S, 2)
+        nc.vector.tensor_copy(early[:, 0:S], e1[:])
+        for t in (2, 3):
+            nc.scalar.copy(ewin[t][:], project(q2[t], 0, S, 1 + t)[:])
+            nc.sync.dma_start(own[t], ewin[t][:].rearrange("p (h c) -> p h c", h=2))
+        nc.scalar.copy(ewin[1][:], e1[:])
+        for pair in range(2):
+            round_w1(1, 2 * pair, 2 * pair + 2, 0, 16)
+        q1 = quant_tiles(g1, 0, 2, "q1") + quant_tiles(g1, 2, PACK, "q1")
+        for t in range(PACK):
+            nc.scalar.copy(ywin[t][:, 0:S], project(q1[t], 0, S, (5 + t) % 8)[:])
+
+        def tap_add(t, half, at=0, width=HALF):
+            c0 = half * HALF + at
+            nc.vector.tensor_tensor(esum[half][:, t, at : at + width], looked_up(ewin[t], c0, width), own[t][:, half, at : at + width], ADD)
+
+        whole = sb([P, S], F32, "whole")
+        fetched = {(1, 0): whole[:, 0:HALF], (1, 1): whole[:, HALF:S]}
+
+        def fetch(half, name):
+            dst = sb([P, PACK - 1, HALF], F32, name)
+            for u, t in enumerate((0, 2, 3)):
+                fetched[t, half] = dst[:, u, :]
+                nc.scalar.activation(dst[:, u, :], looked_up(ywin[t], half * HALF, HALF), COPY)
 
         def turn(dst, src, start, stop):
             nc.tensor.matmul(dst, lhsT=src, rhs=ident[:], start=start, stop=stop, is_transpose=True)
 
-        def fetch(dst, u):
-            nc.vector.tensor_copy(dst, win[u][:].indirect(tap_t[:]))
-
-        def turned_gate(t, fetched, b):
-            acc = bank([P, chunks, P], b)
-            for n in range(chunks):
-                turn(acc[:, n, :], win[t][:, n * CHUNK : (n + 1) * CHUNK], n == 0, False)
-            for n in range(chunks):
-                turn(acc[:, n, :], fetched[:, n * CHUNK : (n + 1) * CHUNK], False, n + 1 == chunks)
-            turned = sb([P, chunks, P], F32, ("q2a_0_s", "q2b_0_s", "turned2", "turned3")[t])
+        def gates(pair, half, b):
+            acc = bank([P, 2, 2, P], b)
+            blocks = [(u, v, half * HALF + v * CHUNK) for u in range(2) for v in range(2)]
+            for u, v, c0 in blocks:
+                turn(acc[:, u, v, :], ywin[2 * pair + u][:, c0 : c0 + CHUNK], (u, v) == (0, 0), False)
+            for u, v, c0 in blocks:
+                turn(acc[:, u, v, :], fetched[2 * pair + u, half][:, v * CHUNK : (v + 1) * CHUNK], False, (u, v) == (1, 1))
+            turned = sb([P, 2, 2, P], F32, "turned%d%d" % (pair, half))
             nc.scalar.activation(turned[:], acc[:], SIGMOID)
+            for u, v, c0 in blocks:
+                nc.tensor.transpose(gate[2 * half + v][:, 2 * pair + u, :], turned[:, u, v, :], ident[:])
             return turned
 
         chunks = S // CHUNK
-        ya = project(q1[0], 0, HALF, 0)
-        yb = project(q1[0], HALF, HALF, 1)
-        nc.scalar.copy(win[0][:, 0:HALF], ya[:])
-        nc.scalar.copy(win[0][:, HALF:S], yb[:])
-        leave_bank(q1[1], 1, 2)
-        fetch(win[1][:, S:], 0)
-        round_half(1, 0, nc.vector.tensor_copy)
-        round_half(1, 1, nc.scalar.copy)
-        leave_bank(q1[2], 2, 3)
-        q2 = quant_tiles(g2[0], 0, 2, "q2a") + quant_tiles(g2[1], 0, 2, "q2b")
-        leave_bank(q1[3], 3, 4)
-        own = {4: win[5][:, S:], 5: win[6][:, S:], 6: sb([P, S], F32, "own6")[:]}
-        own7 = sb([P, S], F32, "own7")
-        accs = []
-        for t in range(PACK):
-            accs.append(leave_bank(q2[t], PACK + t, (5 + t) % 8))
-            if t in (1, 2):
-                nc.sync.dma_start(own[PACK + t], win[PACK + t][:, 0:S])
-            if t == 2:
-                nc.scalar.copy(own[PACK], accs[0][:])
-        nc.sync.dma_start(own7[:], win[7][:])
-        fetched23 = sb([P, 2 * S], F32, "g2_1")
-        fetched = [win[1][:, S:], win[3][:, S:], fetched23[:, 0:S], fetched23[:, S:]]
-        for t in range(1, PACK):
-            fetch(fetched[t], t)
-        turned = [turned_gate(t, fetched[t], (6, 7, 0, 5)[t]) for t in range(PACK)]
-        gate = [bank([P, PACK, CHUNK], (1, 2, 3, 4)[n]) for n in range(chunks)]
-        for t in range(PACK):
-            for n in range(chunks):
-                nc.tensor.transpose(gate[n][:, t, :], turned[t][:, n, :], ident[:])
-        g3 = sb([P, N * PACK], BF16, "q2a_0_s")
-        nc.scalar.copy(g3[:].rearrange("p (c i j) -> p c j i", i=4, j=PACK), raw3[:].rearrange("p j (c i) -> p c j i", i=4))
-        for t in range(PACK - 1):
-            tap_add(esum[:, t, :], win[PACK + t], own[PACK + t], 0, S)
-        tap_add(esum[:, PACK - 1, 0:HALF], win[7], own7[:, 0:HALF], 0, HALF)
-
-        def last_tap(n):
-            tap_add(esum[:, PACK - 1, n * CHUNK : (n + 1) * CHUNK], win[7], own7[:, n * CHUNK : (n + 1) * CHUNK], n * CHUNK, CHUNK)
+        tap_add(0, 0)
+        tap_add(1, 0)
+        nc.vector.tensor_copy(whole[:], looked_up(y1, 0, S))
+        tap_add(2, 0)
+        tap_add(3, 0)
+        fetch(0, "fetched_a")
+        gate = [bank([P, PACK, CHUNK], 1 + n) for n in range(chunks)]
+        t0 = gates(0, 0, 5)
+        ta = gates(1, 0, 6)
+        g3 = sb([P, N * PACK], BF16, "g3")[:]
+        for half in range(2):
+            nc.vector.tensor_copy(g3[:, half * HALF * PACK : (half + 1) * HALF * PACK].rearrange("p (c i j) -> p c j i", i=4, j=PACK),
+                                    raw3[:, :, half * HALF : (half + 1) * HALF].rearrange("p j (c i) -> p c j i", i=4))
+        tap_add(0, 1)
+        tap_add(1, 1)
+        fetch(1, "fetched_a")
+        t2 = gates(0, 1, 7)
+        tb = gates(1, 1, 0)
 
         def product(n):
-            cols = slice(n * CHUNK, (n + 1) * CHUNK)
-            z = sums[:, PACK * S - CHUNK :].bitcast(BF16) if n == 1 else sb([P, CHUNK * PACK], BF16, "z%d" % n)[:]
+            cols = slice(n % 2 * CHUNK, (n % 2 + 1) * CHUNK)
+            z = sb([P, CHUNK * PACK], BF16, "z%d" % n)[:]
             nc.vector.tensor_tensor(z.rearrange("p (c i j) -> p c j i", i=2, j=PACK),
-                                    esum[:, :, cols].rearrange("p j (c i) -> p c j i", i=2),
+                                    esum[n // 2][:, :, cols].rearrange("p j (c i) -> p c j i", i=2),
                                     gate[n][:].rearrange("p j (c i) -> p c j i", i=2), MULT)
             return z
 
-        last_tap(2)
-        zs = [product(0), product(1)]
-        c3, s3 = quant(g3[:], N, "q3")
-        for n in range(chunks):
-            if n >= 2:
-                zs.append(product(n))
-            if n == 2:
-                last_tap(n + 1)
-            zc, zp = quant(zs[n], CHUNK, "z%d" % n)
+        def finish(n, z):
+            zc, zp = quant(z, CHUNK, "z%d" % n, "turned11" if n == 1 else None)
 
             def last_product(dst, m):
-                nc.tensor.matmul_mx(out=dst, lhsT=c3[:, m * P : (m + 1) * P].bitcast(FP8X4), lhsT_scale=s3[:, m * P : (m + 1) * P],
-                                    rhs=zc.bitcast(FP8X4), rhs_scale=zp[:], start=True, stop=True)
+                nc.tensor.matmul_mx(out=dst, lhsT=q3[m][0].bitcast(FP8X4), lhsT_scale=q3[m][1],
+                                    rhs=zc[:].bitcast(FP8X4), rhs_scale=zp[:], start=True, stop=True)
 
             cols = slice(n * CHUNK, (n + 1) * CHUNK)
             if n + 1 < chunks:
                 for half in range(2):
-                    acc = bank([P, 2, CHUNK], ((6, 7), (0, 5), (1, 2))[n][half])
+                    acc = bank([P, 2, CHUNK], ((7, 0), (5, 6), (1, 2))[n][half])
                     for u in range(2):
                         last_product(acc[:, u, :], 2 * half + u)
                     res = sb([P, 2, CHUNK], F32, "res%d_%d" % (n, half))
-                    nc.scalar.copy(res[:], acc[:])
+                    (nc.vector.tensor_copy if (n, half) == (2, 1) else nc.scalar.copy)(res[:], acc[:])
                     nc.sync.dma_start(out[2 * half * P : (2 * half + 2) * P, cols].rearrange("(u p) c -> p u c", p=P), res[:])
             else:
                 for m in range(PACK):
-                    acc = bank([P, CHUNK], (3, 6, 7, 0)[m])
+                    acc = bank([P, CHUNK], (3, 7, 0, 5)[m])
                     last_product(acc[:], m)
                     res = sb([P, CHUNK], F32, "res%d_%d" % (n, m))
                     (nc.vector.tensor_copy if m % 2 else nc.scalar.copy)(res[:], acc[:])
                     nc.sync.dma_start(out[m * P : (m + 1) * P, cols], res[:])
+
+        z0 = product(0)
+        tap_add(2, 1)
+        q3 = quant_tiles(g3.rearrange("p (t c) -> p t c", t=PACK), 0, PACK, "q3")
+        finish(0, z0)
+        z1 = product(1)
+        tap_add(3, 1, 0, CHUNK)
+        finish(1, z1)
+        z2 = product(2)
+        tap_add(3, 1, CHUNK, CHUNK)
+        finish(2, z2)
+        finish(3, product(3))

@@ -22,6 +22,7 @@ P = 128
 PACK = 4
 HALF = S // 2
 CHUNK = 128
+LAST = S - CHUNK
 
 
 def tile_picked_glutap_none_p_kernel(tc, x_words, x_scales, w1, w2, w3, offs, tap, out):
@@ -91,10 +92,9 @@ def tile_picked_glutap_none_p_kernel(tc, x_words, x_scales, w1, w2, w3, offs, ta
         for t in range(2, PACK):
             nc.scalar.copy(dst2[:, t], src2[:, t])
 
-        ewin = [sb([P, S], F32, "e%d" % t) for t in range(PACK)]
-        early = sb([P, 3 * S - CHUNK], F32, "xs")
-        y1 = sb([P, 3 * S], F32, "raw2")
-        raw1 = [early[:, S - CHUNK :].rearrange("p (j c) -> p j c", j=PACK), y1[:, S:].rearrange("p (j c) -> p j c", j=PACK)]
+        ewin = [sb([P, 4 * S - CHUNK], F32, "xs"), sb([P, 2 * S], F32, "e1"), sb([P, S], F32, "e2"), sb([P, S], F32, "e3")]
+        esum = sb([P, PACK, S], F32, "raw2")
+        raw1 = [ewin[0][:, 2 * S - CHUNK :].rearrange("p (j c) -> p j c", j=PACK), esum[:, :, 192 : 192 + HALF]]
         for half in range(2):
             nc.sync.dma_start(raw1[half], w1.rearrange("(p j) c -> p j c", j=PACK)[:, :, half * HALF : (half + 1) * HALF])
         q2 = quant_tiles(g2, 0, 2, "q2") + quant_tiles(g2, 2, PACK, "q2")
@@ -104,8 +104,6 @@ def tile_picked_glutap_none_p_kernel(tc, x_words, x_scales, w1, w2, w3, offs, ta
         w3v = w3.rearrange("(u t i) n -> t u i n", t=PACK, i=4)
         for t in range(PACK):
             nc.sync.dma_start(raw3[:, t, :], w3v[t])
-        later = sb([P, 2, 2 * S], F32, "later")
-        esum = [raw1[1], later[:, 0, :].rearrange("p (t c) -> p t c", t=PACK)]
         g1 = sb([P, PACK, P * PACK], BF16, "g1")
 
         def round_w1(half, t0, t1, u0, u1):
@@ -116,93 +114,98 @@ def tile_picked_glutap_none_p_kernel(tc, x_words, x_scales, w1, w2, w3, offs, ta
         round_w1(0, 0, PACK, 0, 8)
         round_w1(0, 0, PACK, 8, 16)
 
-        ywin = [y1 if t == 1 else sb([P, S], F32, "y%d" % t) for t in range(PACK)]
-        own = [ap.rearrange("p (h c) -> p h c", h=2) for ap in (sb([P, S], F32, "own0")[:], early[:, 0:S])]
-        own.extend(later[:, :, c0 : c0 + HALF] for c0 in (CHUNK, S + CHUNK))
+        ywin = [sb([P, S], F32, "y%d" % t) for t in range(PACK)]
+        own = [ewin[1][:, S:], ewin[0][:, S : 2 * S], sb([P, S], F32, "own2")[:], sb([P, S], F32, "own3")[:]]
         halves = [project(q2[0], half * HALF, HALF, half) for half in range(2)]
-        for dst in (ewin[0][:].rearrange("p (h c) -> p h c", h=2), own[0]):
+        for dst in (ewin[0][:, 0:S], own[0]):
             for half in range(2):
-                nc.scalar.copy(dst[:, half, :], halves[half][:])
+                nc.scalar.copy(dst[:, half * HALF : (half + 1) * HALF], halves[half][:])
         e1 = project(q2[1], 0, S, 2)
-        nc.vector.tensor_copy(early[:, 0:S], e1[:])
+        nc.vector.tensor_copy(own[1], e1[:])
         for t in (2, 3):
             nc.scalar.copy(ewin[t][:], project(q2[t], 0, S, 1 + t)[:])
-            nc.sync.dma_start(own[t], ewin[t][:].rearrange("p (h c) -> p h c", h=2))
-        nc.scalar.copy(ewin[1][:], e1[:])
+            nc.sync.dma_start(own[t], ewin[t][:])
+        nc.scalar.copy(ewin[1][:, 0:S], e1[:])
         for pair in range(2):
             round_w1(1, 2 * pair, 2 * pair + 2, 0, 16)
         q1 = quant_tiles(g1, 0, 2, "q1") + quant_tiles(g1, 2, PACK, "q1")
+        own_y = sb([P, PACK, CHUNK], F32, "own_y")
         for t in range(PACK):
-            nc.scalar.copy(ywin[t][:, 0:S], project(q1[t], 0, S, (5 + t) % 8)[:])
+            nc.scalar.copy(ywin[t][:], project(q1[t], 0, S, (5 + t) % 8)[:])
+            nc.sync.dma_start(own_y[:, t, :], ywin[t][:, LAST:])
 
-        def tap_add(t, half, at=0, width=HALF):
-            c0 = half * HALF + at
-            nc.vector.tensor_tensor(esum[half][:, t, at : at + width], looked_up(ewin[t], c0, width), own[t][:, half, at : at + width], ADD)
+        def tap_add(t, c0, width):
+            nc.vector.tensor_tensor(esum[:, t, c0 : c0 + width], looked_up(ewin[t], c0, width), own[t][:, c0 : c0 + width], ADD)
 
-        whole = sb([P, S], F32, "whole")
-        fetched = {(1, 0): whole[:, 0:HALF], (1, 1): whole[:, HALF:S]}
-
-        def fetch(half, name):
-            dst = sb([P, PACK - 1, HALF], F32, name)
-            for u, t in enumerate((0, 2, 3)):
-                fetched[t, half] = dst[:, u, :]
-                nc.scalar.activation(dst[:, u, :], looked_up(ywin[t], half * HALF, HALF), COPY)
+        def fetch(c0, width):
+            dst = sb([P, PACK, width], F32, "fetched")
+            for t in range(PACK):
+                nc.scalar.activation(dst[:, t, :], looked_up(ywin[t], c0, width), COPY)
+            return dst
 
         def turn(dst, src, start, stop):
             nc.tensor.matmul(dst, lhsT=src, rhs=ident[:], start=start, stop=stop, is_transpose=True)
 
-        def gates(pair, half, b):
-            acc = bank([P, 2, 2, P], b)
-            blocks = [(u, v, half * HALF + v * CHUNK) for u in range(2) for v in range(2)]
-            for u, v, c0 in blocks:
-                turn(acc[:, u, v, :], ywin[2 * pair + u][:, c0 : c0 + CHUNK], (u, v) == (0, 0), False)
-            for u, v, c0 in blocks:
-                turn(acc[:, u, v, :], fetched[2 * pair + u, half][:, v * CHUNK : (v + 1) * CHUNK], False, (u, v) == (1, 1))
-            turned = sb([P, 2, 2, P], F32, "turned%d%d" % (pair, half))
+        def gates(blocks, fetched, c0, b, name):
+            acc = bank([P, len(blocks), P], b)
+            for u, (t, n) in enumerate(blocks):
+                turn(acc[:, u, :], ywin[t][:, n * CHUNK : (n + 1) * CHUNK], u == 0, False)
+            for u, (t, n) in enumerate(blocks):
+                turn(acc[:, u, :], fetched[:, t, n * CHUNK - c0 : (n + 1) * CHUNK - c0], False, u + 1 == len(blocks))
+            turned = sb([P, len(blocks), P], F32, name)
             nc.scalar.activation(turned[:], acc[:], SIGMOID)
-            for u, v, c0 in blocks:
-                nc.tensor.transpose(gate[2 * half + v][:, 2 * pair + u, :], turned[:, u, v, :], ident[:])
+            for u, (t, n) in enumerate(blocks):
+                nc.tensor.transpose(gate[n][:, t, :], turned[:, u, :], ident[:])
             return turned
 
         chunks = S // CHUNK
-        tap_add(0, 0)
-        tap_add(1, 0)
-        nc.vector.tensor_copy(whole[:], looked_up(y1, 0, S))
-        tap_add(2, 0)
-        tap_add(3, 0)
-        fetch(0, "fetched_a")
-        gate = [bank([P, PACK, CHUNK], 1 + n) for n in range(chunks)]
-        t0 = gates(0, 0, 5)
-        ta = gates(1, 0, 6)
+        tap_add(0, 0, S)
+        tap_add(1, 0, S)
+        tap_add(2, 0, HALF)
+        tap_add(3, 0, HALF)
+        gate = [bank([P, PACK, CHUNK], 1 + n) for n in range(chunks - 1)] + [sb([P, PACK, CHUNK], F32, "gate3")]
+        first = fetch(0, HALF)
+        for pair in range(2):
+            ta = gates([(t, n) for t in (2 * pair, 2 * pair + 1) for n in range(2)], first, 0, 5 + pair, "turned%d" % pair)
         g3 = sb([P, N * PACK], BF16, "g3")[:]
         for half in range(2):
             nc.vector.tensor_copy(g3[:, half * HALF * PACK : (half + 1) * HALF * PACK].rearrange("p (c i j) -> p c j i", i=4, j=PACK),
-                                    raw3[:, :, half * HALF : (half + 1) * HALF].rearrange("p j (c i) -> p c j i", i=4))
-        tap_add(0, 1)
-        tap_add(1, 1)
-        fetch(1, "fetched_a")
-        t2 = gates(0, 1, 7)
-        tb = gates(1, 1, 0)
+                                  raw3[:, :, half * HALF : (half + 1) * HALF].rearrange("p j (c i) -> p c j i", i=4))
+        tap_add(2, HALF, HALF)
+        q3 = quant_tiles(g3.rearrange("p (t c) -> p t c", t=PACK), 0, PACK, "q3")
+        tap_add(3, HALF, HALF)
+        tb = gates([(t, 2) for t in range(PACK)], fetch(HALF, CHUNK), HALF, 7, "turned2")
+        ysum = sb([P, PACK, CHUNK], F32, "ysum")
+
+        def tap_y(t):
+            nc.vector.tensor_tensor(ysum[:, t, :], looked_up(ywin[t], LAST, CHUNK), own_y[:, t, :], ADD)
 
         def product(n):
-            cols = slice(n % 2 * CHUNK, (n % 2 + 1) * CHUNK)
+            cols = slice(n * CHUNK, (n + 1) * CHUNK)
             z = sb([P, CHUNK * PACK], BF16, "z%d" % n)[:]
             nc.vector.tensor_tensor(z.rearrange("p (c i j) -> p c j i", i=2, j=PACK),
-                                    esum[n // 2][:, :, cols].rearrange("p j (c i) -> p c j i", i=2),
+                                    esum[:, :, cols].rearrange("p j (c i) -> p c j i", i=2),
                                     gate[n][:].rearrange("p j (c i) -> p c j i", i=2), MULT)
             return z
 
         def finish(n, z):
-            zc, zp = quant(z, CHUNK, "z%d" % n, "turned11" if n == 1 else None)
+            zc, zp = quant(z, CHUNK, "z%d" % n, "turned2" if n == 1 else None)
 
             def last_product(dst, m):
                 nc.tensor.matmul_mx(out=dst, lhsT=q3[m][0].bitcast(FP8X4), lhsT_scale=q3[m][1],
                                     rhs=zc[:].bitcast(FP8X4), rhs_scale=zp[:], start=True, stop=True)
 
             cols = slice(n * CHUNK, (n + 1) * CHUNK)
-            if n + 1 < chunks:
+            if n == 0:
+                acc = bank([P, PACK, CHUNK], 7)
+                for m in range(PACK):
+                    last_product(acc[:, m, :], m)
+                res = sb([P, PACK, CHUNK], F32, "res0")
+                nc.scalar.copy(res[:], acc[:])
+                nc.sync.dma_start(out[:, cols].rearrange("(u p) c -> p u c", p=P), res[:])
+            elif n + 1 < chunks:
                 for half in range(2):
-                    acc = bank([P, 2, CHUNK], ((7, 0), (5, 6), (1, 2))[n][half])
+                    acc = bank([P, 2, CHUNK], ((5, 6), (1, 2))[n - 1][half])
                     for u in range(2):
                         last_product(acc[:, u, :], 2 * half + u)
                     res = sb([P, 2, CHUNK], F32, "res%d_%d" % (n, half))
@@ -210,20 +213,22 @@ def tile_picked_glutap_none_p_kernel(tc, x_words, x_scales, w1, w2, w3, offs, ta
                     nc.sync.dma_start(out[2 * half * P : (2 * half + 2) * P, cols].rearrange("(u p) c -> p u c", p=P), res[:])
             else:
                 for m in range(PACK):
-                    acc = bank([P, CHUNK], (3, 7, 0, 5)[m])
+                    acc = bank([P, CHUNK], (3, 0, 4, 7)[m])
                     last_product(acc[:], m)
                     res = sb([P, CHUNK], F32, "res%d_%d" % (n, m))
                     (nc.vector.tensor_copy if m % 2 else nc.scalar.copy)(res[:], acc[:])
                     nc.sync.dma_start(out[m * P : (m + 1) * P, cols], res[:])
 
+        tap_y(0)
+        tap_y(1)
         z0 = product(0)
-        tap_add(2, 1)
-        q3 = quant_tiles(g3.rearrange("p (t c) -> p t c", t=PACK), 0, PACK, "q3")
+        tap_y(2)
         finish(0, z0)
         z1 = product(1)
-        tap_add(3, 1, 0, CHUNK)
+        tap_y(3)
+        nc.scalar.activation(gate[3][:], ysum[:], SIGMOID)
         finish(1, z1)
         z2 = product(2)
-        tap_add(3, 1, CHUNK, CHUNK)
+        z3 = product(3)
         finish(2, z2)
-        finish(3, product(3))
+        finish(3, z3)

@@ -189,23 +189,16 @@ def tile_picked_glutap_none_p_kernel(tc, x_words, x_scales, w1, w2, w3, offs, ta
             return z
 
         def finish(n, z):
-            zc, zp = quant(z, CHUNK, "z%d" % n, "turned2" if n == 1 else None)
+            zc, zp = quant(z, CHUNK, "z%d" % n, "fetched" if n == 1 else None)
 
             def last_product(dst, m):
                 nc.tensor.matmul_mx(out=dst, lhsT=q3[m][0].bitcast(FP8X4), lhsT_scale=q3[m][1],
                                     rhs=zc[:].bitcast(FP8X4), rhs_scale=zp[:], start=True, stop=True)
 
             cols = slice(n * CHUNK, (n + 1) * CHUNK)
-            if n == 0:
-                acc = bank([P, PACK, CHUNK], 7)
-                for m in range(PACK):
-                    last_product(acc[:, m, :], m)
-                res = sb([P, PACK, CHUNK], F32, "res0")
-                nc.scalar.copy(res[:], acc[:])
-                nc.sync.dma_start(out[:, cols].rearrange("(u p) c -> p u c", p=P), res[:])
-            elif n + 1 < chunks:
+            if n + 1 < chunks:
                 for half in range(2):
-                    acc = bank([P, 2, CHUNK], ((5, 6), (1, 2))[n - 1][half])
+                    acc = bank([P, 2, CHUNK], ((5, 6), (0, 4), (1, 2))[n][half])
                     for u in range(2):
                         last_product(acc[:, u, :], 2 * half + u)
                     res = sb([P, 2, CHUNK], F32, "res%d_%d" % (n, half))
@@ -213,7 +206,7 @@ def tile_picked_glutap_none_p_kernel(tc, x_words, x_scales, w1, w2, w3, offs, ta
                     nc.sync.dma_start(out[2 * half * P : (2 * half + 2) * P, cols].rearrange("(u p) c -> p u c", p=P), res[:])
             else:
                 for m in range(PACK):
-                    acc = bank([P, CHUNK], (3, 0, 4, 7)[m])
+                    acc = bank([P, CHUNK], (3, 5, 6, 7)[m])
                     last_product(acc[:], m)
                     res = sb([P, CHUNK], F32, "res%d_%d" % (n, m))
                     (nc.vector.tensor_copy if m % 2 else nc.scalar.copy)(res[:], acc[:])

@@ -92,15 +92,18 @@ def tile_picked_glutap_none_p_kernel(tc, x_words, x_scales, w1, w2, w3, offs, ta
         for t in range(2, PACK):
             nc.scalar.copy(dst2[:, t], src2[:, t])
 
-        ewin = [sb([P, 4 * S - CHUNK], F32, "xs"), sb([P, 2 * S], F32, "e1"), sb([P, S], F32, "e2"), sb([P, S], F32, "e3")]
-        esum = sb([P, PACK, S], F32, "raw2")
-        raw1 = [ewin[0][:, 2 * S - CHUNK :].rearrange("p (j c) -> p j c", j=PACK), esum[:, :, 192 : 192 + HALF]]
+        ewin = [sb([P, 4 * S - CHUNK], F32, "xs"), sb([P, 2 * S], F32, "e1"), sb([P, 2 * S], F32, "e2"), sb([P, 2 * S], F32, "e3")]
+        for t in (2, 3):
+            nc.gpsimd.memset(ewin[t][:, S:], 0.0)
+        sums = sb([P, PACK * S - CHUNK // 2 + PACK * N], F32, "raw2")
+        esum = sums[:, 0 : PACK * S].rearrange("p (t c) -> p t c", t=PACK)
+        raw3 = sums[:, PACK * S - CHUNK // 2 :].rearrange("p (j c) -> p j c", j=PACK)
+        raw1 = [ewin[0][:, 2 * S - CHUNK :].rearrange("p (j c) -> p j c", j=PACK), esum[:, :, 0:HALF]]
         for half in range(2):
             nc.sync.dma_start(raw1[half], w1.rearrange("(p j) c -> p j c", j=PACK)[:, :, half * HALF : (half + 1) * HALF])
         q2 = quant_tiles(g2, 0, 2, "q2") + quant_tiles(g2, 2, PACK, "q2")
         for half in range(2):
             nc.vector.tensor_copy(xg_w[:, half * HALF : (half + 1) * HALF], xw[:].bitcast(U32).indirect(offs_t[:, half * HALF // 16 : (half + 1) * HALF // 16]))
-        raw3 = sb([P, PACK, N], F32, "xw")
         w3v = w3.rearrange("(u t i) n -> t u i n", t=PACK, i=4)
         for t in range(PACK):
             nc.sync.dma_start(raw3[:, t, :], w3v[t])
@@ -123,8 +126,8 @@ def tile_picked_glutap_none_p_kernel(tc, x_words, x_scales, w1, w2, w3, offs, ta
         e1 = project(q2[1], 0, S, 2)
         nc.vector.tensor_copy(own[1], e1[:])
         for t in (2, 3):
-            nc.scalar.copy(ewin[t][:], project(q2[t], 0, S, 1 + t)[:])
-            nc.sync.dma_start(own[t], ewin[t][:])
+            nc.scalar.copy(ewin[t][:, 0:S], project(q2[t], 0, S, 1 + t)[:])
+            nc.sync.dma_start(own[t], ewin[t][:, 0:S])
         nc.scalar.copy(ewin[1][:, 0:S], e1[:])
         for pair in range(2):
             round_w1(1, 2 * pair, 2 * pair + 2, 0, 16)
@@ -161,20 +164,23 @@ def tile_picked_glutap_none_p_kernel(tc, x_words, x_scales, w1, w2, w3, offs, ta
         chunks = S // CHUNK
         tap_add(0, 0, S)
         tap_add(1, 0, S)
-        tap_add(2, 0, HALF)
-        tap_add(3, 0, HALF)
+        tap_add(2, 0, S)
         gate = [bank([P, PACK, CHUNK], 1 + n) for n in range(chunks - 1)] + [sb([P, PACK, CHUNK], F32, "gate3")]
         first = fetch(0, HALF)
         for pair in range(2):
             ta = gates([(t, n) for t in (2 * pair, 2 * pair + 1) for n in range(2)], first, 0, 5 + pair, "turned%d" % pair)
-        g3 = sb([P, N * PACK], BF16, "g3")[:]
-        for half in range(2):
-            nc.vector.tensor_copy(g3[:, half * HALF * PACK : (half + 1) * HALF * PACK].rearrange("p (c i j) -> p c j i", i=4, j=PACK),
-                                  raw3[:, :, half * HALF : (half + 1) * HALF].rearrange("p j (c i) -> p c j i", i=4))
-        tap_add(2, HALF, HALF)
-        q3 = quant_tiles(g3.rearrange("p (t c) -> p t c", t=PACK), 0, PACK, "q3")
-        tap_add(3, HALF, HALF)
-        tb = gates([(t, 2) for t in range(PACK)], fetch(HALF, CHUNK), HALF, 7, "turned2")
+        g3 = sb([P, PACK, P * PACK], BF16, "g3")
+
+        def round_w3(m0, m1):
+            nc.vector.tensor_copy(g3[:, m0:m1].rearrange("p m (c i j) -> p (m c) j i", i=4, j=PACK),
+                                  raw3[:, :, m0 * P : m1 * P].rearrange("p j (c i) -> p c j i", i=4))
+
+        round_w3(0, 1)
+        round_w3(1, PACK)
+        tap_add(3, 0, S)
+        q3 = quant_tiles(g3, 0, PACK, "q3")
+        third = fetch(HALF, CHUNK)
+        tb = gates([(t, 2) for t in range(PACK)], third, HALF, 7, "turned2")
         ysum = sb([P, PACK, CHUNK], F32, "ysum")
 
         def tap_y(t):
@@ -188,40 +194,34 @@ def tile_picked_glutap_none_p_kernel(tc, x_words, x_scales, w1, w2, w3, offs, ta
                                     gate[n][:].rearrange("p j (c i) -> p c j i", i=2), MULT)
             return z
 
-        def finish(n, z):
-            zc, zp = quant(z, CHUNK, "z%d" % n, "fetched" if n == 1 else None)
+        def quant_z(n, z):
+            return quant(z, CHUNK, "z%d" % n)
 
-            def last_product(dst, m):
-                nc.tensor.matmul_mx(out=dst, lhsT=q3[m][0].bitcast(FP8X4), lhsT_scale=q3[m][1],
-                                    rhs=zc[:].bitcast(FP8X4), rhs_scale=zp[:], start=True, stop=True)
+        def leave(n, qz, m0, count, b, copy):
+            acc = bank([P, count, CHUNK], b)
+            for u in range(count):
+                nc.tensor.matmul_mx(out=acc[:, u, :], lhsT=q3[m0 + u][0].bitcast(FP8X4), lhsT_scale=q3[m0 + u][1],
+                                    rhs=qz[0][:].bitcast(FP8X4), rhs_scale=qz[1][:], start=True, stop=True)
+            res = sb([P, count, CHUNK], F32, "res%d_%d" % (n, m0))
+            copy(res[:], acc[:])
+            nc.sync.dma_start(out[m0 * P : (m0 + count) * P, n * CHUNK : (n + 1) * CHUNK].rearrange("(u p) c -> p u c", p=P), res[:])
 
-            cols = slice(n * CHUNK, (n + 1) * CHUNK)
-            if n + 1 < chunks:
-                for half in range(2):
-                    acc = bank([P, 2, CHUNK], ((5, 6), (0, 4), (1, 2))[n][half])
-                    for u in range(2):
-                        last_product(acc[:, u, :], 2 * half + u)
-                    res = sb([P, 2, CHUNK], F32, "res%d_%d" % (n, half))
-                    (nc.vector.tensor_copy if (n, half) == (2, 1) else nc.scalar.copy)(res[:], acc[:])
-                    nc.sync.dma_start(out[2 * half * P : (2 * half + 2) * P, cols].rearrange("(u p) c -> p u c", p=P), res[:])
-            else:
-                for m in range(PACK):
-                    acc = bank([P, CHUNK], (3, 5, 6, 7)[m])
-                    last_product(acc[:], m)
-                    res = sb([P, CHUNK], F32, "res%d_%d" % (n, m))
-                    (nc.vector.tensor_copy if m % 2 else nc.scalar.copy)(res[:], acc[:])
-                    nc.sync.dma_start(out[m * P : (m + 1) * P, cols], res[:])
-
-        tap_y(0)
-        tap_y(1)
-        z0 = product(0)
-        tap_y(2)
-        finish(0, z0)
-        z1 = product(1)
-        tap_y(3)
+        for t in range(PACK):
+            tap_y(t)
         nc.scalar.activation(gate[3][:], ysum[:], SIGMOID)
-        finish(1, z1)
-        z2 = product(2)
+        z0 = product(0)
+        z1 = product(1)
+        qz0 = quant_z(0, z0)
+        leave(0, qz0, 0, 2, 7, nc.scalar.copy)
+        leave(0, qz0, 2, 2, 5, nc.scalar.copy)
         z3 = product(3)
-        finish(2, z2)
-        finish(3, z3)
+        qz1 = quant_z(1, z1)
+        leave(1, qz1, 0, 2, 0, nc.scalar.copy)
+        leave(1, qz1, 2, 2, 4, nc.scalar.copy)
+        z2 = product(2)
+        qz3 = quant_z(3, z3)
+        leave(3, qz3, 0, 2, 1, nc.scalar.copy)
+        leave(3, qz3, 2, 2, 2, nc.vector.tensor_copy)
+        qz2 = quant_z(2, z2)
+        for m in range(PACK):
+            leave(2, qz2, m, 1, (3, 6, 5, 7)[m], nc.vector.tensor_copy if m % 2 else nc.scalar.copy)

@@ -21,8 +21,10 @@ COPY = mybir.ActivationFunctionType.Copy
 P = 128
 PACK = 4
 HALF = S // 2
-CHUNK = 128
-LAST = S - CHUNK
+PIECE = 128
+LAST = S - PIECE
+GROUP = 16
+RUN = 4
 
 
 def tile_picked_glutap_none_p_kernel(tc, x_words, x_scales, w1, w2, w3, offs, tap, out):
@@ -37,8 +39,8 @@ def tile_picked_glutap_none_p_kernel(tc, x_words, x_scales, w1, w2, w3, offs, ta
         def bank(shape, b):
             return psum.tile(shape, F32, name="bank%d" % b)
 
-        offs_t = keep.tile([P, S // 16], U16, name="offs_t")
-        tap_t = keep.tile([P, S // 16], U16, name="tap_t")
+        offs_t = keep.tile([P, S // GROUP], U16, name="offs_t")
+        tap_t = keep.tile([P, S // GROUP], U16, name="tap_t")
         xw = sb([P, T], I32, "xw")
         xs = sb([P, T], U8, "xs")
         warm = sb([P, 16], F32, "warm")
@@ -50,6 +52,7 @@ def tile_picked_glutap_none_p_kernel(tc, x_words, x_scales, w1, w2, w3, offs, ta
         nc.gpsimd.memset(xg_s[:].bitcast(I32), 0)
         ident = sb([P, P], F32, "ident")
         make_identity(nc, ident[:])
+
         w2v = w2.rearrange("(p j) c -> p j c", j=PACK)
         nc.sync.dma_start(raw2[:, 0:2, :], w2v[:, 0:2, :])
         nc.sync.dma_start(offs_t[:], offs)
@@ -57,20 +60,21 @@ def tile_picked_glutap_none_p_kernel(tc, x_words, x_scales, w1, w2, w3, offs, ta
         nc.sync.dma_start(raw2[:, 2:PACK, :], w2v[:, 2:PACK, :])
         nc.sync.dma_start(xw[:], x_words[0].rearrange("p n t -> p (n t)").bitcast(I32))
         nc.sync.dma_start(tap_t[:], tap)
+
         nc.vector.memset(warm[:, 0:8], 0.0)
         nc.scalar.activation(warm_out[:, 0:8], warm[:, 0:8], SIGMOID)
 
         picked = sb([P, S], U8, "picked")
         xg_w = sb([P, S], U32, "xg_w")
 
-        def quant(g, width, name, codes_name=None):
-            codes = sb([P, width], U32, codes_name or name + "_c")
+        def quant(rounded, width, name):
+            codes = sb([P, width], U32, name + "_c")
             scales = sb([P, width], U8, name + "_s")
-            nc.vector.quantize_mx(out=codes[:].bitcast(FP8X4), scales=scales[:], in_=g)
+            nc.vector.quantize_mx(out=codes[:].bitcast(FP8X4), scales=scales[:], in_=rounded)
             return codes, scales
 
-        def quant_tiles(g, t0, t1, name):
-            codes, scales = quant(g[:, t0:t1, :].rearrange("p t c -> p (t c)"), (t1 - t0) * P, "%s_%d" % (name, t0))
+        def quant_tiles(rounded, t0, t1, name):
+            codes, scales = quant(rounded[:, t0:t1, :].rearrange("p t c -> p (t c)"), (t1 - t0) * P, "%s_%d" % (name, t0))
             return [(codes[:, u * P : (u + 1) * P], scales[:, u * P : (u + 1) * P]) for u in range(t1 - t0)]
 
         def project(q, c0, width, b):
@@ -80,67 +84,74 @@ def tile_picked_glutap_none_p_kernel(tc, x_words, x_scales, w1, w2, w3, offs, ta
             return acc
 
         def looked_up(window, c0, width):
-            return window[:].indirect(tap_t[:, c0 // 16 : (c0 + width) // 16])
+            return window[:].indirect(tap_t[:, c0 // GROUP : (c0 + width) // GROUP])
 
         g2 = sb([P, PACK, P * PACK], BF16, "g2")
         nc.vector.tensor_copy(picked[:], xs[:].indirect(offs_t[:]))
         for r in range(4):
             nc.sync.dma_start(xg_s[r:P:32, :].bitcast(I32), picked[8 * r : P : 32, :].bitcast(I32))
-        dst2 = g2[:].rearrange("p t (u i j) -> p t u j i", i=4, j=PACK)
-        src2 = raw2[:].rearrange("p j (u t i) -> p t u j i", t=PACK, i=4)
+
+        dst2 = g2[:].rearrange("p t (u i j) -> p t u j i", i=RUN, j=PACK)
+        src2 = raw2[:].rearrange("p j (u t i) -> p t u j i", t=PACK, i=RUN)
         nc.vector.tensor_copy(dst2[:, 0:2], src2[:, 0:2])
         for t in range(2, PACK):
             nc.scalar.copy(dst2[:, t], src2[:, t])
 
-        ewin = [sb([P, 4 * S - CHUNK], F32, "xs"), sb([P, 2 * S], F32, "e1"), sb([P, 2 * S], F32, "e2"), sb([P, 2 * S], F32, "e3")]
+        ewin = [sb([P, 4 * S - PIECE], F32, "xs"), sb([P, 2 * S], F32, "e1"), sb([P, 2 * S], F32, "e2"), sb([P, 2 * S], F32, "e3")]
         for t in (2, 3):
             nc.gpsimd.memset(ewin[t][:, S:], 0.0)
-        sums = sb([P, PACK * S - CHUNK // 2 + PACK * N], F32, "raw2")
+        sums = sb([P, PACK * S - PIECE // 2 + PACK * N], F32, "raw2")
         esum = sums[:, 0 : PACK * S].rearrange("p (t c) -> p t c", t=PACK)
-        raw3 = sums[:, PACK * S - CHUNK // 2 :].rearrange("p (j c) -> p j c", j=PACK)
-        raw1 = [ewin[0][:, 2 * S - CHUNK :].rearrange("p (j c) -> p j c", j=PACK), esum[:, :, 0:HALF]]
+        raw3 = sums[:, PACK * S - PIECE // 2 :].rearrange("p (j c) -> p j c", j=PACK)
+        raw1 = [ewin[0][:, 2 * S - PIECE :].rearrange("p (j c) -> p j c", j=PACK), esum[:, :, 0:HALF]]
         for half in range(2):
             nc.sync.dma_start(raw1[half], w1.rearrange("(p j) c -> p j c", j=PACK)[:, :, half * HALF : (half + 1) * HALF])
         q2 = quant_tiles(g2, 0, 2, "q2") + quant_tiles(g2, 2, PACK, "q2")
+
         for half in range(2):
-            nc.vector.tensor_copy(xg_w[:, half * HALF : (half + 1) * HALF], xw[:].bitcast(U32).indirect(offs_t[:, half * HALF // 16 : (half + 1) * HALF // 16]))
-        w3v = w3.rearrange("(u t i) n -> t u i n", t=PACK, i=4)
+            nc.vector.tensor_copy(xg_w[:, half * HALF : (half + 1) * HALF],
+                                  xw[:].bitcast(U32).indirect(offs_t[:, half * HALF // GROUP : (half + 1) * HALF // GROUP]))
+
+        w3v = w3.rearrange("(u t i) n -> t u i n", t=PACK, i=RUN)
         for t in range(PACK):
             nc.sync.dma_start(raw3[:, t, :], w3v[t])
+
         g1 = sb([P, PACK, P * PACK], BF16, "g1")
 
         def round_w1(half, t0, t1, u0, u1):
-            dst = g1[:, t0:t1, half * HALF : (half + 1) * HALF].rearrange("p t (u i j) -> p t u j i", i=4, j=PACK)
-            src = raw1[half].rearrange("p j (u t i) -> p t u j i", t=PACK, i=4)[:, t0:t1]
+            dst = g1[:, t0:t1, half * HALF : (half + 1) * HALF].rearrange("p t (u i j) -> p t u j i", i=RUN, j=PACK)
+            src = raw1[half].rearrange("p j (u t i) -> p t u j i", t=PACK, i=RUN)[:, t0:t1]
             nc.vector.tensor_copy(dst[:, :, u0:u1], src[:, :, u0:u1])
 
         round_w1(0, 0, PACK, 0, 8)
         round_w1(0, 0, PACK, 8, 16)
 
         ywin = [sb([P, S], F32, "y%d" % t) for t in range(PACK)]
-        own = [ewin[1][:, S:], ewin[0][:, S : 2 * S], sb([P, S], F32, "own2")[:], sb([P, S], F32, "own3")[:]]
-        halves = [project(q2[0], half * HALF, HALF, half) for half in range(2)]
-        for dst in (ewin[0][:, 0:S], own[0]):
+        plain_e = [ewin[1][:, S:], ewin[0][:, S : 2 * S], sb([P, S], F32, "plain_e2")[:], sb([P, S], F32, "plain_e3")[:]]
+        e0 = [project(q2[0], half * HALF, HALF, half) for half in range(2)]
+        for dst in (ewin[0][:, 0:S], plain_e[0]):
             for half in range(2):
-                nc.scalar.copy(dst[:, half * HALF : (half + 1) * HALF], halves[half][:])
+                nc.scalar.copy(dst[:, half * HALF : (half + 1) * HALF], e0[half][:])
         e1 = project(q2[1], 0, S, 2)
-        nc.vector.tensor_copy(own[1], e1[:])
+        nc.vector.tensor_copy(plain_e[1], e1[:])
         for t in (2, 3):
             nc.scalar.copy(ewin[t][:, 0:S], project(q2[t], 0, S, 1 + t)[:])
-            nc.sync.dma_start(own[t], ewin[t][:, 0:S])
+            nc.sync.dma_start(plain_e[t], ewin[t][:, 0:S])
         nc.scalar.copy(ewin[1][:, 0:S], e1[:])
+
         for pair in range(2):
             round_w1(1, 2 * pair, 2 * pair + 2, 0, 16)
         q1 = quant_tiles(g1, 0, 2, "q1") + quant_tiles(g1, 2, PACK, "q1")
-        own_y = sb([P, PACK, CHUNK], F32, "own_y")
+
+        plain_y = sb([P, PACK, PIECE], F32, "plain_y")
         for t in range(PACK):
             nc.scalar.copy(ywin[t][:], project(q1[t], 0, S, (5 + t) % 8)[:])
-            nc.sync.dma_start(own_y[:, t, :], ywin[t][:, LAST:])
+            nc.sync.dma_start(plain_y[:, t, :], ywin[t][:, LAST:])
 
-        def tap_add(t, c0, width):
-            nc.vector.tensor_tensor(esum[:, t, c0 : c0 + width], looked_up(ewin[t], c0, width), own[t][:, c0 : c0 + width], ADD)
+        def tap_e(t):
+            nc.vector.tensor_tensor(esum[:, t, :], looked_up(ewin[t], 0, S), plain_e[t], ADD)
 
-        def fetch(c0, width):
+        def fetch_y(c0, width):
             dst = sb([P, PACK, width], F32, "fetched")
             for t in range(PACK):
                 nc.scalar.activation(dst[:, t, :], looked_up(ywin[t], c0, width), COPY)
@@ -149,79 +160,69 @@ def tile_picked_glutap_none_p_kernel(tc, x_words, x_scales, w1, w2, w3, offs, ta
         def turn(dst, src, start, stop):
             nc.tensor.matmul(dst, lhsT=src, rhs=ident[:], start=start, stop=stop, is_transpose=True)
 
-        def gates(blocks, fetched, c0, b, name):
+        def gates_by_transposes(blocks, fetched, c0, b, name):
             acc = bank([P, len(blocks), P], b)
             for u, (t, n) in enumerate(blocks):
-                turn(acc[:, u, :], ywin[t][:, n * CHUNK : (n + 1) * CHUNK], u == 0, False)
+                turn(acc[:, u, :], ywin[t][:, n * PIECE : (n + 1) * PIECE], u == 0, False)
             for u, (t, n) in enumerate(blocks):
-                turn(acc[:, u, :], fetched[:, t, n * CHUNK - c0 : (n + 1) * CHUNK - c0], False, u + 1 == len(blocks))
+                turn(acc[:, u, :], fetched[:, t, n * PIECE - c0 : (n + 1) * PIECE - c0], False, u + 1 == len(blocks))
             turned = sb([P, len(blocks), P], F32, name)
             nc.scalar.activation(turned[:], acc[:], SIGMOID)
             for u, (t, n) in enumerate(blocks):
                 nc.tensor.transpose(gate[n][:, t, :], turned[:, u, :], ident[:])
-            return turned
 
-        chunks = S // CHUNK
-        tap_add(0, 0, S)
-        tap_add(1, 0, S)
-        tap_add(2, 0, S)
-        gate = [bank([P, PACK, CHUNK], 1 + n) for n in range(chunks - 1)] + [sb([P, PACK, CHUNK], F32, "gate3")]
-        first = fetch(0, HALF)
+        for t in range(PACK - 1):
+            tap_e(t)
+
+        gate = [bank([P, PACK, PIECE], 1 + n) for n in range(3)] + [sb([P, PACK, PIECE], F32, "gate3")]
+        fetched01 = fetch_y(0, HALF)
         for pair in range(2):
-            ta = gates([(t, n) for t in (2 * pair, 2 * pair + 1) for n in range(2)], first, 0, 5 + pair, "turned%d" % pair)
+            gates_by_transposes([(t, n) for t in (2 * pair, 2 * pair + 1) for n in range(2)], fetched01, 0, 5 + pair, "turned%d" % pair)
+
         g3 = sb([P, PACK, P * PACK], BF16, "g3")
 
         def round_w3(m0, m1):
-            nc.vector.tensor_copy(g3[:, m0:m1].rearrange("p m (c i j) -> p (m c) j i", i=4, j=PACK),
-                                  raw3[:, :, m0 * P : m1 * P].rearrange("p j (c i) -> p c j i", i=4))
+            nc.vector.tensor_copy(g3[:, m0:m1].rearrange("p m (c i j) -> p (m c) j i", i=RUN, j=PACK),
+                                  raw3[:, :, m0 * P : m1 * P].rearrange("p j (c i) -> p c j i", i=RUN))
 
         round_w3(0, 1)
         round_w3(1, PACK)
-        tap_add(3, 0, S)
+        tap_e(PACK - 1)
         q3 = quant_tiles(g3, 0, PACK, "q3")
-        third = fetch(HALF, CHUNK)
-        tb = gates([(t, 2) for t in range(PACK)], third, HALF, 7, "turned2")
-        ysum = sb([P, PACK, CHUNK], F32, "ysum")
+        gates_by_transposes([(t, 2) for t in range(PACK)], fetch_y(HALF, PIECE), HALF, 7, "turned2")
 
-        def tap_y(t):
-            nc.vector.tensor_tensor(ysum[:, t, :], looked_up(ywin[t], LAST, CHUNK), own_y[:, t, :], ADD)
+        ysum = sb([P, PACK, PIECE], F32, "ysum")
+        for t in range(PACK):
+            nc.vector.tensor_tensor(ysum[:, t, :], looked_up(ywin[t], LAST, PIECE), plain_y[:, t, :], ADD)
+        nc.scalar.activation(gate[3][:], ysum[:], SIGMOID)
 
         def product(n):
-            cols = slice(n * CHUNK, (n + 1) * CHUNK)
-            z = sb([P, CHUNK * PACK], BF16, "z%d" % n)[:]
+            z = sb([P, PIECE * PACK], BF16, "z%d" % n)[:]
             nc.vector.tensor_tensor(z.rearrange("p (c i j) -> p c j i", i=2, j=PACK),
-                                    esum[:, :, cols].rearrange("p j (c i) -> p c j i", i=2),
+                                    esum[:, :, n * PIECE : (n + 1) * PIECE].rearrange("p j (c i) -> p c j i", i=2),
                                     gate[n][:].rearrange("p j (c i) -> p c j i", i=2), MULT)
             return z
 
-        def quant_z(n, z):
-            return quant(z, CHUNK, "z%d" % n)
-
         def leave(n, qz, m0, count, b, copy):
-            acc = bank([P, count, CHUNK], b)
+            acc = bank([P, count, PIECE], b)
             for u in range(count):
                 nc.tensor.matmul_mx(out=acc[:, u, :], lhsT=q3[m0 + u][0].bitcast(FP8X4), lhsT_scale=q3[m0 + u][1],
                                     rhs=qz[0][:].bitcast(FP8X4), rhs_scale=qz[1][:], start=True, stop=True)
-            res = sb([P, count, CHUNK], F32, "res%d_%d" % (n, m0))
+            res = sb([P, count, PIECE], F32, "res%d_%d" % (n, m0))
             copy(res[:], acc[:])
-            nc.sync.dma_start(out[m0 * P : (m0 + count) * P, n * CHUNK : (n + 1) * CHUNK].rearrange("(u p) c -> p u c", p=P), res[:])
+            nc.sync.dma_start(out[m0 * P : (m0 + count) * P, n * PIECE : (n + 1) * PIECE].rearrange("(u p) c -> p u c", p=P), res[:])
 
-        for t in range(PACK):
-            tap_y(t)
-        nc.scalar.activation(gate[3][:], ysum[:], SIGMOID)
+        def leave_in_halves(n, z, banks):
+            qz = quant(z, PIECE, "z%d" % n)
+            for half in range(2):
+                leave(n, qz, 2 * half, 2, banks[half], nc.scalar.copy)
+
         z0 = product(0)
         z1 = product(1)
-        qz0 = quant_z(0, z0)
-        leave(0, qz0, 0, 2, 7, nc.scalar.copy)
-        leave(0, qz0, 2, 2, 5, nc.scalar.copy)
+        leave_in_halves(0, z0, (7, 5))
         z3 = product(3)
-        qz1 = quant_z(1, z1)
-        leave(1, qz1, 0, 2, 0, nc.scalar.copy)
-        leave(1, qz1, 2, 2, 4, nc.scalar.copy)
-        z2 = product(2)
-        qz3 = quant_z(3, z3)
-        leave(3, qz3, 0, 2, 1, nc.scalar.copy)
-        leave(3, qz3, 2, 2, 2, nc.vector.tensor_copy)
-        qz2 = quant_z(2, z2)
-        for m in range(PACK):
-            leave(2, qz2, m, 1, (3, 6, 5, 7)[m], nc.vector.tensor_copy if m % 2 else nc.scalar.copy)
+        leave_in_halves(1, z1, (0, 4))
+        leave_in_halves(3, z3, (1, 2))
+        qz2 = quant(product(2), PIECE, "z2")
+        for m, b in enumerate((3, 6, 5, 7)):
+            leave(2, qz2, m, 1, b, nc.vector.tensor_copy if m % 2 else nc.scalar.copy)

@@ -49,15 +49,14 @@ def tile_picked_glutap_none_p_kernel(tc, x_words, x_scales, w1, w2, w3, offs, ta
         xg_s = sb([P, S], U8, "xg_s")
 
         nc.gpsimd.memset(xs[:].bitcast(I32), 0)
-        nc.gpsimd.memset(xg_s[:].bitcast(I32), 0)
         ident = sb([P, P], F32, "ident")
         make_identity(nc, ident[:])
 
         w2v = w2.rearrange("(p j) c -> p j c", j=PACK)
-        nc.sync.dma_start(raw2[:, 0:2, :], w2v[:, 0:2, :])
+        nc.sync.dma_start(raw2[:, 0:1, :], w2v[:, 0:1, :])
         nc.sync.dma_start(offs_t[:], offs)
         nc.sync.dma_start(xs[0:P:8, :].bitcast(I32), x_scales[0].bitcast(I32))
-        nc.sync.dma_start(raw2[:, 2:PACK, :], w2v[:, 2:PACK, :])
+        nc.sync.dma_start(raw2[:, 1:PACK, :], w2v[:, 1:PACK, :])
         nc.sync.dma_start(xw[:], x_words[0].rearrange("p n t -> p (n t)").bitcast(I32))
         nc.sync.dma_start(tap_t[:], tap)
 
@@ -88,7 +87,8 @@ def tile_picked_glutap_none_p_kernel(tc, x_words, x_scales, w1, w2, w3, offs, ta
 
         g2 = sb([P, PACK, P * PACK], BF16, "g2")
         nc.vector.tensor_copy(picked[:], xs[:].indirect(offs_t[:]))
-        for r in range(4):
+        nc.vector.tensor_copy(xg_s[:].bitcast(I32), picked[:].bitcast(I32))
+        for r in range(1, 4):
             nc.sync.dma_start(xg_s[r:P:32, :].bitcast(I32), picked[8 * r : P : 32, :].bitcast(I32))
 
         dst2 = g2[:].rearrange("p t (u i j) -> p t u j i", i=RUN, j=PACK)
@@ -97,13 +97,13 @@ def tile_picked_glutap_none_p_kernel(tc, x_words, x_scales, w1, w2, w3, offs, ta
         for t in range(2, PACK):
             nc.scalar.copy(dst2[:, t], src2[:, t])
 
-        ewin = [sb([P, 4 * S - PIECE], F32, "xs"), sb([P, 2 * S], F32, "e1"), sb([P, 2 * S], F32, "e2"), sb([P, 2 * S], F32, "e3")]
-        for t in (2, 3):
+        ewin = [sb([P, 2 * S], F32, "e0"), sb([P, 2 * S], F32, "e1"), sb([P, 2 * S], F32, "e2"), sb([P, 2 * S], F32, "e3")]
+        for t in range(PACK):
             nc.gpsimd.memset(ewin[t][:, S:], 0.0)
-        sums = sb([P, PACK * S - PIECE // 2 + PACK * N], F32, "raw2")
+        sums = sb([P, PACK * S - PIECE // 2 + PACK * N + PACK * HALF], F32, "xs")
         esum = sums[:, 0 : PACK * S].rearrange("p (t c) -> p t c", t=PACK)
-        raw3 = sums[:, PACK * S - PIECE // 2 :].rearrange("p (j c) -> p j c", j=PACK)
-        raw1 = [ewin[0][:, 2 * S - PIECE :].rearrange("p (j c) -> p j c", j=PACK), esum[:, :, 0:HALF]]
+        raw3 = sums[:, PACK * S - PIECE // 2 : PACK * S - PIECE // 2 + PACK * N].rearrange("p (j c) -> p j c", j=PACK)
+        raw1 = [sums[:, PACK * S - PIECE // 2 + PACK * N :].rearrange("p (j c) -> p j c", j=PACK), esum[:, :, 0:HALF]]
         for half in range(2):
             nc.sync.dma_start(raw1[half], w1.rearrange("(p j) c -> p j c", j=PACK)[:, :, half * HALF : (half + 1) * HALF])
         q2 = quant_tiles(g2, 0, 2, "q2") + quant_tiles(g2, 2, PACK, "q2")
@@ -123,21 +123,20 @@ def tile_picked_glutap_none_p_kernel(tc, x_words, x_scales, w1, w2, w3, offs, ta
             src = raw1[half].rearrange("p j (u t i) -> p t u j i", t=PACK, i=RUN)[:, t0:t1]
             nc.vector.tensor_copy(dst[:, :, u0:u1], src[:, :, u0:u1])
 
-        round_w1(0, 0, PACK, 0, 8)
-        round_w1(0, 0, PACK, 8, 16)
+        round_w1(0, 0, PACK, 0, 16)
 
         ywin = [sb([P, S], F32, "y%d" % t) for t in range(PACK)]
-        plain_e = [ewin[1][:, S:], ewin[0][:, S : 2 * S], sb([P, S], F32, "plain_e2")[:], sb([P, S], F32, "plain_e3")[:]]
+        plain_e = [sums[:, PACK * S - PIECE // 2 + PACK * N : PACK * S - PIECE // 2 + PACK * N + S], sb([P, S], F32, "plain_e1")[:], sb([P, S], F32, "plain_e2")[:], sb([P, S], F32, "plain_e3")[:]]
         e0 = [project(q2[0], half * HALF, HALF, half) for half in range(2)]
-        for dst in (ewin[0][:, 0:S], plain_e[0]):
+        for dst, copy in ((ewin[0][:, 0:S], nc.scalar.copy), (plain_e[0], nc.vector.tensor_copy)):
             for half in range(2):
-                nc.scalar.copy(dst[:, half * HALF : (half + 1) * HALF], e0[half][:])
-        e1 = project(q2[1], 0, S, 2)
-        nc.vector.tensor_copy(plain_e[1], e1[:])
+                copy(dst[:, half * HALF : (half + 1) * HALF], e0[half][:])
         for t in (2, 3):
             nc.scalar.copy(ewin[t][:, 0:S], project(q2[t], 0, S, 1 + t)[:])
             nc.sync.dma_start(plain_e[t], ewin[t][:, 0:S])
-        nc.scalar.copy(ewin[1][:, 0:S], e1[:])
+        e1 = project(q2[1], 0, S, 2)
+        for dst in (ewin[1][:, 0:S], plain_e[1]):
+            nc.scalar.copy(dst, e1[:])
 
         for pair in range(2):
             round_w1(1, 2 * pair, 2 * pair + 2, 0, 16)
@@ -145,7 +144,8 @@ def tile_picked_glutap_none_p_kernel(tc, x_words, x_scales, w1, w2, w3, offs, ta
 
         plain_y = sb([P, PACK, PIECE], F32, "plain_y")
         for t in range(PACK):
-            nc.scalar.copy(ywin[t][:], project(q1[t], 0, S, (5 + t) % 8)[:])
+            copy = nc.vector.tensor_copy if t == PACK - 1 else nc.scalar.copy
+            copy(ywin[t][:], project(q1[t], 0, S, (5 + t) % 8)[:])
             nc.sync.dma_start(plain_y[:, t, :], ywin[t][:, LAST:])
 
         def tap_e(t):

@@ -144,8 +144,11 @@ def tile_picked_glutap_none_p_kernel(tc, x_words, x_scales, w1, w2, w3, offs, ta
 
         plain_y = sb([P, PACK, PIECE], F32, "plain_y")
         for t in range(PACK):
-            copy = nc.vector.tensor_copy if t == PACK - 1 else nc.scalar.copy
-            copy(ywin[t][:], project(q1[t], 0, S, (5 + t) % 8)[:])
+            if t < PACK - 1:
+                nc.scalar.copy(ywin[t][:], project(q1[t], 0, S, 5 + t)[:])
+            else:
+                for half, copy in enumerate((nc.vector.tensor_copy, nc.scalar.copy)):
+                    copy(ywin[t][:, half * HALF : (half + 1) * HALF], project(q1[t], half * HALF, HALF, half)[:])
             nc.sync.dma_start(plain_y[:, t, :], ywin[t][:, LAST:])
 
         def tap_e(t):

@@ -144,7 +144,10 @@ def tile_picked_glutap_none_p_kernel(tc, x_words, x_scales, w1, w2, w3, offs, ta
 
         plain_y = sb([P, PACK, PIECE], F32, "plain_y")
         for t in range(PACK):
-            if t < PACK - 1:
+            if t == 0:
+                for half, b in enumerate((5, 3)):
+                    nc.scalar.copy(ywin[t][:, half * HALF : (half + 1) * HALF], project(q1[t], half * HALF, HALF, b)[:])
+            elif t < PACK - 1:
                 nc.scalar.copy(ywin[t][:], project(q1[t], 0, S, 5 + t)[:])
             else:
                 for half, copy in enumerate((nc.vector.tensor_copy, nc.scalar.copy)):
@@ -154,11 +157,11 @@ def tile_picked_glutap_none_p_kernel(tc, x_words, x_scales, w1, w2, w3, offs, ta
         def tap_e(t):
             nc.vector.tensor_tensor(esum[:, t, :], looked_up(ewin[t], 0, S), plain_e[t], ADD)
 
-        def fetch_y(c0, width):
-            dst = sb([P, PACK, width], F32, "fetched")
-            for t in range(PACK):
-                nc.scalar.activation(dst[:, t, :], looked_up(ywin[t], c0, width), COPY)
-            return dst
+        def fetch_y(tiles, c0, width, name):
+            dst = sb([P, len(tiles), width], F32, name)
+            for u, t in enumerate(tiles):
+                nc.scalar.activation(dst[:, u, :], looked_up(ywin[t], c0, width), COPY)
+            return [dst[:, u, :] for u in range(len(tiles))]
 
         def turn(dst, src, start, stop):
             nc.tensor.matmul(dst, lhsT=src, rhs=ident[:], start=start, stop=stop, is_transpose=True)
@@ -168,7 +171,7 @@ def tile_picked_glutap_none_p_kernel(tc, x_words, x_scales, w1, w2, w3, offs, ta
             for u, (t, n) in enumerate(blocks):
                 turn(acc[:, u, :], ywin[t][:, n * PIECE : (n + 1) * PIECE], u == 0, False)
             for u, (t, n) in enumerate(blocks):
-                turn(acc[:, u, :], fetched[:, t, n * PIECE - c0 : (n + 1) * PIECE - c0], False, u + 1 == len(blocks))
+                turn(acc[:, u, :], fetched[t][:, n * PIECE - c0 : (n + 1) * PIECE - c0], False, u + 1 == len(blocks))
             turned = sb([P, len(blocks), P], F32, name)
             nc.scalar.activation(turned[:], acc[:], SIGMOID)
             for u, (t, n) in enumerate(blocks):
@@ -177,8 +180,8 @@ def tile_picked_glutap_none_p_kernel(tc, x_words, x_scales, w1, w2, w3, offs, ta
         for t in range(PACK - 1):
             tap_e(t)
 
-        gate = [bank([P, PACK, PIECE], 1 + n) for n in range(3)] + [sb([P, PACK, PIECE], F32, "gate3")]
-        fetched01 = fetch_y(0, HALF)
+        gate = [bank([P, PACK, PIECE], 1 + n) for n in range(3)]
+        fetched01 = fetch_y((0, 1), 0, HALF, "fetched_a") + fetch_y((2, 3), 0, HALF, "fetched_b")
         for pair in range(2):
             gates_by_transposes([(t, n) for t in (2 * pair, 2 * pair + 1) for n in range(2)], fetched01, 0, 5 + pair, "turned%d" % pair)
 
@@ -192,11 +195,12 @@ def tile_picked_glutap_none_p_kernel(tc, x_words, x_scales, w1, w2, w3, offs, ta
         round_w3(1, PACK)
         tap_e(PACK - 1)
         q3 = quant_tiles(g3, 0, PACK, "q3")
-        gates_by_transposes([(t, 2) for t in range(PACK)], fetch_y(HALF, PIECE), HALF, 7, "turned2")
+        gates_by_transposes([(t, 2) for t in range(PACK)], fetch_y((0,), HALF, PIECE, "fetched_a") + fetch_y((1, 2, 3), HALF, PIECE, "fetched_b"), HALF, 7, "turned2")
 
         ysum = sb([P, PACK, PIECE], F32, "ysum")
         for t in range(PACK):
             nc.vector.tensor_tensor(ysum[:, t, :], looked_up(ywin[t], LAST, PIECE), plain_y[:, t, :], ADD)
+        gate.append(sb([P, PACK, PIECE], F32, "fetched_b"))
         nc.scalar.activation(gate[3][:], ysum[:], SIGMOID)
 
         def product(n):

@@ -150,7 +150,7 @@ def tile_picked_glutap_none_p_kernel(tc, x_words, x_scales, w1, w2, w3, offs, ta
             elif t < PACK - 1:
                 nc.scalar.copy(ywin[t][:], project(q1[t], 0, S, 5 + t)[:])
             else:
-                for half, copy in enumerate((nc.vector.tensor_copy, nc.scalar.copy)):
+                for half, copy in enumerate((nc.scalar.copy, nc.scalar.copy)):
                     copy(ywin[t][:, half * HALF : (half + 1) * HALF], project(q1[t], half * HALF, HALF, half)[:])
             nc.sync.dma_start(plain_y[:, t, :], ywin[t][:, LAST:])
 
@@ -195,13 +195,15 @@ def tile_picked_glutap_none_p_kernel(tc, x_words, x_scales, w1, w2, w3, offs, ta
         round_w3(1, PACK)
         tap_e(PACK - 1)
         q3 = quant_tiles(g3, 0, PACK, "q3")
-        gates_by_transposes([(t, 2) for t in range(PACK)], fetch_y((0,), HALF, PIECE, "fetched_a") + fetch_y((1, 2, 3), HALF, PIECE, "fetched_b"), HALF, 7, "turned2")
+        fetched2 = fetch_y((0,), HALF, PIECE, "fetched_a") + fetch_y((1,), HALF, PIECE, "fetched_b") + fetch_y((2, 3), HALF, PIECE, "turned0")
+        gates_by_transposes([(0, 2), (1, 2)], fetched2, HALF, 7, "turned2")
 
         ysum = sb([P, PACK, PIECE], F32, "ysum")
         for t in range(PACK):
             nc.vector.tensor_tensor(ysum[:, t, :], looked_up(ywin[t], LAST, PIECE), plain_y[:, t, :], ADD)
         gate.append(sb([P, PACK, PIECE], F32, "fetched_b"))
         nc.scalar.activation(gate[3][:], ysum[:], SIGMOID)
+        gates_by_transposes([(2, 2), (3, 2)], fetched2, HALF, 4, "turned3")
 
         def product(n):
             z = sb([P, PIECE * PACK], BF16, "z%d" % n)[:]
@@ -226,10 +228,10 @@ def tile_picked_glutap_none_p_kernel(tc, x_words, x_scales, w1, w2, w3, offs, ta
 
         z0 = product(0)
         z1 = product(1)
-        leave_in_halves(0, z0, (7, 5))
+        leave_in_halves(0, z0, (4, 5))
         z3 = product(3)
-        leave_in_halves(1, z1, (0, 4))
+        leave_in_halves(1, z1, (0, 7))
         leave_in_halves(3, z3, (1, 2))
         qz2 = quant(product(2), PIECE, "z2")
-        for m, b in enumerate((3, 6, 5, 7)):
-            leave(2, qz2, m, 1, b, nc.vector.tensor_copy if m % 2 else nc.scalar.copy)
+        for m, b in enumerate((3, 6, 5, 4)):
+            leave(2, qz2, m, 1, b, nc.scalar.copy if m == 2 else nc.vector.tensor_copy)

from contextlib import ExitStack

import concourse.mybir as mybir
from concourse.masks import make_identity

K, T, S, N, H = 512, 2048, 512, 512, 512
FLOPS = 2 * K * H * S * 2 + 2 * H * N * S

F32 = mybir.dt.float32
BF16 = mybir.dt.bfloat16
I32 = mybir.dt.int32
U32 = mybir.dt.uint32
U16 = mybir.dt.uint16
U8 = mybir.dt.uint8
FP8X4 = mybir.dt.float8_e4m3fn_x4
ADD = mybir.AluOpType.add
MULT = mybir.AluOpType.mult
SIGMOID = mybir.ActivationFunctionType.Sigmoid
COPY = mybir.ActivationFunctionType.Copy

P = 128
PACK = 4
HALF = S // 2
PIECE = 128
LAST = S - PIECE
GROUP = 16
RUN = 4


def tile_picked_glutap_none_p_kernel(tc, x_words, x_scales, w1, w2, w3, offs, tap, out):
    nc = tc.nc
    with ExitStack() as ctx:
        keep = ctx.enter_context(tc.tile_pool(name="keep", bufs=1))
        psum = ctx.enter_context(tc.psum_pool(name="psum", bufs=1))

        def sb(shape, dtype, name):
            return keep.tile(shape, dtype, name=name, align_bytes=64)

        def bank(shape, b):
            return psum.tile(shape, F32, name="bank%d" % b)

        offs_t = keep.tile([P, S // GROUP], U16, name="offs_t")
        tap_t = keep.tile([P, S // GROUP], U16, name="tap_t")
        xw = sb([P, T], I32, "xw")
        xs = sb([P, T], U8, "xs")
        warm = sb([P, 16], F32, "warm")
        warm_out = sb([P, 16], F32, "warm_out")
        raw2 = sb([P, PACK, H], F32, "raw2")
        xg_s = sb([P, S], U8, "xg_s")

        nc.gpsimd.memset(xs[:].bitcast(I32), 0)
        ident = sb([P, P], F32, "ident")
        make_identity(nc, ident[:])

        w2v = w2.rearrange("(p j) c -> p j c", j=PACK)
        nc.sync.dma_start(raw2[:, 0:1, :], w2v[:, 0:1, :])
        nc.sync.dma_start(offs_t[:], offs)
        nc.sync.dma_start(xs[0:P:8, :].bitcast(I32), x_scales[0].bitcast(I32))
        nc.sync.dma_start(raw2[:, 1:PACK, :], w2v[:, 1:PACK, :])
        nc.sync.dma_start(xw[:], x_words[0].rearrange("p n t -> p (n t)").bitcast(I32))
        nc.sync.dma_start(tap_t[:], tap)

        nc.vector.memset(warm[:, 0:8], 0.0)
        nc.scalar.activation(warm_out[:, 0:8], warm[:, 0:8], SIGMOID)

        picked = sb([P, S], U8, "picked")
        xg_w = sb([P, S], U32, "xg_w")

        def quant(rounded, width, name):
            codes = sb([P, width], U32, name + "_c")
            scales = sb([P, width], U8, name + "_s")
            nc.vector.quantize_mx(out=codes[:].bitcast(FP8X4), scales=scales[:], in_=rounded)
            return codes, scales

        def quant_tiles(rounded, t0, t1, name):
            codes, scales = quant(rounded[:, t0:t1, :].rearrange("p t c -> p (t c)"), (t1 - t0) * P, "%s_%d" % (name, t0))
            return [(codes[:, u * P : (u + 1) * P], scales[:, u * P : (u + 1) * P]) for u in range(t1 - t0)]

        def project(q, c0, width, b):
            acc = bank([P, width], b)
            nc.tensor.matmul_mx(out=acc[:], lhsT=q[0].bitcast(FP8X4), lhsT_scale=q[1],
                                rhs=xg_w[:, c0 : c0 + width].bitcast(FP8X4), rhs_scale=xg_s[:, c0 : c0 + width], start=True, stop=True)
            return acc

        def looked_up(window, c0, width):
            return window[:].indirect(tap_t[:, c0 // GROUP : (c0 + width) // GROUP])

        g2 = sb([P, PACK, P * PACK], BF16, "g2")
        nc.vector.tensor_copy(picked[:], xs[:].indirect(offs_t[:]))
        nc.vector.tensor_copy(xg_s[:].bitcast(I32), picked[:].bitcast(I32))
        for r in range(1, 4):
            nc.sync.dma_start(xg_s[r:P:32, :].bitcast(I32), picked[8 * r : P : 32, :].bitcast(I32))

        dst2 = g2[:].rearrange("p t (u i j) -> p t u j i", i=RUN, j=PACK)
        src2 = raw2[:].rearrange("p j (u t i) -> p t u j i", t=PACK, i=RUN)
        nc.vector.tensor_copy(dst2[:, 0:2], src2[:, 0:2])
        for t in range(2, PACK):
            nc.scalar.copy(dst2[:, t], src2[:, t])

        ewin = [sb([P, 2 * S], F32, "e0"), sb([P, 2 * S], F32, "e1"), sb([P, 2 * S], F32, "e2"), sb([P, 2 * S], F32, "e3")]
        for t in range(PACK):
            nc.gpsimd.memset(ewin[t][:, S:], 0.0)
        sums = sb([P, PACK * S - PIECE // 2 + PACK * N + PACK * HALF], F32, "xs")
        esum = sums[:, 0 : PACK * S].rearrange("p (t c) -> p t c", t=PACK)
        raw3 = sums[:, PACK * S - PIECE // 2 : PACK * S - PIECE // 2 + PACK * N].rearrange("p (j c) -> p j c", j=PACK)
        raw1 = [sums[:, PACK * S - PIECE // 2 + PACK * N :].rearrange("p (j c) -> p j c", j=PACK), esum[:, :, 0:HALF]]
        for half in range(2):
            nc.sync.dma_start(raw1[half], w1.rearrange("(p j) c -> p j c", j=PACK)[:, :, half * HALF : (half + 1) * HALF])
        q2 = quant_tiles(g2, 0, 2, "q2") + quant_tiles(g2, 2, PACK, "q2")

        for half in range(2):
            nc.vector.tensor_copy(xg_w[:, half * HALF : (half + 1) * HALF],
                                  xw[:].bitcast(U32).indirect(offs_t[:, half * HALF // GROUP : (half + 1) * HALF // GROUP]))

        w3v = w3.rearrange("(u t i) n -> t u i n", t=PACK, i=RUN)
        for t in range(PACK):
            nc.sync.dma_start(raw3[:, t, :], w3v[t])

        g1 = sb([P, PACK, P * PACK], BF16, "g1")

        def round_w1(half, t0, t1, u0, u1):
            dst = g1[:, t0:t1, half * HALF : (half + 1) * HALF].rearrange("p t (u i j) -> p t u j i", i=RUN, j=PACK)
            src = raw1[half].rearrange("p j (u t i) -> p t u j i", t=PACK, i=RUN)[:, t0:t1]
            nc.vector.tensor_copy(dst[:, :, u0:u1], src[:, :, u0:u1])

        round_w1(0, 0, PACK, 0, 16)

        ywin = [sb([P, S], F32, "y%d" % t) for t in range(PACK)]
        plain_e = [sums[:, PACK * S - PIECE // 2 + PACK * N : PACK * S - PIECE // 2 + PACK * N + S], sb([P, S], F32, "plain_e1")[:], sb([P, S], F32, "plain_e2")[:], sb([P, S], F32, "plain_e3")[:]]
        e0 = [project(q2[0], half * HALF, HALF, half) for half in range(2)]
        for dst, copy in ((ewin[0][:, 0:S], nc.scalar.copy), (plain_e[0], nc.vector.tensor_copy)):
            for half in range(2):
                copy(dst[:, half * HALF : (half + 1) * HALF], e0[half][:])
        for t in (2, 3):
            nc.scalar.copy(ewin[t][:, 0:S], project(q2[t], 0, S, 1 + t)[:])
            nc.sync.dma_start(plain_e[t], ewin[t][:, 0:S])
        e1 = project(q2[1], 0, S, 2)
        for dst in (ewin[1][:, 0:S], plain_e[1]):
            nc.scalar.copy(dst, e1[:])

        for pair in range(2):
            round_w1(1, 2 * pair, 2 * pair + 2, 0, 16)
        q1 = quant_tiles(g1, 0, 2, "q1") + quant_tiles(g1, 2, PACK, "q1")

        plain_y = sb([P, PACK, PIECE], F32, "plain_y")
        for t in range(PACK):
            if t == 0:
                for half, b in enumerate((5, 3)):
                    nc.scalar.copy(ywin[t][:, half * HALF : (half + 1) * HALF], project(q1[t], half * HALF, HALF, b)[:])
            elif t < PACK - 1:
                nc.scalar.copy(ywin[t][:], project(q1[t], 0, S, 5 + t)[:])
            else:
                for half, copy in enumerate((nc.scalar.copy, nc.scalar.copy)):
                    copy(ywin[t][:, half * HALF : (half + 1) * HALF], project(q1[t], half * HALF, HALF, half)[:])
            nc.sync.dma_start(plain_y[:, t, :], ywin[t][:, LAST:])

        def tap_e(t):
            nc.vector.tensor_tensor(esum[:, t, :], looked_up(ewin[t], 0, S), plain_e[t], ADD)

        def fetch_y(tiles, c0, width, name):
            dst = sb([P, len(tiles), width], F32, name)
            for u, t in enumerate(tiles):
                nc.scalar.activation(dst[:, u, :], looked_up(ywin[t], c0, width), COPY)
            return [dst[:, u, :] for u in range(len(tiles))]

        def turn(dst, src, start, stop):
            nc.tensor.matmul(dst, lhsT=src, rhs=ident[:], start=start, stop=stop, is_transpose=True)

        def gates_by_transposes(blocks, fetched, c0, b, name):
            acc = bank([P, len(blocks), P], b)
            for u, (t, n) in enumerate(blocks):
                turn(acc[:, u, :], ywin[t][:, n * PIECE : (n + 1) * PIECE], u == 0, False)
            for u, (t, n) in enumerate(blocks):
                turn(acc[:, u, :], fetched[t][:, n * PIECE - c0 : (n + 1) * PIECE - c0], False, u + 1 == len(blocks))
            turned = sb([P, len(blocks), P], F32, name)
            nc.scalar.activation(turned[:], acc[:], SIGMOID)
            for u, (t, n) in enumerate(blocks):
                nc.tensor.transpose(gate[n][:, t, :], turned[:, u, :], ident[:])

        for t in range(PACK - 1):
            tap_e(t)

        gate = [bank([P, PACK, PIECE], 1 + n) for n in range(3)]
        fetched01 = fetch_y((0, 1), 0, HALF, "fetched_a") + fetch_y((2, 3), 0, HALF, "fetched_b")
        for pair in range(2):
            gates_by_transposes([(t, n) for t in (2 * pair, 2 * pair + 1) for n in range(2)], fetched01, 0, 5 + pair, "turned%d" % pair)

        g3 = sb([P, PACK, P * PACK], BF16, "g3")

        def round_w3(m0, m1):
            nc.vector.tensor_copy(g3[:, m0:m1].rearrange("p m (c i j) -> p (m c) j i", i=RUN, j=PACK),
                                  raw3[:, :, m0 * P : m1 * P].rearrange("p j (c i) -> p c j i", i=RUN))

        round_w3(0, 1)
        round_w3(1, PACK)
        tap_e(PACK - 1)
        q3 = quant_tiles(g3, 0, PACK, "q3")
        fetched2 = fetch_y((0,), HALF, PIECE, "fetched_a") + fetch_y((1,), HALF, PIECE, "fetched_b") + fetch_y((2, 3), HALF, PIECE, "turned0")
        gates_by_transposes([(0, 2), (1, 2)], fetched2, HALF, 7, "turned2")

        ysum = sb([P, PACK, PIECE], F32, "ysum")
        for t in range(PACK):
            nc.vector.tensor_tensor(ysum[:, t, :], looked_up(ywin[t], LAST, PIECE), plain_y[:, t, :], ADD)
        gate.append(sb([P, PACK, PIECE], F32, "fetched_b"))
        nc.scalar.activation(gate[3][:], ysum[:], SIGMOID)
        gates_by_transposes([(2, 2), (3, 2)], fetched2, HALF, 4, "turned3")

        def product(n):
            z = sb([P, PIECE * PACK], BF16, "z%d" % n)[:]
            nc.vector.tensor_tensor(z.rearrange("p (c i j) -> p c j i", i=2, j=PACK),
                                    esum[:, :, n * PIECE : (n + 1) * PIECE].rearrange("p j (c i) -> p c j i", i=2),
                                    gate[n][:].rearrange("p j (c i) -> p c j i", i=2), MULT)
            return z

        def leave(n, qz, m0, count, b, copy):
            acc = bank([P, count, PIECE], b)
            for u in range(count):
                nc.tensor.matmul_mx(out=acc[:, u, :], lhsT=q3[m0 + u][0].bitcast(FP8X4), lhsT_scale=q3[m0 + u][1],
                                    rhs=qz[0][:].bitcast(FP8X4), rhs_scale=qz[1][:], start=True, stop=True)
            res = sb([P, count, PIECE], F32, "res%d_%d" % (n, m0))
            copy(res[:], acc[:])
            nc.sync.dma_start(out[m0 * P : (m0 + count) * P, n * PIECE : (n + 1) * PIECE].rearrange("(u p) c -> p u c", p=P), res[:])

        def leave_in_halves(n, z, banks):
            qz = quant(z, PIECE, "z%d" % n)
            for half in range(2):
                leave(n, qz, 2 * half, 2, banks[half], nc.scalar.copy)

        z0 = product(0)
        z1 = product(1)
        leave_in_halves(0, z0, (4, 5))
        z3 = product(3)
        leave_in_halves(1, z1, (0, 7))
        leave_in_halves(3, z3, (1, 2))
        qz2 = quant(product(2), PIECE, "z2")
        for m, b in enumerate((3, 6, 5, 4)):
            leave(2, qz2, m, 1, b, nc.scalar.copy if m == 2 else nc.vector.tensor_copy)
